import numpy as np
import ml_dtypes


def mxq(x, axis, fmt="e4m3"):
    dtype, down = {"e4m3": (ml_dtypes.float8_e4m3fn, 7), "e5m2": (ml_dtypes.float8_e5m2, 14)}[fmt]
    v = np.moveaxis(np.asarray(x, np.float32).astype(ml_dtypes.bfloat16).astype(np.float64), axis, -1)
    blocks = v.reshape(v.shape[:-1] + (-1, 32))
    amax = np.abs(blocks).max(-1, keepdims=True)
    byte = np.maximum(np.where(amax > 0, np.frexp(amax)[1] - 1 + 127, 0) - down, 1)
    scale = np.exp2(byte - 127.0)
    codes = (blocks / scale).astype(np.float32).astype(dtype).astype(np.float64)
    return np.moveaxis((codes * scale).reshape(v.shape), -1, axis)


WIDE = False


def mx_kscale(k):
    if not WIDE:
        return np.ones(k)
    levels = np.array([10, -10, 5, -5, 0])
    if k % 512:
        return np.exp2(np.random.permutation(np.resize(levels, k // 32))).repeat(32)
    a = np.empty((k // 512, 16))
    for p in range(k // 512):
        a[p, :8] = np.random.permutation(np.resize(levels, 8))
        for g in range(8):
            far = levels[np.abs(levels - a[p, g]) >= 10]
            a[p, g + 8] = far[np.random.randint(len(far))]
    return np.exp2(a.ravel()).repeat(32)


def f64(x):
    return np.asarray(x).astype(np.float64)


def striped(idx):
    return np.tile(idx.reshape(-1, 16).T, (8, 1)).astype(np.uint16)


def unstriped(offs):
    return offs[:16].T.reshape(-1).astype(np.int64)


E2M1 = np.array([0.0, 0.5, 1.0, 1.5, 2.0, 3.0, 4.0, 6.0, -0.0, -0.5, -1.0, -1.5, -2.0, -3.0, -4.0, -6.0])


def pack_weight(w, fmt):
    k, n = w.shape
    w = f64(np.asarray(w, np.float32).astype(ml_dtypes.bfloat16)).reshape(k // 32, 32, n)
    amax = np.abs(w).max(1)
    if fmt == "e4m3":
        byte = np.frexp(amax)[1] - 1 + 127 - 7
    else:
        mant, ex = np.frexp(amax / 6.0)
        byte = np.where(mant > 0.5, ex, ex - 1) + 127
    byte = np.clip(np.where(amax > 0, byte, 1), 1, 254)
    scaled = (w * np.exp2(127.0 - byte)[:, None, :]).reshape(k, n).astype(np.float32)
    by_word = np.ascontiguousarray(scaled.reshape(k // 512, 128, 4, n).transpose(0, 1, 3, 2))
    if fmt == "e4m3":
        words = by_word.astype(ml_dtypes.float8_e4m3fn).view(np.uint8)
    else:
        c = by_word.astype(ml_dtypes.float4_e2m1fn).view(np.uint8) & 0xF
        words = (c[..., 0::2] | (c[..., 1::2] << 4)).reshape(k // 512, 128, 2 * n)
    return np.ascontiguousarray(words), np.ascontiguousarray(byte.astype(np.uint8).reshape(k // 512, 16, n))


def unpack_weight(words, scales, fmt):
    g, _, n = scales.shape
    words = np.ascontiguousarray(words).reshape(g, 128, n, -1)
    if fmt == "e4m3":
        vals = words.view(ml_dtypes.float8_e4m3fn).astype(np.float64)
    else:
        nib = np.empty((g, 128, n, 4), np.uint8)
        nib[..., 0::2] = words & 0xF
        nib[..., 1::2] = words >> 4
        vals = E2M1[nib]
    vals = vals * np.repeat(np.exp2(scales.astype(np.float64) - 127.0), 8, axis=1)[..., None]
    return vals.transpose(0, 1, 3, 2).reshape(g * 512, n)


def gelu(v):
    return 0.5 * v * (1.0 + np.tanh(np.sqrt(2.0 / np.pi) * (v + 0.044715 * v**3)))


K, T, S, P, H, N = 1024, 4096, 1024, 512, 1024, 512

def setup_inputs():
    n = np.random.standard_normal
    s = mx_kscale(K)[:, None]
    u = mx_kscale(H)[:, None]
    tab_words, tab_scales = pack_weight(n((K, T)) * s, "e4m3")
    w1 = (n((K, H)) / np.sqrt(K) / s).astype(np.float32)
    gain = (2.0 * np.exp(0.3 * n(H)) * u[:, 0]).astype(np.float32)
    w2_words, w2_scales = pack_weight(n((H, N)) / np.sqrt(H) / u, "e2m1")
    return {"tab_words": tab_words, "tab_scales": tab_scales,
            "offs": striped(np.random.permutation(T)[:S]),
            "pos1": striped(np.random.permutation(S)[:P]),
            "pos2": striped(np.random.permutation(S)[:P]),
            "w1": w1, "gain": gain,
            "w2_words": w2_words, "w2_scales": w2_scales}

def reference(tab_words, tab_scales, offs, pos1, pos2, w1, gain, w2_words, w2_scales):
    v = unpack_weight(tab_words, tab_scales, "e4m3")[:, unstriped(offs)]
    w1q = mxq(f64(w1), 0, "e4m3")
    w2 = unpack_weight(w2_words, w2_scales, "e2m1")
    x = w1q.T @ v
    h = np.log(1.0 + np.abs(x))
    a = h[:, unstriped(pos1)]
    b = h[:, unstriped(pos2)]
    z = f64(gain)[:, None] * (a - b)
    zq = mxq(z, 0, "e4m3")
    return w2.T @ zq

@@ -1,0 +1,233 @@
+from contextlib import ExitStack
+
+import concourse.mybir as mybir
+
+K, T, S, Q, H, N = 1024, 4096, 1024, 512, 1024, 512
+FLOPS = 2 * K * H * S + 2 * H * N * Q
+
+F32 = mybir.dt.float32
+BF16 = mybir.dt.bfloat16
+I32 = mybir.dt.int32
+U32 = mybir.dt.uint32
+U16 = mybir.dt.uint16
+U8 = mybir.dt.uint8
+FP8X4 = mybir.dt.float8_e4m3fn_x4
+FP4X4 = mybir.dt.float4_e2m1fn_x4
+ACT = mybir.ActivationFunctionType
+ALU = mybir.AluOpType
+
+P = 128
+PACK = 4
+K_PASS = P * PACK
+BANK = 512
+LANES = 16
+CHUNKS = 2
+
+
+def tile_list_frame_delta_logits_kernel(
+    tc, tab_words, tab_scales, offs, pos1, pos2, w1, gain, w2_words, w2_scales, out
+):
+    nc = tc.nc
+    with ExitStack() as ctx:
+        keep = ctx.enter_context(tc.tile_pool(name="keep", bufs=1))
+        ring = ctx.enter_context(tc.tile_pool(name="ring", bufs=3))
+        psum = ctx.enter_context(tc.psum_pool(name="psum", bufs=4))
+
+        offs_sb = keep.tile([P, S // LANES], U16, name="offs_sb")
+        pos1_sb = keep.tile([P, Q // LANES], U16, name="pos1_sb")
+        pos2_sb = keep.tile([P, Q // LANES], U16, name="pos2_sb")
+        gain_sb = keep.tile([P, 2, PACK], F32, name="gain_sb")
+        table = [keep.tile([P, T], I32, name=f"table{a}") for a in range(2)]
+        table_scales = keep.tile([P, T // 4], I32, name="table_scales")
+        w1_raw = {
+            (a, b): keep.tile([P, PACK, K_PASS], F32, name=f"w1_raw{a}{b}") for a in range(2) for b in range(2)
+        }
+        w2_codes = keep.tile([P, 2, 2 * N], U8, name="w2_codes", align_bytes=64)
+        w2_planes = keep.tile([P, 2, N // 4], I32, name="w2_planes", align_bytes=64)
+        one = keep.tile([P, 1], F32, name="one")
+        zero = keep.tile([P, 1], F32, name="zero")
+
+        def load_table(a):
+            nc.sync.dma_start(table[a][:], tab_words[a].rearrange("p t i -> p (t i)").bitcast(I32))
+
+        def load_w1(a, b):
+            rows = w1[a * K_PASS : (a + 1) * K_PASS, b * K_PASS : (b + 1) * K_PASS]
+            nc.sync.dma_start(w1_raw[a, b][:], rows.rearrange("(p j) c -> p j c", j=PACK))
+
+        nc.scalar.dma_start(gain_sb[:], gain.rearrange("(b p t) -> p b t", b=2, t=PACK))
+        nc.sync.dma_start(offs_sb[:], offs)
+        load_table(0)
+        load_w1(0, 0)
+        load_w1(1, 0)
+        nc.sync.dma_start(pos1_sb[:], pos1)
+        nc.sync.dma_start(pos2_sb[:], pos2)
+        load_table(1)
+        load_w1(0, 1)
+        load_w1(1, 1)
+        nc.sync.dma_start(w2_codes[:].bitcast(I32), w2_words.rearrange("b p c -> p b c").bitcast(I32))
+
+        nc.vector.memset(table_scales[:], 0)
+        nc.vector.memset(one[:], 1.0)
+        nc.vector.memset(w2_planes[:], 0)
+        for quad in range(4):
+            nc.gpsimd.dma_start(
+                table_scales[32 * quad : 32 * quad + 8, :], tab_scales.bitcast(I32)[:, 4 * quad : 4 * quad + 4, :]
+            )
+        for quad in range(4):
+            nc.gpsimd.dma_start(
+                w2_planes[32 * quad : 32 * quad + 4, :, :],
+                w2_scales.bitcast(I32)[:, 4 * quad : 4 * quad + 4, :].rearrange("b r c -> r b c"),
+            )
+
+        nc.scalar.activation(out=zero[:], in_=one[:], func=ACT.Ln)
+        gain_rows = keep.tile([P, 2 * PACK, Q], F32, name="gain_rows")
+        nc.scalar.copy(
+            out=gain_rows[:],
+            in_=gain_sb[:].rearrange("p b t -> p (b t)").unsqueeze(2).to_broadcast([P, 2 * PACK, Q]),
+        )
+
+        v_codes = [keep.tile([P, S], U32, name=f"v_codes{a}", align_bytes=64) for a in range(2)]
+        v_planes = keep.tile([P, S], U8, name="v_planes", align_bytes=64)
+        w1_bf = {
+            (a, b): keep.tile([P, K_PASS * PACK], BF16, name=f"w1_bf{a}{b}", align_bytes=64)
+            for a in range(2)
+            for b in range(2)
+        }
+        w1_codes = {
+            (a, b): keep.tile([P, K_PASS], U32, name=f"w1_codes{a}{b}", align_bytes=64)
+            for a in range(2)
+            for b in range(2)
+        }
+        w1_planes = {
+            (a, b): keep.tile([P, K_PASS], U8, name=f"w1_planes{a}{b}", align_bytes=64)
+            for a in range(2)
+            for b in range(2)
+        }
+
+        def round_w1(a, b, copy):
+            copy(
+                out=w1_bf[a, b][:].rearrange("p (t m j) -> p m t j", t=PACK, j=PACK),
+                in_=w1_raw[a, b][:].rearrange("p j (m t) -> p m t j", t=PACK),
+            )
+
+        def quantize_w1(a, b):
+            nc.vector.quantize_mx(out=w1_codes[a, b][:].bitcast(FP8X4), scales=w1_planes[a, b][:], in_=w1_bf[a, b][:])
+
+        nc.vector.tensor_copy(v_codes[0][:], table[0][:].bitcast(U32).indirect(offs_sb[:]))
+        nc.vector.tensor_copy(v_planes[:], table_scales[:].bitcast(U8).indirect(offs_sb[:]))
+        for a in range(2):
+            round_w1(a, 0, nc.scalar.copy)
+            quantize_w1(a, 0)
+        for s in range(2):
+            nc.vector.tensor_copy(
+                v_codes[1][:, s * BANK : (s + 1) * BANK],
+                table[1][:].bitcast(U32).indirect(offs_sb[:, s * BANK // LANES : (s + 1) * BANK // LANES]),
+            )
+
+        def project(b, t):
+            banks = [psum.tile([P, BANK], F32, name="x_bank") for s in range(2)]
+            cols = slice(t * P, (t + 1) * P)
+            for a in range(2):
+                for s in range(2):
+                    frames = slice(s * BANK, (s + 1) * BANK)
+                    nc.tensor.matmul_mx(
+                        out=banks[s][:],
+                        lhsT=w1_codes[a, b][:, cols].bitcast(FP8X4),
+                        lhsT_scale=w1_planes[a, b][:, cols],
+                        rhs=v_codes[a][:, frames].bitcast(FP8X4),
+                        rhs_scale=v_planes[4 * a :, frames],
+                        start=(a == 0),
+                        stop=(a == 1),
+                    )
+            magnitude = ring.tile([P, S], F32, name="magnitude")
+            h = ring.tile([P, S], F32, name="h")
+            for s in range(2):
+                frames = slice(s * BANK, (s + 1) * BANK)
+                nc.scalar.activation(out=magnitude[:, frames], in_=banks[s][:], func=ACT.Abs, bias=zero[:])
+                nc.scalar.activation(out=h[:, frames], in_=magnitude[:, frames], func=ACT.Ln, bias=one[:])
+            return h
+
+        first = [keep.tile([P, PACK, Q], F32, name=f"first{b}") for b in range(2)]
+        second = [keep.tile([P, PACK, Q], F32, name=f"second{b}") for b in range(2)]
+        z_bf = [keep.tile([P, Q * PACK], BF16, name=f"z_bf{b}", align_bytes=64) for b in range(2)]
+        z_codes = [keep.tile([P, Q], U32, name=f"z_codes{b}", align_bytes=64) for b in range(2)]
+        z_planes = [keep.tile([P, Q], U8, name=f"z_planes{b}", align_bytes=64) for b in range(2)]
+
+        def pick(picked, pos_sb, h, b, t, q0, q1):
+            nc.vector.tensor_tensor(
+                picked[b][:, t, q0:q1],
+                h[:].indirect(pos_sb[:, q0 // LANES : q1 // LANES]),
+                gain_rows[:, PACK * b + t, q0:q1],
+                ALU.mult,
+            )
+
+        def subtract(b, q0, q1):
+            nc.vector.tensor_tensor(
+                z_bf[b][:, PACK * q0 : PACK * q1].rearrange("p (c i t) -> p c t i", i=2, t=PACK),
+                first[b][:, :, q0:q1].rearrange("p t (c i) -> p c t i", i=2),
+                second[b][:, :, q0:q1].rearrange("p t (c i) -> p c t i", i=2),
+                ALU.subtract,
+            )
+
+        def quantize_z(b, q0, q1):
+            nc.vector.quantize_mx(
+                out=z_codes[b][:, q0:q1].bitcast(FP8X4),
+                scales=z_planes[b][:, q0:q1],
+                in_=z_bf[b][:, PACK * q0 : PACK * q1],
+            )
+
+        def logits(q0, q1, copies):
+            width = q1 - q0
+            per_bank = BANK // width
+            for n0 in range(0, N // P, per_bank):
+                bank = psum.tile([P, per_bank, width], F32, name="out_bank")
+                for n in range(n0, n0 + per_bank):
+                    for q in range(q0, q1, P):
+                        for b in range(2):
+                            nc.tensor.matmul_mx(
+                                out=bank[:, n - n0, q - q0 : q - q0 + P],
+                                lhsT=w2_codes[:, b, 2 * n * P : 2 * (n + 1) * P].bitcast(FP4X4),
+                                lhsT_scale=w2_planes[:, b, :].bitcast(U8)[:, n * P : (n + 1) * P],
+                                rhs=z_codes[b][:, q : q + P].bitcast(FP8X4),
+                                rhs_scale=z_planes[b][:, q : q + P],
+                                start=(b == 0),
+                                stop=(b == 1),
+                            )
+                staged = ring.tile([P, per_bank, width], F32, name="staged", bufs=4)
+                copies[(n0 // per_bank) % len(copies)](out=staged[:], in_=bank[:])
+                nc.sync.dma_start(
+                    out[n0 * P : (n0 + per_bank) * P, q0:q1].rearrange("(n p) q -> p n q", p=P), staged[:]
+                )
+
+        for t in range(PACK):
+            h = project(0, t)
+            if t == 0:
+                round_w1(0, 1, nc.vector.tensor_copy)
+            if t == PACK - 1:
+                round_w1(1, 1, nc.scalar.copy)
+                quantize_w1(0, 1)
+                quantize_w1(1, 1)
+            pick(first, pos1_sb, h, 0, t, 0, Q)
+            pick(second, pos2_sb, h, 0, t, 0, Q)
+        for t in range(PACK - 1):
+            h = project(1, t)
+            if t == 0:
+                subtract(0, 0, Q)
+            pick(first, pos1_sb, h, 1, t, 0, Q)
+            if t == 0:
+                quantize_z(0, 0, Q)
+            pick(second, pos2_sb, h, 1, t, 0, Q)
+        h = project(1, PACK - 1)
+        width = Q // CHUNKS
+        pick(first, pos1_sb, h, 1, PACK - 1, 0, width)
+        pick(second, pos2_sb, h, 1, PACK - 1, 0, width)
+        for c in range(CHUNKS):
+            q0, q1 = c * width, (c + 1) * width
+            last = c == CHUNKS - 1
+            if not last:
+                pick(first, pos1_sb, h, 1, PACK - 1, q1, q1 + width)
+            subtract(1, q0, q1)
+            if not last:
+                pick(second, pos2_sb, h, 1, PACK - 1, q1, q1 + width)
+            quantize_z(1, q0, q1)
+            logits(q0, q1, [nc.scalar.copy, nc.vector.tensor_copy] if last else [nc.scalar.copy])

@@ -1,6 +1,7 @@
 from contextlib import ExitStack
 
 import concourse.mybir as mybir
+from concourse.masks import make_identity
 
 K, T, S, Q, H, N = 1024, 4096, 1024, 512, 1024, 512
 FLOPS = 2 * K * H * S + 2 * H * N * Q
@@ -21,7 +22,9 @@ PACK = 4
 K_PASS = P * PACK
 BANK = 512
 LANES = 16
-CHUNKS = 2
+HALF = K_PASS // 2
+CHUNKS = [0, 256, 384, 512]
+PROBES = []
 
 
 def tile_list_frame_delta_logits_kernel(
@@ -30,142 +33,206 @@ def tile_list_frame_delta_logits_kernel(
     nc = tc.nc
     with ExitStack() as ctx:
         keep = ctx.enter_context(tc.tile_pool(name="keep", bufs=1))
-        ring = ctx.enter_context(tc.tile_pool(name="ring", bufs=3))
-        psum = ctx.enter_context(tc.psum_pool(name="psum", bufs=4))
+        ring = ctx.enter_context(tc.tile_pool(name="ring", bufs=4))
+        psum = ctx.enter_context(tc.psum_pool(name="psum", bufs=6))
 
         offs_sb = keep.tile([P, S // LANES], U16, name="offs_sb")
         pos1_sb = keep.tile([P, Q // LANES], U16, name="pos1_sb")
         pos2_sb = keep.tile([P, Q // LANES], U16, name="pos2_sb")
-        gain_sb = keep.tile([P, 2, PACK], F32, name="gain_sb")
+        gain_lo = keep.tile([P, PACK], F32, name="gain_lo")
+        gain_hi = keep.tile([P, PACK], F32, name="gain_hi")
         table = [keep.tile([P, T], I32, name=f"table{a}") for a in range(2)]
-        table_scales = keep.tile([P, T // 4], I32, name="table_scales")
-        w1_raw = {
-            (a, b): keep.tile([P, PACK, K_PASS], F32, name=f"w1_raw{a}{b}") for a in range(2) for b in range(2)
-        }
+        table_scales = keep.tile([P, T // 4], I32, name="table_scales", tag="kilo", align_bytes=64)
+        lo_raw = [keep.tile([P, 2, PACK, HALF], F32, name=f"lo_raw{g}") for g in range(2)]
+        hi_raw = [keep.tile([P, PACK, K_PASS], F32, name=f"hi_raw{a}") for a in range(2)]
         w2_codes = keep.tile([P, 2, 2 * N], U8, name="w2_codes", align_bytes=64)
         w2_planes = keep.tile([P, 2, N // 4], I32, name="w2_planes", align_bytes=64)
         one = keep.tile([P, 1], F32, name="one")
         zero = keep.tile([P, 1], F32, name="zero")
+        ident = keep.tile([P, P], F32, name="ident")
+
+        def probe(label, ap, dtype):
+            if label in PROBES:
+                spot = keep.tile([P, 1], dtype, name=f"probe_{label}")
+                nc.gpsimd.tensor_copy(spot[:], ap)
 
         def load_table(a):
             nc.sync.dma_start(table[a][:], tab_words[a].rearrange("p t i -> p (t i)").bitcast(I32))
 
-        def load_w1(a, b):
-            rows = w1[a * K_PASS : (a + 1) * K_PASS, b * K_PASS : (b + 1) * K_PASS]
-            nc.sync.dma_start(w1_raw[a, b][:], rows.rearrange("(p j) c -> p j c", j=PACK))
+        def load_w1(dst, a, c0, c1):
+            nc.sync.dma_start(dst, w1[a * K_PASS : (a + 1) * K_PASS, c0:c1].rearrange("(p j) c -> p j c", j=PACK))
 
-        nc.scalar.dma_start(gain_sb[:], gain.rearrange("(b p t) -> p b t", b=2, t=PACK))
+        nc.gpsimd.memset(table_scales[:], 0)
         nc.sync.dma_start(offs_sb[:], offs)
-        load_table(0)
-        load_w1(0, 0)
-        load_w1(1, 0)
-        nc.sync.dma_start(pos1_sb[:], pos1)
-        nc.sync.dma_start(pos2_sb[:], pos2)
-        load_table(1)
-        load_w1(0, 1)
-        load_w1(1, 1)
-        nc.sync.dma_start(w2_codes[:].bitcast(I32), w2_words.rearrange("b p c -> p b c").bitcast(I32))
-
-        nc.vector.memset(table_scales[:], 0)
-        nc.vector.memset(one[:], 1.0)
-        nc.vector.memset(w2_planes[:], 0)
+        with nc.allow_non_contiguous_dma(reason="one gain value to a partition"):
+            nc.sync.dma_start(gain_lo[:], gain[0:K_PASS].rearrange("(j p) -> p j", p=P))
+        nc.sync.dma_start(gain_hi[:], gain[K_PASS:H].rearrange("(p t) -> p t", t=PACK))
         for quad in range(4):
             nc.gpsimd.dma_start(
                 table_scales[32 * quad : 32 * quad + 8, :], tab_scales.bitcast(I32)[:, 4 * quad : 4 * quad + 4, :]
             )
+        load_table(0)
+        for a in range(2):
+            load_w1(lo_raw[0][:, a], a, 0, HALF)
+        nc.sync.dma_start(pos1_sb[:], pos1)
+        nc.sync.dma_start(pos2_sb[:], pos2)
+        load_table(1)
+        for a in range(2):
+            load_w1(lo_raw[1][:, a], a, HALF, K_PASS)
+        for a in range(2):
+            load_w1(hi_raw[a][:], a, K_PASS, H)
+        nc.sync.dma_start(w2_codes[:].bitcast(I32), w2_words.rearrange("b p c -> p b c").bitcast(I32))
+
+        nc.vector.memset(one[:], 1.0)
+        nc.vector.memset(w2_planes[:], 0)
         for quad in range(4):
-            nc.gpsimd.dma_start(
+            nc.sync.dma_start(
                 w2_planes[32 * quad : 32 * quad + 4, :, :],
                 w2_scales.bitcast(I32)[:, 4 * quad : 4 * quad + 4, :].rearrange("b r c -> r b c"),
             )
+        make_identity(nc, ident[:])
 
         nc.scalar.activation(out=zero[:], in_=one[:], func=ACT.Ln)
-        gain_rows = keep.tile([P, 2 * PACK, Q], F32, name="gain_rows")
-        nc.scalar.copy(
-            out=gain_rows[:],
-            in_=gain_sb[:].rearrange("p b t -> p (b t)").unsqueeze(2).to_broadcast([P, 2 * PACK, Q]),
-        )
+        gain_rows = [keep.tile([P, PACK, Q], F32, name=f"gain_rows{b}") for b in range(2)]
+        minus_rows = keep.tile([P, PACK, Q], F32, name="minus_rows")
+        spread_lo = gain_lo[:].unsqueeze(2).to_broadcast([P, PACK, Q])
+        nc.scalar.copy(out=gain_rows[0][:], in_=spread_lo)
+        nc.scalar.activation(out=minus_rows[:], in_=spread_lo, func=ACT.Copy, scale=-1.0)
 
-        v_codes = [keep.tile([P, S], U32, name=f"v_codes{a}", align_bytes=64) for a in range(2)]
+        v_codes = [keep.tile([P, S], U32, name="v_codes0", align_bytes=64)]
         v_planes = keep.tile([P, S], U8, name="v_planes", align_bytes=64)
-        w1_bf = {
-            (a, b): keep.tile([P, K_PASS * PACK], BF16, name=f"w1_bf{a}{b}", align_bytes=64)
-            for a in range(2)
-            for b in range(2)
-        }
-        w1_codes = {
-            (a, b): keep.tile([P, K_PASS], U32, name=f"w1_codes{a}{b}", align_bytes=64)
-            for a in range(2)
-            for b in range(2)
-        }
-        w1_planes = {
-            (a, b): keep.tile([P, K_PASS], U8, name=f"w1_planes{a}{b}", align_bytes=64)
-            for a in range(2)
-            for b in range(2)
-        }
+        lo_bf = [keep.tile([P, 2, HALF * PACK], BF16, name=f"lo_bf{g}", align_bytes=64) for g in range(2)]
+        lo_codes = [keep.tile([P, 2, HALF], U32, name=f"lo_codes{g}", align_bytes=64) for g in range(2)]
+        lo_planes = [keep.tile([P, 2, HALF], U8, name=f"lo_planes{g}", align_bytes=64) for g in range(2)]
+        hi_bf = [keep.tile([P, K_PASS * PACK], BF16, name=f"hi_bf{a}", tag=f"hi_bf{a}", align_bytes=64) for a in range(2)]
+        hi_codes = [keep.tile([P, K_PASS], U32, name=f"hi_codes{a}", align_bytes=64) for a in range(2)]
+        hi_planes = [keep.tile([P, K_PASS], U8, name=f"hi_planes{a}", align_bytes=64) for a in range(2)]
 
-        def round_w1(a, b, copy):
+        def round_lo(g, a, copy):
             copy(
-                out=w1_bf[a, b][:].rearrange("p (t m j) -> p m t j", t=PACK, j=PACK),
-                in_=w1_raw[a, b][:].rearrange("p j (m t) -> p m t j", t=PACK),
+                out=lo_bf[g][:, a].rearrange("p (c i j) -> p c j i", i=4, j=PACK),
+                in_=lo_raw[g][:, a].rearrange("p j (c i) -> p c j i", i=4),
             )
 
-        def quantize_w1(a, b):
-            nc.vector.quantize_mx(out=w1_codes[a, b][:].bitcast(FP8X4), scales=w1_planes[a, b][:], in_=w1_bf[a, b][:])
+        def quantize_lo(g):
+            nc.vector.quantize_mx(
+                out=lo_codes[g][:].rearrange("p a c -> p (a c)").bitcast(FP8X4),
+                scales=lo_planes[g][:].rearrange("p a c -> p (a c)"),
+                in_=lo_bf[g][:].rearrange("p a c -> p (a c)"),
+            )
+
+        def round_hi(a, copy):
+            copy(
+                out=hi_bf[a][:].rearrange("p (t m j) -> p m t j", t=PACK, j=PACK),
+                in_=hi_raw[a][:].rearrange("p j (m t) -> p m t j", t=PACK),
+            )
+
+        def quantize_hi(a):
+            nc.vector.quantize_mx(out=hi_codes[a][:].bitcast(FP8X4), scales=hi_planes[a][:], in_=hi_bf[a][:])
 
         nc.vector.tensor_copy(v_codes[0][:], table[0][:].bitcast(U32).indirect(offs_sb[:]))
         nc.vector.tensor_copy(v_planes[:], table_scales[:].bitcast(U8).indirect(offs_sb[:]))
         for a in range(2):
-            round_w1(a, 0, nc.scalar.copy)
-            quantize_w1(a, 0)
+            round_lo(0, a, nc.scalar.copy)
+        quantize_lo(0)
+        nc.scalar.copy(out=gain_rows[1][:], in_=gain_hi[:].unsqueeze(2).to_broadcast([P, PACK, Q]))
+        probe("x", table[1][:, T - 1 : T], I32)
+        v_codes.append(keep.tile([P, S], U32, name="v_codes1", tag="kilo", align_bytes=64))
         for s in range(2):
             nc.vector.tensor_copy(
                 v_codes[1][:, s * BANK : (s + 1) * BANK],
                 table[1][:].bitcast(U32).indirect(offs_sb[:, s * BANK // LANES : (s + 1) * BANK // LANES]),
             )
+        for a in range(2):
+            round_lo(1, a, nc.vector.tensor_copy)
+        quantize_lo(1)
+
+        def stationary(b, t, a):
+            if b == 0:
+                cols = slice((t % 2) * P, (t % 2 + 1) * P)
+                return lo_codes[t // 2][:, a, cols], lo_planes[t // 2][:, a, cols]
+            cols = slice(t * P, (t + 1) * P)
+            return hi_codes[a][:, cols], hi_planes[a][:, cols]
 
         def project(b, t):
-            banks = [psum.tile([P, BANK], F32, name="x_bank") for s in range(2)]
-            cols = slice(t * P, (t + 1) * P)
-            for a in range(2):
-                for s in range(2):
+            banks = [psum.tile([P, BANK], F32, name="x_bank", bufs=2) for s in range(2)]
+            for s in range(2):
+                for a in range(2):
                     frames = slice(s * BANK, (s + 1) * BANK)
+                    codes, planes = stationary(b, t, a)
                     nc.tensor.matmul_mx(
                         out=banks[s][:],
-                        lhsT=w1_codes[a, b][:, cols].bitcast(FP8X4),
-                        lhsT_scale=w1_planes[a, b][:, cols],
+                        lhsT=codes.bitcast(FP8X4),
+                        lhsT_scale=planes,
                         rhs=v_codes[a][:, frames].bitcast(FP8X4),
                         rhs_scale=v_planes[4 * a :, frames],
                         start=(a == 0),
                         stop=(a == 1),
                     )
-            magnitude = ring.tile([P, S], F32, name="magnitude")
+            magnitude = ring.tile([P, S], F32, name="magnitude", bufs=2)
             h = ring.tile([P, S], F32, name="h")
-            for s in range(2):
-                frames = slice(s * BANK, (s + 1) * BANK)
-                nc.scalar.activation(out=magnitude[:, frames], in_=banks[s][:], func=ACT.Abs, bias=zero[:])
-                nc.scalar.activation(out=h[:, frames], in_=magnitude[:, frames], func=ACT.Ln, bias=one[:])
+            piece = BANK // 2 if (b, t) == (0, 0) else BANK
+            for pair in range(0, S, 2 * piece):
+                for f in (pair, pair + piece):
+                    nc.scalar.activation(
+                        out=magnitude[:, f : f + piece],
+                        in_=banks[f // BANK][:, f % BANK : f % BANK + piece],
+                        func=ACT.Abs,
+                        bias=zero[:],
+                    )
+                for f in (pair, pair + piece):
+                    nc.scalar.activation(
+                        out=h[:, f : f + piece], in_=magnitude[:, f : f + piece], func=ACT.Ln, bias=one[:]
+                    )
+            probe(f"h{b}{t}", h[:, S - 1 : S], F32)
             return h
 
-        first = [keep.tile([P, PACK, Q], F32, name=f"first{b}") for b in range(2)]
-        second = [keep.tile([P, PACK, Q], F32, name=f"second{b}") for b in range(2)]
+        first = keep.tile([P, PACK, Q], F32, name="first")
+        second = keep.tile([P, PACK, Q], F32, name="second")
+        terms = []
+        z_rows = keep.tile([P, Q // P, K_PASS], BF16, name="z_rows")
         z_bf = [keep.tile([P, Q * PACK], BF16, name=f"z_bf{b}", align_bytes=64) for b in range(2)]
         z_codes = [keep.tile([P, Q], U32, name=f"z_codes{b}", align_bytes=64) for b in range(2)]
         z_planes = [keep.tile([P, Q], U8, name=f"z_planes{b}", align_bytes=64) for b in range(2)]
 
-        def pick(picked, pos_sb, h, b, t, q0, q1):
+        def pick(picked, pos_sb, rows, h, t, q0, q1):
             nc.vector.tensor_tensor(
-                picked[b][:, t, q0:q1],
+                picked[:, q0:q1],
                 h[:].indirect(pos_sb[:, q0 // LANES : q1 // LANES]),
-                gain_rows[:, PACK * b + t, q0:q1],
+                rows[:, t, q0:q1],
                 ALU.mult,
             )
 
-        def subtract(b, q0, q1):
+        def turn_delta(t):
+            bank = psum.tile([P, Q // P, P], F32, name="aux_bank")
+            for g in range(Q // P):
+                for i in range(2):
+                    nc.tensor.matmul(
+                        bank[:, g, :],
+                        terms[t][i][:, g * P : (g + 1) * P],
+                        ident[:],
+                        start=(i == 0),
+                        stop=(i == 1),
+                        is_transpose=True,
+                    )
+            nc.scalar.copy(out=z_rows[:, :, t * P : (t + 1) * P], in_=bank[:])
+
+        def turn_back(g0):
+            bank = psum.tile([P, 2, 2, P], F32, name="aux_bank")
+            for g in range(2):
+                words = z_rows[:, g0 + g, :].bitcast(F32)
+                for u in range(2):
+                    nc.tensor.transpose(bank[:, g, u, :], words[:, u : K_PASS // 2 : 2], ident[:])
+            nc.scalar.copy(
+                out=z_bf[0][:, PACK * g0 * P : PACK * (g0 + 2) * P].bitcast(F32).rearrange("p (g q u) -> p g q u", g=2, u=2),
+                in_=bank[:].rearrange("p g u q -> p g q u"),
+            )
+
+        def subtract(q0, q1):
             nc.vector.tensor_tensor(
-                z_bf[b][:, PACK * q0 : PACK * q1].rearrange("p (c i t) -> p c t i", i=2, t=PACK),
-                first[b][:, :, q0:q1].rearrange("p t (c i) -> p c t i", i=2),
-                second[b][:, :, q0:q1].rearrange("p t (c i) -> p c t i", i=2),
+                z_bf[1][:, PACK * q0 : PACK * q1].rearrange("p (c i t) -> p c t i", i=2, t=PACK),
+                first[:, :, q0:q1].rearrange("p t (c i) -> p c t i", i=2),
+                second[:, :, q0:q1].rearrange("p t (c i) -> p c t i", i=2),
                 ALU.subtract,
             )
 
@@ -178,9 +245,9 @@ def tile_list_frame_delta_logits_kernel(
 
         def logits(q0, q1, copies):
             width = q1 - q0
-            per_bank = BANK // width
+            per_bank = len(copies) if q1 == Q else BANK // width
             for n0 in range(0, N // P, per_bank):
-                bank = psum.tile([P, per_bank, width], F32, name="out_bank")
+                bank = psum.tile([P, per_bank, width], F32, name="aux_bank")
                 for n in range(n0, n0 + per_bank):
                     for q in range(q0, q1, P):
                         for b in range(2):
@@ -193,7 +260,7 @@ def tile_list_frame_delta_logits_kernel(
                                 start=(b == 0),
                                 stop=(b == 1),
                             )
-                staged = ring.tile([P, per_bank, width], F32, name="staged", bufs=4)
+                staged = ring.tile([P, per_bank, width], F32, name="staged", bufs=5)
                 copies[(n0 // per_bank) % len(copies)](out=staged[:], in_=bank[:])
                 nc.sync.dma_start(
                     out[n0 * P : (n0 + per_bank) * P, q0:q1].rearrange("(n p) q -> p n q", p=P), staged[:]
@@ -201,33 +268,39 @@ def tile_list_frame_delta_logits_kernel(
 
         for t in range(PACK):
             h = project(0, t)
+            if t == 1:
+                round_hi(1, nc.scalar.copy)
+            tags = [f"hi_bf{i}" if t == 2 else f"term{t}{i}" for i in range(2)]
+            terms.append([keep.tile([P, Q], F32, name=f"term{t}{i}", tag=tags[i], align_bytes=64) for i in range(2)])
+            pick(terms[t][0], pos1_sb, gain_rows[0], h, t, 0, Q)
+            pick(terms[t][1], pos2_sb, minus_rows, h, t, 0, Q)
             if t == 0:
-                round_w1(0, 1, nc.vector.tensor_copy)
-            if t == PACK - 1:
-                round_w1(1, 1, nc.scalar.copy)
-                quantize_w1(0, 1)
-                quantize_w1(1, 1)
-            pick(first, pos1_sb, h, 0, t, 0, Q)
-            pick(second, pos2_sb, h, 0, t, 0, Q)
+                round_hi(0, nc.vector.tensor_copy)
+            if t == 1:
+                quantize_hi(0)
+            if t == 1:
+                quantize_hi(1)
         for t in range(PACK - 1):
+            turn_delta(t)
             h = project(1, t)
-            if t == 0:
-                subtract(0, 0, Q)
-            pick(first, pos1_sb, h, 1, t, 0, Q)
-            if t == 0:
-                quantize_z(0, 0, Q)
-            pick(second, pos2_sb, h, 1, t, 0, Q)
+            pick(first[:, t], pos1_sb, gain_rows[1], h, t, 0, Q)
+            pick(second[:, t], pos2_sb, gain_rows[1], h, t, 0, Q)
+        turn_delta(PACK - 1)
         h = project(1, PACK - 1)
-        width = Q // CHUNKS
-        pick(first, pos1_sb, h, 1, PACK - 1, 0, width)
-        pick(second, pos2_sb, h, 1, PACK - 1, 0, width)
-        for c in range(CHUNKS):
-            q0, q1 = c * width, (c + 1) * width
-            last = c == CHUNKS - 1
+        for g0 in range(0, Q // P, 2):
+            turn_back(g0)
+        probe("z0", z_bf[0][:, PACK * Q - 1 : PACK * Q], BF16)
+        pick(first[:, PACK - 1], pos1_sb, gain_rows[1], h, PACK - 1, CHUNKS[0], CHUNKS[1])
+        pick(second[:, PACK - 1], pos2_sb, gain_rows[1], h, PACK - 1, CHUNKS[0], CHUNKS[1])
+        for c in range(len(CHUNKS) - 1):
+            q0, q1 = CHUNKS[c], CHUNKS[c + 1]
+            last = q1 == Q
             if not last:
-                pick(first, pos1_sb, h, 1, PACK - 1, q1, q1 + width)
-            subtract(1, q0, q1)
+                pick(first[:, PACK - 1], pos1_sb, gain_rows[1], h, PACK - 1, q1, CHUNKS[c + 2])
+            subtract(q0, q1)
+            if c == 0:
+                quantize_z(0, 0, Q)
             if not last:
-                pick(second, pos2_sb, h, 1, PACK - 1, q1, q1 + width)
+                pick(second[:, PACK - 1], pos2_sb, gain_rows[1], h, PACK - 1, q1, CHUNKS[c + 2])
             quantize_z(1, q0, q1)
             logits(q0, q1, [nc.scalar.copy, nc.vector.tensor_copy] if last else [nc.scalar.copy])

@@ -22,7 +22,6 @@ PACK = 4
 K_PASS = P * PACK
 BANK = 512
 LANES = 16
-HALF = K_PASS // 2
 CHUNKS = [0, 256, 384, 512]
 PROBES = []
 
@@ -34,17 +33,19 @@ def tile_list_frame_delta_logits_kernel(
     with ExitStack() as ctx:
         keep = ctx.enter_context(tc.tile_pool(name="keep", bufs=1))
         ring = ctx.enter_context(tc.tile_pool(name="ring", bufs=4))
-        psum = ctx.enter_context(tc.psum_pool(name="psum", bufs=6))
+        psum = ctx.enter_context(tc.psum_pool(name="psum", bufs=1))
 
+        banks = [psum.tile([P, BANK], F32, name=f"bank{i}") for i in range(8)]
         offs_sb = keep.tile([P, S // LANES], U16, name="offs_sb")
         pos1_sb = keep.tile([P, Q // LANES], U16, name="pos1_sb")
         pos2_sb = keep.tile([P, Q // LANES], U16, name="pos2_sb")
+        gain_flat = keep.tile([P, P], F32, name="gain_flat")
         gain_lo = keep.tile([P, PACK], F32, name="gain_lo")
         gain_hi = keep.tile([P, PACK], F32, name="gain_hi")
-        table = [keep.tile([P, T], I32, name=f"table{a}") for a in range(2)]
+        table = [keep.tile([P, T], I32, name=f"table{a}", tag=f"table{a}", align_bytes=64) for a in range(2)]
         table_scales = keep.tile([P, T // 4], I32, name="table_scales", tag="kilo", align_bytes=64)
-        lo_raw = [keep.tile([P, 2, PACK, HALF], F32, name=f"lo_raw{g}") for g in range(2)]
-        hi_raw = [keep.tile([P, PACK, K_PASS], F32, name=f"hi_raw{a}") for a in range(2)]
+        lo_raw = [keep.tile([P, 2 * PACK, P], F32, name=f"lo_raw{t}", align_bytes=64) for t in range(PACK)]
+        hi_raw = [keep.tile([P, PACK, K_PASS], F32, name=f"hi_raw{a}", tag=f"hi_raw{a}", align_bytes=64) for a in range(2)]
         w2_codes = keep.tile([P, 2, 2 * N], U8, name="w2_codes", align_bytes=64)
         w2_planes = keep.tile([P, 2, N // 4], I32, name="w2_planes", align_bytes=64)
         one = keep.tile([P, 1], F32, name="one")
@@ -62,106 +63,80 @@ def tile_list_frame_delta_logits_kernel(
         def load_w1(dst, a, c0, c1):
             nc.sync.dma_start(dst, w1[a * K_PASS : (a + 1) * K_PASS, c0:c1].rearrange("(p j) c -> p j c", j=PACK))
 
-        nc.gpsimd.memset(table_scales[:], 0)
-        nc.sync.dma_start(offs_sb[:], offs)
-        with nc.allow_non_contiguous_dma(reason="one gain value to a partition"):
-            nc.sync.dma_start(gain_lo[:], gain[0:K_PASS].rearrange("(j p) -> p j", p=P))
-        nc.sync.dma_start(gain_hi[:], gain[K_PASS:H].rearrange("(p t) -> p t", t=PACK))
+        nc.vector.memset(gain_flat[:], 0.0)
+        nc.vector.memset(table_scales[:], 0)
+        nc.vector.memset(one[:], 1.0)
+        make_identity(nc, ident[:])
+        nc.scalar.dma_start(gain_flat[0:PACK, :], gain[0:K_PASS].rearrange("(t p) -> t p", p=P))
         for quad in range(4):
             nc.gpsimd.dma_start(
                 table_scales[32 * quad : 32 * quad + 8, :], tab_scales.bitcast(I32)[:, 4 * quad : 4 * quad + 4, :]
             )
+        nc.sync.dma_start(offs_sb[:], offs)
         load_table(0)
         for a in range(2):
-            load_w1(lo_raw[0][:, a], a, 0, HALF)
+            load_w1(lo_raw[0][:, a * PACK : (a + 1) * PACK], a, 0, P)
+        load_table(1)
         nc.sync.dma_start(pos1_sb[:], pos1)
         nc.sync.dma_start(pos2_sb[:], pos2)
-        load_table(1)
-        for a in range(2):
-            load_w1(lo_raw[1][:, a], a, HALF, K_PASS)
+        for t in range(1, PACK):
+            for a in range(2):
+                load_w1(lo_raw[t][:, a * PACK : (a + 1) * PACK], a, t * P, (t + 1) * P)
         for a in range(2):
             load_w1(hi_raw[a][:], a, K_PASS, H)
+        nc.sync.dma_start(gain_hi[:], gain[K_PASS:H].rearrange("(p t) -> p t", t=PACK))
         nc.sync.dma_start(w2_codes[:].bitcast(I32), w2_words.rearrange("b p c -> p b c").bitcast(I32))
-
-        nc.vector.memset(one[:], 1.0)
         nc.vector.memset(w2_planes[:], 0)
         for quad in range(4):
             nc.sync.dma_start(
                 w2_planes[32 * quad : 32 * quad + 4, :, :],
                 w2_scales.bitcast(I32)[:, 4 * quad : 4 * quad + 4, :].rearrange("b r c -> r b c"),
             )
-        make_identity(nc, ident[:])
 
         nc.scalar.activation(out=zero[:], in_=one[:], func=ACT.Ln)
-        gain_rows = [keep.tile([P, PACK, Q], F32, name=f"gain_rows{b}") for b in range(2)]
-        minus_rows = keep.tile([P, PACK, Q], F32, name="minus_rows")
-        spread_lo = gain_lo[:].unsqueeze(2).to_broadcast([P, PACK, Q])
-        nc.scalar.copy(out=gain_rows[0][:], in_=spread_lo)
-        nc.scalar.activation(out=minus_rows[:], in_=spread_lo, func=ACT.Copy, scale=-1.0)
+        plus_rows = keep.tile([P, PACK * Q], F32, name="plus_rows", align_bytes=64)
+        minus_rows = keep.tile([P, PACK * Q], F32, name="minus_rows")
 
+        magnitudes = [keep.tile([P, S], F32, name=f"magnitude{i}", align_bytes=64)[:] for i in range(4)]
         v_codes = [keep.tile([P, S], U32, name="v_codes0", align_bytes=64)]
         v_planes = keep.tile([P, S], U8, name="v_planes", align_bytes=64)
-        lo_bf = [keep.tile([P, 2, HALF * PACK], BF16, name=f"lo_bf{g}", align_bytes=64) for g in range(2)]
-        lo_codes = [keep.tile([P, 2, HALF], U32, name=f"lo_codes{g}", align_bytes=64) for g in range(2)]
-        lo_planes = [keep.tile([P, 2, HALF], U8, name=f"lo_planes{g}", align_bytes=64) for g in range(2)]
-        hi_bf = [keep.tile([P, K_PASS * PACK], BF16, name=f"hi_bf{a}", tag=f"hi_bf{a}", align_bytes=64) for a in range(2)]
-        hi_codes = [keep.tile([P, K_PASS], U32, name=f"hi_codes{a}", align_bytes=64) for a in range(2)]
+        lo_codes = [keep.tile([P, 2 * P], U32, name=f"lo_codes{t}", align_bytes=64) for t in range(PACK)]
+        lo_planes = [keep.tile([P, 2 * P], U8, name=f"lo_planes{t}", align_bytes=64) for t in range(PACK)]
+        hi_codes = [
+            keep.tile([P, K_PASS], U32, name="hi_codes0", tag="hi_raw1", align_bytes=64),
+            keep.tile([P, K_PASS], U32, name="hi_codes1", align_bytes=64),
+        ]
         hi_planes = [keep.tile([P, K_PASS], U8, name=f"hi_planes{a}", align_bytes=64) for a in range(2)]
 
-        def round_lo(g, a, copy):
+        def round_lo(dst, t, copy):
             copy(
-                out=lo_bf[g][:, a].rearrange("p (c i j) -> p c j i", i=4, j=PACK),
-                in_=lo_raw[g][:, a].rearrange("p j (c i) -> p c j i", i=4),
+                out=dst.rearrange("p (a c i j) -> p a c j i", a=2, i=4, j=PACK),
+                in_=lo_raw[t][:].rearrange("p (a j) (c i) -> p a c j i", a=2, i=4),
             )
 
-        def quantize_lo(g):
-            nc.vector.quantize_mx(
-                out=lo_codes[g][:].rearrange("p a c -> p (a c)").bitcast(FP8X4),
-                scales=lo_planes[g][:].rearrange("p a c -> p (a c)"),
-                in_=lo_bf[g][:].rearrange("p a c -> p (a c)"),
-            )
-
-        def round_hi(a, copy):
+        def round_hi(dst, a, copy):
             copy(
-                out=hi_bf[a][:].rearrange("p (t m j) -> p m t j", t=PACK, j=PACK),
+                out=dst.rearrange("p (t m j) -> p m t j", t=PACK, j=PACK),
                 in_=hi_raw[a][:].rearrange("p j (m t) -> p m t j", t=PACK),
             )
 
-        def quantize_hi(a):
-            nc.vector.quantize_mx(out=hi_codes[a][:].bitcast(FP8X4), scales=hi_planes[a][:], in_=hi_bf[a][:])
+        def quantize(codes, planes, src):
+            nc.vector.quantize_mx(out=codes.bitcast(FP8X4), scales=planes, in_=src)
 
-        nc.vector.tensor_copy(v_codes[0][:], table[0][:].bitcast(U32).indirect(offs_sb[:]))
-        nc.vector.tensor_copy(v_planes[:], table_scales[:].bitcast(U8).indirect(offs_sb[:]))
-        for a in range(2):
-            round_lo(0, a, nc.scalar.copy)
-        quantize_lo(0)
-        nc.scalar.copy(out=gain_rows[1][:], in_=gain_hi[:].unsqueeze(2).to_broadcast([P, PACK, Q]))
-        probe("x", table[1][:, T - 1 : T], I32)
-        v_codes.append(keep.tile([P, S], U32, name="v_codes1", tag="kilo", align_bytes=64))
-        for s in range(2):
-            nc.vector.tensor_copy(
-                v_codes[1][:, s * BANK : (s + 1) * BANK],
-                table[1][:].bitcast(U32).indirect(offs_sb[:, s * BANK // LANES : (s + 1) * BANK // LANES]),
-            )
-        for a in range(2):
-            round_lo(1, a, nc.vector.tensor_copy)
-        quantize_lo(1)
-
-        def stationary(b, t, a):
-            if b == 0:
-                cols = slice((t % 2) * P, (t % 2 + 1) * P)
-                return lo_codes[t // 2][:, a, cols], lo_planes[t // 2][:, a, cols]
-            cols = slice(t * P, (t + 1) * P)
+        def stationary(i, a):
+            if i < PACK:
+                cols = slice(a * P, (a + 1) * P)
+                return lo_codes[i][:, cols], lo_planes[i][:, cols]
+            cols = slice((i - PACK) * P, (i - PACK + 1) * P)
             return hi_codes[a][:, cols], hi_planes[a][:, cols]
 
-        def project(b, t):
-            banks = [psum.tile([P, BANK], F32, name="x_bank", bufs=2) for s in range(2)]
+        def project(i, pair, magnitude):
             for s in range(2):
                 for a in range(2):
                     frames = slice(s * BANK, (s + 1) * BANK)
-                    codes, planes = stationary(b, t, a)
+                    codes, planes = stationary(i, a)
                     nc.tensor.matmul_mx(
-                        out=banks[s][:],
+                        out=banks[2 * pair + s][:],
                         lhsT=codes.bitcast(FP8X4),
                         lhsT_scale=planes,
                         rhs=v_codes[a][:, frames].bitcast(FP8X4),
@@ -169,42 +144,110 @@ def tile_list_frame_delta_logits_kernel(
                         start=(a == 0),
                         stop=(a == 1),
                     )
-            magnitude = ring.tile([P, S], F32, name="magnitude", bufs=2)
             h = ring.tile([P, S], F32, name="h")
-            piece = BANK // 2 if (b, t) == (0, 0) else BANK
-            for pair in range(0, S, 2 * piece):
-                for f in (pair, pair + piece):
+            piece = BANK // 2 if i == 0 else BANK
+            for both in range(0, S, 2 * piece):
+                for f in (both, both + piece):
                     nc.scalar.activation(
                         out=magnitude[:, f : f + piece],
-                        in_=banks[f // BANK][:, f % BANK : f % BANK + piece],
+                        in_=banks[2 * pair + f // BANK][:, f % BANK : f % BANK + piece],
                         func=ACT.Abs,
                         bias=zero[:],
                     )
-                for f in (pair, pair + piece):
+                for f in (both, both + piece):
                     nc.scalar.activation(
                         out=h[:, f : f + piece], in_=magnitude[:, f : f + piece], func=ACT.Ln, bias=one[:]
                     )
-            probe(f"h{b}{t}", h[:, S - 1 : S], F32)
+            probe(f"h{i}", h[:, S - 1 : S], F32)
             return h
 
-        first = keep.tile([P, PACK, Q], F32, name="first")
-        second = keep.tile([P, PACK, Q], F32, name="second")
-        terms = []
+        def offsets(pos_sb, q0, q1):
+            return pos_sb[:, q0 // LANES : q1 // LANES]
+
+        def pick_scaled(dst, pos_sb, rows, h, t):
+            nc.vector.tensor_tensor(dst, h[:].indirect(pos_sb[:]), rows[:, t * Q : (t + 1) * Q], ALU.mult)
+
+        nc.vector.tensor_copy(v_planes[:], table_scales[:].bitcast(U8).indirect(offs_sb[:]))
+        nc.vector.tensor_copy(v_codes[0][:], table[0][:].bitcast(U32).indirect(offs_sb[:]))
+        lo_bf0 = keep.tile([P, 2 * K_PASS], BF16, name="lo_bf0", align_bytes=64)
+        round_lo(lo_bf0[:], 0, nc.scalar.copy)
+        quantize(lo_codes[0][:], lo_planes[0][:], lo_bf0[:])
+        nc.tensor.transpose(banks[6][:, 0:P], gain_flat[:], ident[:])
+        nc.scalar.copy(out=gain_lo[:], in_=banks[6][:, 0:PACK])
+        for t0 in (0, 2):
+            spread = gain_lo[:, t0 : t0 + 2].unsqueeze(2).to_broadcast([P, 2, Q])
+            rows = slice(t0 * Q, (t0 + 2) * Q)
+            nc.scalar.copy(out=plus_rows[:, rows].rearrange("p (t q) -> p t q", t=2), in_=spread)
+            nc.scalar.activation(
+                out=minus_rows[:, rows].rearrange("p (t q) -> p t q", t=2), in_=spread, func=ACT.Copy, scale=-1.0
+            )
+        probe("x", table[1][:, T - 1 : T], I32)
+        v_codes.append(keep.tile([P, S], U32, name="v_codes1", tag="kilo", align_bytes=64))
+        for s in range(2):
+            nc.vector.tensor_copy(
+                v_codes[1][:, s * BANK : (s + 1) * BANK],
+                table[1][:].bitcast(U32).indirect(offsets(offs_sb, s * BANK, (s + 1) * BANK)),
+            )
+        lo_bf12 = keep.tile([P, 4 * K_PASS], BF16, name="lo_bf12", tag="table1", align_bytes=64)
+        round_lo(lo_bf12[:, 0 : 2 * K_PASS], 1, nc.vector.tensor_copy)
+        quantize(lo_codes[1][:], lo_planes[1][:], lo_bf12[:, 0 : 2 * K_PASS])
+        round_lo(lo_bf12[:, 2 * K_PASS :], 2, nc.vector.tensor_copy)
+
+        spare = [keep.tile([P, Q], F32, name=f"term{i}")[:] for i in range(4)]
+        lo_flat = [raw[:].rearrange("p j c -> p (j c)") for raw in lo_raw]
+        terms = [
+            [lo_flat[2][:, 0:Q], lo_flat[2][:, Q:]],
+            [spare[0], spare[1]],
+            [spare[2], plus_rows[:, Q // 2 : 3 * Q // 2]],
+            [spare[3], lo_flat[3][:, Q:]],
+        ]
+
+        h = project(0, 0, magnitudes[0])
+        pick_scaled(terms[0][0], pos1_sb, plus_rows, h, 0)
+        quantize(lo_codes[2][:], lo_planes[2][:], lo_bf12[:, 2 * K_PASS :])
+        pick_scaled(terms[0][1], pos2_sb, minus_rows, h, 0)
+        h = project(1, 1, magnitudes[1])
+        lo_bf3 = magnitudes[1][:, 0:K_PASS].bitcast(BF16)
+        round_lo(lo_bf3, 3, nc.scalar.copy)
+        pick_scaled(terms[1][0], pos1_sb, plus_rows, h, 1)
+        quantize(lo_codes[3][:], lo_planes[3][:], lo_bf3)
+        pick_scaled(terms[1][1], pos2_sb, minus_rows, h, 1)
+        h = project(2, 0, lo_flat[3])
+        hi_bf = [lo_flat[3].bitcast(BF16), plus_rows[:, Q : 3 * Q].bitcast(BF16)]
+        round_hi(hi_bf[0], 0, nc.scalar.copy)
+        pick_scaled(terms[2][0], pos1_sb, plus_rows, h, 2)
+        round_hi(hi_bf[1], 1, nc.vector.tensor_copy)
+        for a in range(2):
+            quantize(hi_codes[a][:, 0:P], hi_planes[a][:, 0:P], hi_bf[a][:, 0:K_PASS])
+        pick_scaled(terms[2][1], pos2_sb, minus_rows, h, 2)
+        for a in range(2):
+            quantize(hi_codes[a][:, P : 2 * P], hi_planes[a][:, P : 2 * P], hi_bf[a][:, K_PASS : 2 * K_PASS])
+        h = project(3, 1, hi_raw[0][:, 0:2].rearrange("p j c -> p (j c)"))
+        pick_scaled(terms[3][0], pos1_sb, plus_rows, h, 3)
+        for a in range(2):
+            quantize(hi_codes[a][:, 2 * P :], hi_planes[a][:, 2 * P :], hi_bf[a][:, 2 * K_PASS :])
+        pick_scaled(terms[3][1], pos2_sb, minus_rows, h, 3)
+        probe("g3", terms[3][1][:, Q - 1 : Q], F32)
+
+        delta = keep.tile([P, PACK, Q], F32, name="delta")
         z_rows = keep.tile([P, Q // P, K_PASS], BF16, name="z_rows")
-        z_bf = [keep.tile([P, Q * PACK], BF16, name=f"z_bf{b}", align_bytes=64) for b in range(2)]
+        z_lo = [keep.tile([P, 2 * PACK * P], BF16, name=f"z_lo{i}", align_bytes=64) for i in range(2)]
+        z_hi = [keep.tile([P, 2 * PACK * P], BF16, name="z_hi0", align_bytes=64)[:]]
+        z_hi.append(keep.tile([P, PACK * P], BF16, name="z_hi1", align_bytes=64)[:])
+        z_hi.append(z_lo[0][:, 0 : PACK * P])
         z_codes = [keep.tile([P, Q], U32, name=f"z_codes{b}", align_bytes=64) for b in range(2)]
         z_planes = [keep.tile([P, Q], U8, name=f"z_planes{b}", align_bytes=64) for b in range(2)]
 
-        def pick(picked, pos_sb, rows, h, t, q0, q1):
+        def pick_second(second, h, q0, q1):
+            nc.vector.tensor_copy(second[:, q0:q1], h[:].indirect(offsets(pos2_sb, q0, q1)))
+
+        def pick_delta(second, h, t, q0, q1):
             nc.vector.tensor_tensor(
-                picked[:, q0:q1],
-                h[:].indirect(pos_sb[:, q0 // LANES : q1 // LANES]),
-                rows[:, t, q0:q1],
-                ALU.mult,
+                delta[:, t, q0:q1], h[:].indirect(offsets(pos1_sb, q0, q1)), second[:, q0:q1], ALU.subtract
             )
 
         def turn_delta(t):
-            bank = psum.tile([P, Q // P, P], F32, name="aux_bank")
+            bank = banks[4 + t][:].rearrange("p (g r) -> p g r", r=P)
             for g in range(Q // P):
                 for i in range(2):
                     nc.tensor.matmul(
@@ -215,92 +258,84 @@ def tile_list_frame_delta_logits_kernel(
                         stop=(i == 1),
                         is_transpose=True,
                     )
-            nc.scalar.copy(out=z_rows[:, :, t * P : (t + 1) * P], in_=bank[:])
+            nc.scalar.copy(out=z_rows[:, :, t * P : (t + 1) * P], in_=bank)
 
-        def turn_back(g0):
-            bank = psum.tile([P, 2, 2, P], F32, name="aux_bank")
+        def turn_back(half):
+            bank = banks[half][:].rearrange("p (g u q) -> p g u q", g=2, u=2)
             for g in range(2):
-                words = z_rows[:, g0 + g, :].bitcast(F32)
+                words = z_rows[:, 2 * half + g, :].bitcast(F32)
                 for u in range(2):
                     nc.tensor.transpose(bank[:, g, u, :], words[:, u : K_PASS // 2 : 2], ident[:])
             nc.scalar.copy(
-                out=z_bf[0][:, PACK * g0 * P : PACK * (g0 + 2) * P].bitcast(F32).rearrange("p (g q u) -> p g q u", g=2, u=2),
-                in_=bank[:].rearrange("p g u q -> p g q u"),
+                out=z_lo[half][:].bitcast(F32).rearrange("p (g q u) -> p g q u", g=2, u=2),
+                in_=bank.rearrange("p g u q -> p g q u"),
             )
 
-        def subtract(q0, q1):
+        def scale_delta(c):
+            q0, q1 = CHUNKS[c], CHUNKS[c + 1]
             nc.vector.tensor_tensor(
-                z_bf[1][:, PACK * q0 : PACK * q1].rearrange("p (c i t) -> p c t i", i=2, t=PACK),
-                first[:, :, q0:q1].rearrange("p t (c i) -> p c t i", i=2),
-                second[:, :, q0:q1].rearrange("p t (c i) -> p c t i", i=2),
-                ALU.subtract,
+                z_hi[c].rearrange("p (c i t) -> p c t i", i=2, t=PACK),
+                delta[:, :, q0:q1].rearrange("p t (c i) -> p c t i", i=2),
+                gain_hi[:].unsqueeze(1).unsqueeze(3).to_broadcast([P, (q1 - q0) // 2, PACK, 2]),
+                ALU.mult,
             )
 
-        def quantize_z(b, q0, q1):
-            nc.vector.quantize_mx(
-                out=z_codes[b][:, q0:q1].bitcast(FP8X4),
-                scales=z_planes[b][:, q0:q1],
-                in_=z_bf[b][:, PACK * q0 : PACK * q1],
-            )
+        def quantize_z(b, q0, q1, src):
+            quantize(z_codes[b][:, q0:q1], z_planes[b][:, q0:q1], src)
 
-        def logits(q0, q1, copies):
-            width = q1 - q0
-            per_bank = len(copies) if q1 == Q else BANK // width
-            for n0 in range(0, N // P, per_bank):
-                bank = psum.tile([P, per_bank, width], F32, name="aux_bank")
+        def logits(g, targets):
+            per_bank = (N // P) // len(targets)
+            for part, (bank_no, copy) in enumerate(targets):
+                bank = banks[bank_no][:, 0 : per_bank * P].rearrange("p (n q) -> p n q", q=P)
+                n0 = part * per_bank
                 for n in range(n0, n0 + per_bank):
-                    for q in range(q0, q1, P):
-                        for b in range(2):
-                            nc.tensor.matmul_mx(
-                                out=bank[:, n - n0, q - q0 : q - q0 + P],
-                                lhsT=w2_codes[:, b, 2 * n * P : 2 * (n + 1) * P].bitcast(FP4X4),
-                                lhsT_scale=w2_planes[:, b, :].bitcast(U8)[:, n * P : (n + 1) * P],
-                                rhs=z_codes[b][:, q : q + P].bitcast(FP8X4),
-                                rhs_scale=z_planes[b][:, q : q + P],
-                                start=(b == 0),
-                                stop=(b == 1),
-                            )
-                staged = ring.tile([P, per_bank, width], F32, name="staged", bufs=5)
-                copies[(n0 // per_bank) % len(copies)](out=staged[:], in_=bank[:])
+                    for b in range(2):
+                        nc.tensor.matmul_mx(
+                            out=bank[:, n - n0, :],
+                            lhsT=w2_codes[:, b, 2 * n * P : 2 * (n + 1) * P].bitcast(FP4X4),
+                            lhsT_scale=w2_planes[:, b, :].bitcast(U8)[:, n * P : (n + 1) * P],
+                            rhs=z_codes[b][:, g * P : (g + 1) * P].bitcast(FP8X4),
+                            rhs_scale=z_planes[b][:, g * P : (g + 1) * P],
+                            start=(b == 0),
+                            stop=(b == 1),
+                        )
+                staged = keep.tile([P, per_bank, P], F32, name=f"staged{g}{part}")
+                copy(out=staged[:], in_=bank)
                 nc.sync.dma_start(
-                    out[n0 * P : (n0 + per_bank) * P, q0:q1].rearrange("(n p) q -> p n q", p=P), staged[:]
+                    out[n0 * P : (n0 + per_bank) * P, g * P : (g + 1) * P].rearrange("(n p) q -> p n q", p=P), staged[:]
                 )
 
-        for t in range(PACK):
-            h = project(0, t)
-            if t == 1:
-                round_hi(1, nc.scalar.copy)
-            tags = [f"hi_bf{i}" if t == 2 else f"term{t}{i}" for i in range(2)]
-            terms.append([keep.tile([P, Q], F32, name=f"term{t}{i}", tag=tags[i], align_bytes=64) for i in range(2)])
-            pick(terms[t][0], pos1_sb, gain_rows[0], h, t, 0, Q)
-            pick(terms[t][1], pos2_sb, minus_rows, h, t, 0, Q)
-            if t == 0:
-                round_hi(0, nc.vector.tensor_copy)
-            if t == 1:
-                quantize_hi(0)
-            if t == 1:
-                quantize_hi(1)
         for t in range(PACK - 1):
+            h = project(PACK + t, (2 + t) % 4, magnitudes[3 - t % 2])
+            second = ring.tile([P, Q], F32, name="second", bufs=2)
+            for q0 in (0, Q // 2):
+                pick_second(second, h, q0, q0 + Q // 2)
+            for q0 in (0, Q // 2):
+                pick_delta(second, h, t, q0, q0 + Q // 2)
+        h = project(2 * PACK - 1, 1, magnitudes[2])
+        for t in range(PACK):
             turn_delta(t)
-            h = project(1, t)
-            pick(first[:, t], pos1_sb, gain_rows[1], h, t, 0, Q)
-            pick(second[:, t], pos2_sb, gain_rows[1], h, t, 0, Q)
-        turn_delta(PACK - 1)
-        h = project(1, PACK - 1)
-        for g0 in range(0, Q // P, 2):
-            turn_back(g0)
-        probe("z0", z_bf[0][:, PACK * Q - 1 : PACK * Q], BF16)
-        pick(first[:, PACK - 1], pos1_sb, gain_rows[1], h, PACK - 1, CHUNKS[0], CHUNKS[1])
-        pick(second[:, PACK - 1], pos2_sb, gain_rows[1], h, PACK - 1, CHUNKS[0], CHUNKS[1])
-        for c in range(len(CHUNKS) - 1):
-            q0, q1 = CHUNKS[c], CHUNKS[c + 1]
-            last = q1 == Q
-            if not last:
-                pick(first[:, PACK - 1], pos1_sb, gain_rows[1], h, PACK - 1, q1, CHUNKS[c + 2])
-            subtract(q0, q1)
-            if c == 0:
-                quantize_z(0, 0, Q)
-            if not last:
-                pick(second[:, PACK - 1], pos2_sb, gain_rows[1], h, PACK - 1, q1, CHUNKS[c + 2])
-            quantize_z(1, q0, q1)
-            logits(q0, q1, [nc.scalar.copy, nc.vector.tensor_copy] if last else [nc.scalar.copy])
+        for half in range(2):
+            turn_back(half)
+        probe("z0", z_lo[1][:, 2 * PACK * P - 1 : 2 * PACK * P], BF16)
+        second = ring.tile([P, Q], F32, name="second", bufs=2)
+        last = PACK - 1
+        pick_second(second, h, CHUNKS[0], CHUNKS[1])
+        pick_second(second, h, CHUNKS[1], CHUNKS[2])
+        pick_delta(second, h, last, CHUNKS[0], CHUNKS[1])
+        pick_delta(second, h, last, CHUNKS[1], CHUNKS[2])
+        scale_delta(0)
+        pick_second(second, h, CHUNKS[2], CHUNKS[3])
+        quantize_z(1, CHUNKS[0], CHUNKS[1], z_hi[0])
+        scale_delta(1)
+        quantize_z(0, 0, Q // 2, z_lo[0][:])
+        logits(0, [(2, nc.scalar.copy)])
+        logits(1, [(3, nc.scalar.copy)])
+        pick_delta(second, h, last, CHUNKS[2], CHUNKS[3])
+        quantize_z(1, CHUNKS[1], CHUNKS[2], z_hi[1])
+        scale_delta(2)
+        quantize_z(0, Q // 2, Q, z_lo[1][:])
+        quantize_z(1, CHUNKS[2], CHUNKS[3], z_hi[2])
+        probe("z1", z_codes[1][:, Q - 1 : Q], U32)
+        logits(2, [(4, nc.scalar.copy)])
+        logits(3, [(5, nc.scalar.copy), (6, nc.vector.tensor_copy)])

@@ -22,7 +22,7 @@ PACK = 4
 K_PASS = P * PACK
 BANK = 512
 LANES = 16
-CHUNKS = [0, 256, 384, 512]
+HALF = K_PASS // 2
 PROBES = []
 
 
@@ -33,6 +33,7 @@ def tile_list_frame_delta_logits_kernel(
     with ExitStack() as ctx:
         keep = ctx.enter_context(tc.tile_pool(name="keep", bufs=1))
         ring = ctx.enter_context(tc.tile_pool(name="ring", bufs=4))
+        shared = ctx.enter_context(tc.tile_pool(name="shared", bufs=1))
         psum = ctx.enter_context(tc.psum_pool(name="psum", bufs=1))
 
         banks = [psum.tile([P, BANK], F32, name=f"bank{i}") for i in range(8)]
@@ -40,12 +41,13 @@ def tile_list_frame_delta_logits_kernel(
         pos1_sb = keep.tile([P, Q // LANES], U16, name="pos1_sb")
         pos2_sb = keep.tile([P, Q // LANES], U16, name="pos2_sb")
         gain_flat = keep.tile([P, P], F32, name="gain_flat")
-        gain_lo = keep.tile([P, PACK], F32, name="gain_lo")
+        lo_bf0 = keep.tile([P, 2 * K_PASS], BF16, name="lo_bf0", tag="chain", align_bytes=64)
+        gain_lo = lo_bf0[:, 0 : 2 * PACK].bitcast(F32)
         gain_hi = keep.tile([P, PACK], F32, name="gain_hi")
         table = [keep.tile([P, T], I32, name=f"table{a}", tag=f"table{a}", align_bytes=64) for a in range(2)]
-        table_scales = keep.tile([P, T // 4], I32, name="table_scales", tag="kilo", align_bytes=64)
-        lo_raw = [keep.tile([P, 2 * PACK, P], F32, name=f"lo_raw{t}", align_bytes=64) for t in range(PACK)]
-        hi_raw = [keep.tile([P, PACK, K_PASS], F32, name=f"hi_raw{a}", tag=f"hi_raw{a}", align_bytes=64) for a in range(2)]
+        table_scales = shared.tile([P, T // 4], I32, name="table_scales", offset=0, align_bytes=64)
+        lo_raw = [keep.tile([P, PACK, K_PASS], F32, name=f"lo_raw{a}", tag=f"lo_raw{a}", align_bytes=64) for a in range(2)]
+        hi_raw = [keep.tile([P, PACK, K_PASS], F32, name=f"hi_raw{a}") for a in range(2)]
         w2_codes = keep.tile([P, 2, 2 * N], U8, name="w2_codes", align_bytes=64)
         w2_planes = keep.tile([P, 2, N // 4], I32, name="w2_planes", align_bytes=64)
         one = keep.tile([P, 1], F32, name="one")
@@ -67,6 +69,7 @@ def tile_list_frame_delta_logits_kernel(
         nc.vector.memset(table_scales[:], 0)
         nc.vector.memset(one[:], 1.0)
         make_identity(nc, ident[:])
+        nc.scalar.dma_start(gain_hi[:], gain[K_PASS:H].rearrange("(p t) -> p t", t=PACK))
         nc.scalar.dma_start(gain_flat[0:PACK, :], gain[0:K_PASS].rearrange("(t p) -> t p", p=P))
         for quad in range(4):
             nc.gpsimd.dma_start(
@@ -74,17 +77,13 @@ def tile_list_frame_delta_logits_kernel(
             )
         nc.sync.dma_start(offs_sb[:], offs)
         load_table(0)
-        for a in range(2):
-            load_w1(lo_raw[0][:, a * PACK : (a + 1) * PACK], a, 0, P)
+        load_w1(lo_raw[0][:], 0, 0, K_PASS)
         load_table(1)
+        load_w1(lo_raw[1][:], 1, 0, K_PASS)
         nc.sync.dma_start(pos1_sb[:], pos1)
         nc.sync.dma_start(pos2_sb[:], pos2)
-        for t in range(1, PACK):
-            for a in range(2):
-                load_w1(lo_raw[t][:, a * PACK : (a + 1) * PACK], a, t * P, (t + 1) * P)
         for a in range(2):
             load_w1(hi_raw[a][:], a, K_PASS, H)
-        nc.sync.dma_start(gain_hi[:], gain[K_PASS:H].rearrange("(p t) -> p t", t=PACK))
         nc.sync.dma_start(w2_codes[:].bitcast(I32), w2_words.rearrange("b p c -> p b c").bitcast(I32))
         nc.vector.memset(w2_planes[:], 0)
         for quad in range(4):
@@ -94,30 +93,38 @@ def tile_list_frame_delta_logits_kernel(
             )
 
         nc.scalar.activation(out=zero[:], in_=one[:], func=ACT.Ln)
-        plus_rows = keep.tile([P, PACK * Q], F32, name="plus_rows", align_bytes=64)
+        plus_rows = keep.tile([P, PACK * Q], F32, name="plus_rows")
         minus_rows = keep.tile([P, PACK * Q], F32, name="minus_rows")
+        hi_rows = keep.tile([P, PACK * Q], F32, name="hi_rows")
+        nc.scalar.copy(
+            out=hi_rows[:].rearrange("p (t q) -> p t q", t=PACK), in_=gain_hi[:].unsqueeze(2).to_broadcast([P, PACK, Q])
+        )
 
-        magnitudes = [keep.tile([P, S], F32, name=f"magnitude{i}", align_bytes=64)[:] for i in range(4)]
+        magnitudes = [keep.tile([P, S], F32, name=f"magnitude{i}")[:] for i in range(2)]
         v_codes = [keep.tile([P, S], U32, name="v_codes0", align_bytes=64)]
         v_planes = keep.tile([P, S], U8, name="v_planes", align_bytes=64)
-        lo_codes = [keep.tile([P, 2 * P], U32, name=f"lo_codes{t}", align_bytes=64) for t in range(PACK)]
-        lo_planes = [keep.tile([P, 2 * P], U8, name=f"lo_planes{t}", align_bytes=64) for t in range(PACK)]
-        hi_codes = [
-            keep.tile([P, K_PASS], U32, name="hi_codes0", tag="hi_raw1", align_bytes=64),
-            keep.tile([P, K_PASS], U32, name="hi_codes1", align_bytes=64),
+        early_codes = [
+            shared.tile([P, HALF], U32, name="early_codes0", offset=T // 2, align_bytes=64),
+            keep.tile([P, HALF], U32, name="early_codes1", align_bytes=64),
         ]
-        hi_planes = [keep.tile([P, K_PASS], U8, name=f"hi_planes{a}", align_bytes=64) for a in range(2)]
+        late_codes = [
+            keep.tile([P, HALF], U32, name="late_codes0", align_bytes=64),
+            keep.tile([P, HALF], U32, name="late_codes1", tag="lo_raw1", align_bytes=64),
+        ]
+        lo_planes = [keep.tile([P, K_PASS], U8, name=f"lo_planes{a}", align_bytes=64) for a in range(2)]
+        hi_codes = keep.tile([P, 2 * K_PASS], U32, name="hi_codes", align_bytes=64)
+        hi_planes = keep.tile([P, 2 * K_PASS], U8, name="hi_planes", align_bytes=64)
 
-        def round_lo(dst, t, copy):
+        def round_lo(dst, a, c0, c1, copy):
             copy(
-                out=dst.rearrange("p (a c i j) -> p a c j i", a=2, i=4, j=PACK),
-                in_=lo_raw[t][:].rearrange("p (a j) (c i) -> p a c j i", a=2, i=4),
+                out=dst.rearrange("p (c i j) -> p c j i", i=4, j=PACK),
+                in_=lo_raw[a][:, :, c0:c1].rearrange("p j (c i) -> p c j i", i=4),
             )
 
-        def round_hi(dst, a, copy):
+        def round_hi(dst, a, m0, m1, copy):
             copy(
-                out=dst.rearrange("p (t m j) -> p m t j", t=PACK, j=PACK),
-                in_=hi_raw[a][:].rearrange("p j (m t) -> p m t j", t=PACK),
+                out=dst.rearrange("p (t m j) -> p m t j", t=PACK, j=PACK)[:, m0:m1],
+                in_=hi_raw[a][:].rearrange("p j (m t) -> p m t j", t=PACK)[:, m0:m1],
             )
 
         def quantize(codes, planes, src):
@@ -125,12 +132,14 @@ def tile_list_frame_delta_logits_kernel(
 
         def stationary(i, a):
             if i < PACK:
-                cols = slice(a * P, (a + 1) * P)
-                return lo_codes[i][:, cols], lo_planes[i][:, cols]
-            cols = slice((i - PACK) * P, (i - PACK + 1) * P)
-            return hi_codes[a][:, cols], hi_planes[a][:, cols]
+                cols = slice(i * P, (i + 1) * P)
+                codes = (early_codes, late_codes)[a][i // 2]
+                return codes[:, (i % 2) * P : (i % 2 + 1) * P], lo_planes[a][:, cols]
+            cols = slice(a * K_PASS + (i - PACK) * P, a * K_PASS + (i - PACK + 1) * P)
+            return hi_codes[:, cols], hi_planes[:, cols]
 
-        def project(i, pair, magnitude):
+        def project(i, magnitude):
+            pair = i % 4
             for s in range(2):
                 for a in range(2):
                     frames = slice(s * BANK, (s + 1) * BANK)
@@ -145,109 +154,102 @@ def tile_list_frame_delta_logits_kernel(
                         stop=(a == 1),
                     )
             h = ring.tile([P, S], F32, name="h")
-            piece = BANK // 2 if i == 0 else BANK
-            for both in range(0, S, 2 * piece):
-                for f in (both, both + piece):
-                    nc.scalar.activation(
-                        out=magnitude[:, f : f + piece],
-                        in_=banks[2 * pair + f // BANK][:, f % BANK : f % BANK + piece],
-                        func=ACT.Abs,
-                        bias=zero[:],
-                    )
-                for f in (both, both + piece):
-                    nc.scalar.activation(
-                        out=h[:, f : f + piece], in_=magnitude[:, f : f + piece], func=ACT.Ln, bias=one[:]
-                    )
+            for s in range(2):
+                frames = slice(s * BANK, (s + 1) * BANK)
+                nc.scalar.activation(out=magnitude[:, frames], in_=banks[2 * pair + s][:], func=ACT.Abs, bias=zero[:])
+            for s in range(2):
+                frames = slice(s * BANK, (s + 1) * BANK)
+                nc.scalar.activation(out=h[:, frames], in_=magnitude[:, frames], func=ACT.Ln, bias=one[:])
             probe(f"h{i}", h[:, S - 1 : S], F32)
             return h
 
         def offsets(pos_sb, q0, q1):
             return pos_sb[:, q0 // LANES : q1 // LANES]
 
-        def pick_scaled(dst, pos_sb, rows, h, t):
-            nc.vector.tensor_tensor(dst, h[:].indirect(pos_sb[:]), rows[:, t * Q : (t + 1) * Q], ALU.mult)
+        def pick_scaled(dst, pos_sb, row, h, q0=0, q1=Q):
+            nc.vector.tensor_tensor(dst[:, q0:q1], h[:].indirect(offsets(pos_sb, q0, q1)), row[:, q0:q1], ALU.mult)
 
-        nc.vector.tensor_copy(v_planes[:], table_scales[:].bitcast(U8).indirect(offs_sb[:]))
+        nc.tensor.transpose(banks[7][:, 0:P], gain_flat[:], ident[:])
+        nc.scalar.copy(out=gain_lo, in_=banks[7][:, 0:PACK])
+        nc.scalar.copy(
+            out=plus_rows[:].rearrange("p (t q) -> p t q", q=Q), in_=gain_lo.unsqueeze(2).to_broadcast([P, PACK, Q])
+        )
+        nc.scalar.activation(
+            out=minus_rows[:].rearrange("p (t q) -> p t q", q=Q),
+            in_=gain_lo.unsqueeze(2).to_broadcast([P, PACK, Q]),
+            func=ACT.Copy,
+            scale=-1.0,
+        )
+        plus = [plus_rows[:, t * Q : (t + 1) * Q] for t in range(PACK)]
+        minus = [minus_rows[:, t * Q : (t + 1) * Q] for t in range(PACK)]
+        upper = [hi_rows[:, t * Q : (t + 1) * Q] for t in range(PACK)]
         nc.vector.tensor_copy(v_codes[0][:], table[0][:].bitcast(U32).indirect(offs_sb[:]))
-        lo_bf0 = keep.tile([P, 2 * K_PASS], BF16, name="lo_bf0", align_bytes=64)
-        round_lo(lo_bf0[:], 0, nc.scalar.copy)
-        quantize(lo_codes[0][:], lo_planes[0][:], lo_bf0[:])
-        nc.tensor.transpose(banks[6][:, 0:P], gain_flat[:], ident[:])
-        nc.scalar.copy(out=gain_lo[:], in_=banks[6][:, 0:PACK])
-        for t0 in (0, 2):
-            spread = gain_lo[:, t0 : t0 + 2].unsqueeze(2).to_broadcast([P, 2, Q])
-            rows = slice(t0 * Q, (t0 + 2) * Q)
-            nc.scalar.copy(out=plus_rows[:, rows].rearrange("p (t q) -> p t q", t=2), in_=spread)
-            nc.scalar.activation(
-                out=minus_rows[:, rows].rearrange("p (t q) -> p t q", t=2), in_=spread, func=ACT.Copy, scale=-1.0
-            )
+        nc.vector.tensor_copy(v_planes[:], table_scales[:].bitcast(U8).indirect(offs_sb[:]))
+        lo_bf1 = shared.tile([P, 2 * K_PASS], BF16, name="lo_bf1", offset=0, align_bytes=64)
+        lo_bf2 = lo_raw[0][:, 0].bitcast(BF16)
+        round_lo(lo_bf0[:], 0, 0, HALF, nc.scalar.copy)
+        round_lo(lo_bf1[:], 0, HALF, K_PASS, nc.vector.tensor_copy)
+        quantize(early_codes[0][:], lo_planes[0][:, 0:HALF], lo_bf0[:])
+        quantize(early_codes[1][:], lo_planes[0][:, HALF:], lo_bf1[:])
+        round_lo(lo_bf2, 1, HALF, K_PASS, nc.scalar.copy)
         probe("x", table[1][:, T - 1 : T], I32)
-        v_codes.append(keep.tile([P, S], U32, name="v_codes1", tag="kilo", align_bytes=64))
+        v_codes.append(keep.tile([P, S], U32, name="v_codes1", tag="chain", align_bytes=64))
         for s in range(2):
             nc.vector.tensor_copy(
                 v_codes[1][:, s * BANK : (s + 1) * BANK],
                 table[1][:].bitcast(U32).indirect(offsets(offs_sb, s * BANK, (s + 1) * BANK)),
             )
-        lo_bf12 = keep.tile([P, 4 * K_PASS], BF16, name="lo_bf12", tag="table1", align_bytes=64)
-        round_lo(lo_bf12[:, 0 : 2 * K_PASS], 1, nc.vector.tensor_copy)
-        quantize(lo_codes[1][:], lo_planes[1][:], lo_bf12[:, 0 : 2 * K_PASS])
-        round_lo(lo_bf12[:, 2 * K_PASS :], 2, nc.vector.tensor_copy)
+        hi_bf = keep.tile([P, 2 * PACK * K_PASS], BF16, name="hi_bf", tag="table1", align_bytes=64)
+        for t in range(2):
+            round_lo(hi_bf[:, t * K_PASS : (t + 1) * K_PASS], 1, t * P, (t + 1) * P, nc.vector.tensor_copy)
+        for t in range(2):
+            cols = slice(t * P, (t + 1) * P)
+            quantize(late_codes[0][:, cols], lo_planes[1][:, cols], hi_bf[:, t * K_PASS : (t + 1) * K_PASS])
+        quantize(late_codes[1][:], lo_planes[1][:, HALF:], lo_bf2)
+        round_hi(hi_bf[:, 0 : 2 * S], 0, 0, P, nc.vector.tensor_copy)
+        work = hi_bf[:, 2 * S :].bitcast(F32)
 
-        spare = [keep.tile([P, Q], F32, name=f"term{i}")[:] for i in range(4)]
-        lo_flat = [raw[:].rearrange("p j c -> p (j c)") for raw in lo_raw]
+        spare = [keep.tile([P, Q], F32, name=f"term{i}")[:] for i in range(5)]
+        raw_flat = hi_raw[0][:].rearrange("p j c -> p (j c)")
         terms = [
-            [lo_flat[2][:, 0:Q], lo_flat[2][:, Q:]],
-            [spare[0], spare[1]],
-            [spare[2], plus_rows[:, Q // 2 : 3 * Q // 2]],
-            [spare[3], lo_flat[3][:, Q:]],
+            [raw_flat[:, 0:Q], raw_flat[:, Q : 2 * Q]],
+            [spare[0], work[:, Q:]],
+            [spare[1], spare[2]],
+            [spare[3], spare[4]],
         ]
+        hi_bf1 = hi_bf[:, 2 * S :]
 
-        h = project(0, 0, magnitudes[0])
-        pick_scaled(terms[0][0], pos1_sb, plus_rows, h, 0)
-        quantize(lo_codes[2][:], lo_planes[2][:], lo_bf12[:, 2 * K_PASS :])
-        pick_scaled(terms[0][1], pos2_sb, minus_rows, h, 0)
-        h = project(1, 1, magnitudes[1])
-        lo_bf3 = magnitudes[1][:, 0:K_PASS].bitcast(BF16)
-        round_lo(lo_bf3, 3, nc.scalar.copy)
-        pick_scaled(terms[1][0], pos1_sb, plus_rows, h, 1)
-        quantize(lo_codes[3][:], lo_planes[3][:], lo_bf3)
-        pick_scaled(terms[1][1], pos2_sb, minus_rows, h, 1)
-        h = project(2, 0, lo_flat[3])
-        hi_bf = [lo_flat[3].bitcast(BF16), plus_rows[:, Q : 3 * Q].bitcast(BF16)]
-        round_hi(hi_bf[0], 0, nc.scalar.copy)
-        pick_scaled(terms[2][0], pos1_sb, plus_rows, h, 2)
-        round_hi(hi_bf[1], 1, nc.vector.tensor_copy)
-        for a in range(2):
-            quantize(hi_codes[a][:, 0:P], hi_planes[a][:, 0:P], hi_bf[a][:, 0:K_PASS])
-        pick_scaled(terms[2][1], pos2_sb, minus_rows, h, 2)
-        for a in range(2):
-            quantize(hi_codes[a][:, P : 2 * P], hi_planes[a][:, P : 2 * P], hi_bf[a][:, K_PASS : 2 * K_PASS])
-        h = project(3, 1, hi_raw[0][:, 0:2].rearrange("p j c -> p (j c)"))
-        pick_scaled(terms[3][0], pos1_sb, plus_rows, h, 3)
-        for a in range(2):
-            quantize(hi_codes[a][:, 2 * P :], hi_planes[a][:, 2 * P :], hi_bf[a][:, 2 * K_PASS :])
-        pick_scaled(terms[3][1], pos2_sb, minus_rows, h, 3)
+        h = project(0, magnitudes[0])
+        pick_scaled(terms[0][0], pos1_sb, plus[0], h)
+        pick_scaled(terms[0][1], pos2_sb, minus[0], h)
+        h = project(1, work)
+        round_hi(hi_bf1, 1, 0, P // 2, nc.scalar.copy)
+        round_hi(hi_bf1, 1, P // 2, P, nc.vector.tensor_copy)
+        pick_scaled(terms[1][0], pos1_sb, plus[1], h)
+        quantize(hi_codes[:], hi_planes[:], hi_bf[:])
+        probe("q", hi_codes[:, 0:1], U32)
+        pick_scaled(terms[1][1], pos2_sb, minus[1], h)
+        h = project(2, hi_raw[1][:, 0:2].rearrange("p j c -> p (j c)"))
+        pick_scaled(terms[2][0], pos1_sb, plus[2], h)
+        pick_scaled(terms[2][1], pos2_sb, minus[2], h)
+        h = project(3, magnitudes[1])
+        pick_scaled(terms[3][0], pos1_sb, plus[3], h)
+        pick_scaled(terms[3][1], pos2_sb, minus[3], h)
         probe("g3", terms[3][1][:, Q - 1 : Q], F32)
 
-        delta = keep.tile([P, PACK, Q], F32, name="delta")
+        first_and_z = keep.tile([P, PACK * Q + HALF + K_PASS], F32, name="first_and_z", align_bytes=64)
+        first = first_and_z[:, 0 : PACK * Q].rearrange("p (t q) -> p t q", q=Q)
+        second = keep.tile([P, PACK, Q], F32, name="second")
         z_rows = keep.tile([P, Q // P, K_PASS], BF16, name="z_rows")
-        z_lo = [keep.tile([P, 2 * PACK * P], BF16, name=f"z_lo{i}", align_bytes=64) for i in range(2)]
-        z_hi = [keep.tile([P, 2 * PACK * P], BF16, name="z_hi0", align_bytes=64)[:]]
-        z_hi.append(keep.tile([P, PACK * P], BF16, name="z_hi1", align_bytes=64)[:])
-        z_hi.append(z_lo[0][:, 0 : PACK * P])
-        z_codes = [keep.tile([P, Q], U32, name=f"z_codes{b}", align_bytes=64) for b in range(2)]
-        z_planes = [keep.tile([P, Q], U8, name=f"z_planes{b}", align_bytes=64) for b in range(2)]
-
-        def pick_second(second, h, q0, q1):
-            nc.vector.tensor_copy(second[:, q0:q1], h[:].indirect(offsets(pos2_sb, q0, q1)))
-
-        def pick_delta(second, h, t, q0, q1):
-            nc.vector.tensor_tensor(
-                delta[:, t, q0:q1], h[:].indirect(offsets(pos1_sb, q0, q1)), second[:, q0:q1], ALU.subtract
-            )
+        z_early = first_and_z[:, PACK * Q - HALF :].bitcast(BF16)
+        z_late = keep.tile([P, S], BF16, name="z_late", align_bytes=64)
+        z_lo = [z_early[:, S:], z_late[:]]
+        z_hi = [z_early[:, 0:S], z_late[:]]
+        z_codes = keep.tile([P, 2 * Q], U32, name="z_codes", align_bytes=64)
+        z_planes = keep.tile([P, 2 * Q], U8, name="z_planes", align_bytes=64)
 
         def turn_delta(t):
-            bank = banks[4 + t][:].rearrange("p (g r) -> p g r", r=P)
+            bank = banks[t][:].rearrange("p (g r) -> p g r", r=P)
             for g in range(Q // P):
                 for i in range(2):
                     nc.tensor.matmul(
@@ -261,81 +263,79 @@ def tile_list_frame_delta_logits_kernel(
             nc.scalar.copy(out=z_rows[:, :, t * P : (t + 1) * P], in_=bank)
 
         def turn_back(half):
-            bank = banks[half][:].rearrange("p (g u q) -> p g u q", g=2, u=2)
+            bank = banks[4 + half][:].rearrange("p (g u q) -> p g u q", g=2, u=2)
             for g in range(2):
                 words = z_rows[:, 2 * half + g, :].bitcast(F32)
                 for u in range(2):
                     nc.tensor.transpose(bank[:, g, u, :], words[:, u : K_PASS // 2 : 2], ident[:])
             nc.scalar.copy(
-                out=z_lo[half][:].bitcast(F32).rearrange("p (g q u) -> p g q u", g=2, u=2),
+                out=z_lo[half].bitcast(F32).rearrange("p (g q u) -> p g q u", g=2, u=2),
                 in_=bank.rearrange("p g u q -> p g q u"),
             )
 
-        def scale_delta(c):
-            q0, q1 = CHUNKS[c], CHUNKS[c + 1]
+        def subtract(dst, q0, q1):
             nc.vector.tensor_tensor(
-                z_hi[c].rearrange("p (c i t) -> p c t i", i=2, t=PACK),
-                delta[:, :, q0:q1].rearrange("p t (c i) -> p c t i", i=2),
-                gain_hi[:].unsqueeze(1).unsqueeze(3).to_broadcast([P, (q1 - q0) // 2, PACK, 2]),
-                ALU.mult,
+                dst.rearrange("p (c i t) -> p c t i", i=2, t=PACK),
+                first[:, :, q0:q1].rearrange("p t (c i) -> p c t i", i=2),
+                second[:, :, q0:q1].rearrange("p t (c i) -> p c t i", i=2),
+                ALU.subtract,
             )
 
-        def quantize_z(b, q0, q1, src):
-            quantize(z_codes[b][:, q0:q1], z_planes[b][:, q0:q1], src)
+        def z_columns(half, b):
+            start = half * Q + (1 - b) * HALF
+            return slice(start, start + HALF)
 
-        def logits(g, targets):
-            per_bank = (N // P) // len(targets)
-            for part, (bank_no, copy) in enumerate(targets):
-                bank = banks[bank_no][:, 0 : per_bank * P].rearrange("p (n q) -> p n q", q=P)
-                n0 = part * per_bank
-                for n in range(n0, n0 + per_bank):
-                    for b in range(2):
-                        nc.tensor.matmul_mx(
-                            out=bank[:, n - n0, :],
-                            lhsT=w2_codes[:, b, 2 * n * P : 2 * (n + 1) * P].bitcast(FP4X4),
-                            lhsT_scale=w2_planes[:, b, :].bitcast(U8)[:, n * P : (n + 1) * P],
-                            rhs=z_codes[b][:, g * P : (g + 1) * P].bitcast(FP8X4),
-                            rhs_scale=z_planes[b][:, g * P : (g + 1) * P],
-                            start=(b == 0),
-                            stop=(b == 1),
-                        )
-                staged = keep.tile([P, per_bank, P], F32, name=f"staged{g}{part}")
+        def logit_pass(bank_no, half, n0, n1, b, groups=(0, P), copy=None):
+            bank = banks[bank_no][:, 0 : (n1 - n0) * HALF].rearrange("p (n q) -> p n q", q=HALF)
+            for n in range(n0, n1):
+                for q in groups:
+                    cols = slice(z_columns(half, b).start + q, z_columns(half, b).start + q + P)
+                    nc.tensor.matmul_mx(
+                        out=bank[:, n - n0, q : q + P],
+                        lhsT=w2_codes[:, b, 2 * n * P : 2 * (n + 1) * P].bitcast(FP4X4),
+                        lhsT_scale=w2_planes[:, b, :].bitcast(U8)[:, n * P : (n + 1) * P],
+                        rhs=z_codes[:, cols].bitcast(FP8X4),
+                        rhs_scale=z_planes[:, cols],
+                        start=(b == 0 and n == n0 and q == 0),
+                        stop=(b == 1 and n == n1 - 1 and q == P),
+                    )
+            if copy is not None:
+                staged = keep.tile([P, n1 - n0, HALF], F32, name=f"staged{bank_no}")
                 copy(out=staged[:], in_=bank)
-                nc.sync.dma_start(
-                    out[n0 * P : (n0 + per_bank) * P, g * P : (g + 1) * P].rearrange("(n p) q -> p n q", p=P), staged[:]
-                )
+                rows = out[n0 * P : n1 * P, half * HALF : (half + 1) * HALF]
+                nc.sync.dma_start(rows.rearrange("(n p) q -> p n q", p=P), staged[:])
 
         for t in range(PACK - 1):
-            h = project(PACK + t, (2 + t) % 4, magnitudes[3 - t % 2])
-            second = ring.tile([P, Q], F32, name="second", bufs=2)
-            for q0 in (0, Q // 2):
-                pick_second(second, h, q0, q0 + Q // 2)
-            for q0 in (0, Q // 2):
-                pick_delta(second, h, t, q0, q0 + Q // 2)
-        h = project(2 * PACK - 1, 1, magnitudes[2])
-        for t in range(PACK):
+            h = project(PACK + t, magnitudes[t % 2])
+            pick_scaled(first[:, t], pos1_sb, upper[t], h)
+            pick_scaled(second[:, t], pos2_sb, upper[t], h)
+        turn_delta(0)
+        h = project(2 * PACK - 1, magnitudes[1])
+        for t in range(1, PACK):
             turn_delta(t)
         for half in range(2):
             turn_back(half)
-        probe("z0", z_lo[1][:, 2 * PACK * P - 1 : 2 * PACK * P], BF16)
-        second = ring.tile([P, Q], F32, name="second", bufs=2)
+        probe("z0", z_late[:, S - 1 : S], BF16)
         last = PACK - 1
-        pick_second(second, h, CHUNKS[0], CHUNKS[1])
-        pick_second(second, h, CHUNKS[1], CHUNKS[2])
-        pick_delta(second, h, last, CHUNKS[0], CHUNKS[1])
-        pick_delta(second, h, last, CHUNKS[1], CHUNKS[2])
-        scale_delta(0)
-        pick_second(second, h, CHUNKS[2], CHUNKS[3])
-        quantize_z(1, CHUNKS[0], CHUNKS[1], z_hi[0])
-        scale_delta(1)
-        quantize_z(0, 0, Q // 2, z_lo[0][:])
-        logits(0, [(2, nc.scalar.copy)])
-        logits(1, [(3, nc.scalar.copy)])
-        pick_delta(second, h, last, CHUNKS[2], CHUNKS[3])
-        quantize_z(1, CHUNKS[1], CHUNKS[2], z_hi[1])
-        scale_delta(2)
-        quantize_z(0, Q // 2, Q, z_lo[1][:])
-        quantize_z(1, CHUNKS[2], CHUNKS[3], z_hi[2])
-        probe("z1", z_codes[1][:, Q - 1 : Q], U32)
-        logits(2, [(4, nc.scalar.copy)])
-        logits(3, [(5, nc.scalar.copy), (6, nc.vector.tensor_copy)])
+        pick_scaled(first[:, last], pos1_sb, upper[last], h, 0, HALF)
+        pick_scaled(second[:, last], pos2_sb, upper[last], h, 0, HALF)
+        subtract(z_hi[0], 0, HALF)
+        pick_scaled(second[:, last], pos2_sb, upper[last], h, HALF, Q)
+        quantize(z_codes[:, 0:Q], z_planes[:, 0:Q], z_early)
+        for pair in range(2):
+            logit_pass(6 + pair, 0, 2 * pair, 2 * pair + 2, 0)
+            logit_pass(6 + pair, 0, 2 * pair, 2 * pair + 2, 1, copy=nc.scalar.copy)
+        pick_scaled(first[:, last], pos1_sb, upper[last], h, HALF, Q)
+        quantize(z_codes[:, z_columns(1, 0)], z_planes[:, z_columns(1, 0)], z_lo[1])
+        for n in range(N // P):
+            logit_pass(n, 1, n, n + 1, 0)
+        for q in (0, P):
+            subtract(z_hi[1][:, PACK * q : PACK * (q + P)], HALF + q, HALF + q + P)
+        for q in (0, P):
+            cols = slice(Q + q, Q + q + P)
+            quantize(z_codes[:, cols], z_planes[:, cols], z_hi[1][:, PACK * q : PACK * (q + P)])
+        probe("z1", z_codes[:, Q + P : Q + P + 1], U32)
+        for n in range(N // P):
+            logit_pass(n, 1, n, n + 1, 1, groups=(0,))
+        for n in range(N // P):
+            logit_pass(n, 1, n, n + 1, 1, groups=(P,), copy=nc.vector.tensor_copy if n % 2 else nc.scalar.copy)

@@ -21,9 +21,10 @@ P = 128
 PACK = 4
 K_PASS = P * PACK
 BANK = 512
+BANKS = 8
 LANES = 16
-HALF = K_PASS // 2
-PROBES = []
+QUAD = 32
+HALF = 256
 
 
 def tile_list_frame_delta_logits_kernel(
@@ -36,7 +37,7 @@ def tile_list_frame_delta_logits_kernel(
         shared = ctx.enter_context(tc.tile_pool(name="shared", bufs=1))
         psum = ctx.enter_context(tc.psum_pool(name="psum", bufs=1))
 
-        banks = [psum.tile([P, BANK], F32, name=f"bank{i}") for i in range(8)]
+        banks = [psum.tile([P, BANK], F32, name=f"bank{i}") for i in range(BANKS)]
         offs_sb = keep.tile([P, S // LANES], U16, name="offs_sb")
         pos1_sb = keep.tile([P, Q // LANES], U16, name="pos1_sb")
         pos2_sb = keep.tile([P, Q // LANES], U16, name="pos2_sb")
@@ -54,11 +55,6 @@ def tile_list_frame_delta_logits_kernel(
         zero = keep.tile([P, 1], F32, name="zero")
         ident = keep.tile([P, P], F32, name="ident")
 
-        def probe(label, ap, dtype):
-            if label in PROBES:
-                spot = keep.tile([P, 1], dtype, name=f"probe_{label}")
-                nc.gpsimd.tensor_copy(spot[:], ap)
-
         def load_table(a):
             nc.sync.dma_start(table[a][:], tab_words[a].rearrange("p t i -> p (t i)").bitcast(I32))
 
@@ -71,24 +67,24 @@ def tile_list_frame_delta_logits_kernel(
         make_identity(nc, ident[:])
         nc.scalar.dma_start(gain_hi[:], gain[K_PASS:H].rearrange("(p t) -> p t", t=PACK))
         nc.scalar.dma_start(gain_flat[0:PACK, :], gain[0:K_PASS].rearrange("(t p) -> t p", p=P))
-        for quad in range(4):
+        for quad in range(P // QUAD):
             nc.gpsimd.dma_start(
-                table_scales[32 * quad : 32 * quad + 8, :], tab_scales.bitcast(I32)[:, 4 * quad : 4 * quad + 4, :]
+                table_scales[QUAD * quad : QUAD * quad + 8, :], tab_scales.bitcast(I32)[:, 4 * quad : 4 * quad + 4, :]
             )
         nc.sync.dma_start(offs_sb[:], offs)
         load_table(0)
         load_w1(lo_raw[0][:], 0, 0, K_PASS)
         load_table(1)
         load_w1(lo_raw[1][:], 1, 0, K_PASS)
+        load_w1(hi_raw[0][:], 0, K_PASS, H)
         nc.sync.dma_start(pos1_sb[:], pos1)
         nc.sync.dma_start(pos2_sb[:], pos2)
-        for a in range(2):
-            load_w1(hi_raw[a][:], a, K_PASS, H)
+        load_w1(hi_raw[1][:], 1, K_PASS, H)
         nc.sync.dma_start(w2_codes[:].bitcast(I32), w2_words.rearrange("b p c -> p b c").bitcast(I32))
         nc.vector.memset(w2_planes[:], 0)
-        for quad in range(4):
+        for quad in range(P // QUAD):
             nc.sync.dma_start(
-                w2_planes[32 * quad : 32 * quad + 4, :, :],
+                w2_planes[QUAD * quad : QUAD * quad + 4, :, :],
                 w2_scales.bitcast(I32)[:, 4 * quad : 4 * quad + 4, :].rearrange("b r c -> r b c"),
             )
 
@@ -139,7 +135,7 @@ def tile_list_frame_delta_logits_kernel(
             return hi_codes[:, cols], hi_planes[:, cols]
 
         def project(i, magnitude):
-            pair = i % 4
+            pair = i % (BANKS // 2)
             for s in range(2):
                 for a in range(2):
                     frames = slice(s * BANK, (s + 1) * BANK)
@@ -160,17 +156,17 @@ def tile_list_frame_delta_logits_kernel(
             for s in range(2):
                 frames = slice(s * BANK, (s + 1) * BANK)
                 nc.scalar.activation(out=h[:, frames], in_=magnitude[:, frames], func=ACT.Ln, bias=one[:])
-            probe(f"h{i}", h[:, S - 1 : S], F32)
             return h
 
-        def offsets(pos_sb, q0, q1):
-            return pos_sb[:, q0 // LANES : q1 // LANES]
+        def offsets(list_sb, j0, j1):
+            return list_sb[:, j0 // LANES : j1 // LANES]
 
         def pick_scaled(dst, pos_sb, row, h, q0=0, q1=Q):
             nc.vector.tensor_tensor(dst[:, q0:q1], h[:].indirect(offsets(pos_sb, q0, q1)), row[:, q0:q1], ALU.mult)
 
-        nc.tensor.transpose(banks[7][:, 0:P], gain_flat[:], ident[:])
-        nc.scalar.copy(out=gain_lo, in_=banks[7][:, 0:PACK])
+        gain_bank = banks[BANKS - 1]
+        nc.tensor.transpose(gain_bank[:, 0:P], gain_flat[:], ident[:])
+        nc.scalar.copy(out=gain_lo, in_=gain_bank[:, 0:PACK])
         nc.scalar.copy(
             out=plus_rows[:].rearrange("p (t q) -> p t q", q=Q), in_=gain_lo.unsqueeze(2).to_broadcast([P, PACK, Q])
         )
@@ -183,6 +179,7 @@ def tile_list_frame_delta_logits_kernel(
         plus = [plus_rows[:, t * Q : (t + 1) * Q] for t in range(PACK)]
         minus = [minus_rows[:, t * Q : (t + 1) * Q] for t in range(PACK)]
         upper = [hi_rows[:, t * Q : (t + 1) * Q] for t in range(PACK)]
+
         nc.vector.tensor_copy(v_codes[0][:], table[0][:].bitcast(U32).indirect(offs_sb[:]))
         nc.vector.tensor_copy(v_planes[:], table_scales[:].bitcast(U8).indirect(offs_sb[:]))
         lo_bf1 = shared.tile([P, 2 * K_PASS], BF16, name="lo_bf1", offset=0, align_bytes=64)
@@ -191,8 +188,8 @@ def tile_list_frame_delta_logits_kernel(
         round_lo(lo_bf1[:], 0, HALF, K_PASS, nc.vector.tensor_copy)
         quantize(early_codes[0][:], lo_planes[0][:, 0:HALF], lo_bf0[:])
         quantize(early_codes[1][:], lo_planes[0][:, HALF:], lo_bf1[:])
+
         round_lo(lo_bf2, 1, HALF, K_PASS, nc.scalar.copy)
-        probe("x", table[1][:, T - 1 : T], I32)
         v_codes.append(keep.tile([P, S], U32, name="v_codes1", tag="chain", align_bytes=64))
         for s in range(2):
             nc.vector.tensor_copy(
@@ -206,28 +203,27 @@ def tile_list_frame_delta_logits_kernel(
             cols = slice(t * P, (t + 1) * P)
             quantize(late_codes[0][:, cols], lo_planes[1][:, cols], hi_bf[:, t * K_PASS : (t + 1) * K_PASS])
         quantize(late_codes[1][:], lo_planes[1][:, HALF:], lo_bf2)
-        round_hi(hi_bf[:, 0 : 2 * S], 0, 0, P, nc.vector.tensor_copy)
-        work = hi_bf[:, 2 * S :].bitcast(F32)
+        round_hi(hi_bf[:, 0 : PACK * K_PASS], 0, 0, P, nc.vector.tensor_copy)
+        hi_bf1 = hi_bf[:, PACK * K_PASS :]
+        hi_bf1_f32 = hi_bf1.bitcast(F32)
 
         spare = [keep.tile([P, Q], F32, name=f"term{i}")[:] for i in range(5)]
         raw_flat = hi_raw[0][:].rearrange("p j c -> p (j c)")
         terms = [
             [raw_flat[:, 0:Q], raw_flat[:, Q : 2 * Q]],
-            [spare[0], work[:, Q:]],
+            [spare[0], hi_bf1_f32[:, Q:]],
             [spare[1], spare[2]],
             [spare[3], spare[4]],
         ]
-        hi_bf1 = hi_bf[:, 2 * S :]
 
         h = project(0, magnitudes[0])
         pick_scaled(terms[0][0], pos1_sb, plus[0], h)
         pick_scaled(terms[0][1], pos2_sb, minus[0], h)
-        h = project(1, work)
+        h = project(1, hi_bf1_f32)
         round_hi(hi_bf1, 1, 0, P // 2, nc.scalar.copy)
         round_hi(hi_bf1, 1, P // 2, P, nc.vector.tensor_copy)
         pick_scaled(terms[1][0], pos1_sb, plus[1], h)
         quantize(hi_codes[:], hi_planes[:], hi_bf[:])
-        probe("q", hi_codes[:, 0:1], U32)
         pick_scaled(terms[1][1], pos2_sb, minus[1], h)
         h = project(2, hi_raw[1][:, 0:2].rearrange("p j c -> p (j c)"))
         pick_scaled(terms[2][0], pos1_sb, plus[2], h)
@@ -235,16 +231,15 @@ def tile_list_frame_delta_logits_kernel(
         h = project(3, magnitudes[1])
         pick_scaled(terms[3][0], pos1_sb, plus[3], h)
         pick_scaled(terms[3][1], pos2_sb, minus[3], h)
-        probe("g3", terms[3][1][:, Q - 1 : Q], F32)
 
         first_and_z = keep.tile([P, PACK * Q + HALF + K_PASS], F32, name="first_and_z", align_bytes=64)
         first = first_and_z[:, 0 : PACK * Q].rearrange("p (t q) -> p t q", q=Q)
         second = keep.tile([P, PACK, Q], F32, name="second")
-        z_rows = keep.tile([P, Q // P, K_PASS], BF16, name="z_rows")
+        z_rows = keep.tile([P, Q // P, 2, HALF], BF16, name="z_rows")
         z_early = first_and_z[:, PACK * Q - HALF :].bitcast(BF16)
-        z_late = keep.tile([P, S], BF16, name="z_late", align_bytes=64)
-        z_lo = [z_early[:, S:], z_late[:]]
-        z_hi = [z_early[:, 0:S], z_late[:]]
+        z_late = keep.tile([P, PACK * HALF], BF16, name="z_late", align_bytes=64)
+        z_lo = [z_early[:, PACK * HALF :], z_late[:]]
+        z_hi = [z_early[:, 0 : PACK * HALF], z_late[:]]
         z_codes = keep.tile([P, 2 * Q], U32, name="z_codes", align_bytes=64)
         z_planes = keep.tile([P, 2 * Q], U8, name="z_planes", align_bytes=64)
 
@@ -260,14 +255,17 @@ def tile_list_frame_delta_logits_kernel(
                         stop=(i == 1),
                         is_transpose=True,
                     )
-            nc.scalar.copy(out=z_rows[:, :, t * P : (t + 1) * P], in_=bank)
+            places = slice(t * P // 2, (t + 1) * P // 2)
+            nc.scalar.copy(
+                out=z_rows[:, :, :, places].rearrange("p g u (m e) -> p g u m e", e=2),
+                in_=bank.rearrange("p g (m u e) -> p g u m e", u=2, e=2),
+            )
 
         def turn_back(half):
-            bank = banks[4 + half][:].rearrange("p (g u q) -> p g u q", g=2, u=2)
+            bank = banks[PACK + half][:].rearrange("p (g u q) -> p g u q", g=2, u=2)
             for g in range(2):
-                words = z_rows[:, 2 * half + g, :].bitcast(F32)
                 for u in range(2):
-                    nc.tensor.transpose(bank[:, g, u, :], words[:, u : K_PASS // 2 : 2], ident[:])
+                    nc.tensor.transpose(bank[:, g, u, :], z_rows[:, 2 * half + g, u].bitcast(F32), ident[:])
             nc.scalar.copy(
                 out=z_lo[half].bitcast(F32).rearrange("p (g q u) -> p g q u", g=2, u=2),
                 in_=bank.rearrange("p g u q -> p g q u"),
@@ -281,15 +279,14 @@ def tile_list_frame_delta_logits_kernel(
                 ALU.subtract,
             )
 
-        def z_columns(half, b):
-            start = half * Q + (1 - b) * HALF
-            return slice(start, start + HALF)
+        def z_start(half, b):
+            return half * Q + (1 - b) * HALF
 
         def logit_pass(bank_no, half, n0, n1, b, groups=(0, P), copy=None):
             bank = banks[bank_no][:, 0 : (n1 - n0) * HALF].rearrange("p (n q) -> p n q", q=HALF)
             for n in range(n0, n1):
                 for q in groups:
-                    cols = slice(z_columns(half, b).start + q, z_columns(half, b).start + q + P)
+                    cols = slice(z_start(half, b) + q, z_start(half, b) + q + P)
                     nc.tensor.matmul_mx(
                         out=bank[:, n - n0, q : q + P],
                         lhsT=w2_codes[:, b, 2 * n * P : 2 * (n + 1) * P].bitcast(FP4X4),
@@ -305,36 +302,37 @@ def tile_list_frame_delta_logits_kernel(
                 rows = out[n0 * P : n1 * P, half * HALF : (half + 1) * HALF]
                 nc.sync.dma_start(rows.rearrange("(n p) q -> p n q", p=P), staged[:])
 
-        for t in range(PACK - 1):
+        last = PACK - 1
+        for t in range(last):
             h = project(PACK + t, magnitudes[t % 2])
             pick_scaled(first[:, t], pos1_sb, upper[t], h)
             pick_scaled(second[:, t], pos2_sb, upper[t], h)
         turn_delta(0)
-        h = project(2 * PACK - 1, magnitudes[1])
+        h = project(PACK + last, magnitudes[last % 2])
         for t in range(1, PACK):
             turn_delta(t)
         for half in range(2):
             turn_back(half)
-        probe("z0", z_late[:, S - 1 : S], BF16)
-        last = PACK - 1
+
         pick_scaled(first[:, last], pos1_sb, upper[last], h, 0, HALF)
         pick_scaled(second[:, last], pos2_sb, upper[last], h, 0, HALF)
         subtract(z_hi[0], 0, HALF)
         pick_scaled(second[:, last], pos2_sb, upper[last], h, HALF, Q)
         quantize(z_codes[:, 0:Q], z_planes[:, 0:Q], z_early)
         for pair in range(2):
-            logit_pass(6 + pair, 0, 2 * pair, 2 * pair + 2, 0)
-            logit_pass(6 + pair, 0, 2 * pair, 2 * pair + 2, 1, copy=nc.scalar.copy)
+            logit_pass(BANKS - 2 + pair, 0, 2 * pair, 2 * pair + 2, 0)
+            logit_pass(BANKS - 2 + pair, 0, 2 * pair, 2 * pair + 2, 1, copy=nc.scalar.copy)
+
         pick_scaled(first[:, last], pos1_sb, upper[last], h, HALF, Q)
-        quantize(z_codes[:, z_columns(1, 0)], z_planes[:, z_columns(1, 0)], z_lo[1])
+        lower_cols = slice(z_start(1, 0), z_start(1, 0) + HALF)
+        quantize(z_codes[:, lower_cols], z_planes[:, lower_cols], z_lo[1])
         for n in range(N // P):
             logit_pass(n, 1, n, n + 1, 0)
         for q in (0, P):
             subtract(z_hi[1][:, PACK * q : PACK * (q + P)], HALF + q, HALF + q + P)
         for q in (0, P):
-            cols = slice(Q + q, Q + q + P)
+            cols = slice(z_start(1, 1) + q, z_start(1, 1) + q + P)
             quantize(z_codes[:, cols], z_planes[:, cols], z_hi[1][:, PACK * q : PACK * (q + P)])
-        probe("z1", z_codes[:, Q + P : Q + P + 1], U32)
         for n in range(N // P):
             logit_pass(n, 1, n, n + 1, 1, groups=(0,))
         for n in range(N // P):

@@ -25,6 +25,12 @@ BANKS = 8
 LANES = 16
 QUAD = 32
 HALF = 256
+ROW = 4 * Q
+AT_SCALES = 0
+AT_TABLE1 = AT_SCALES + T
+AT_FRONT = AT_TABLE1 + 4 * T
+AT_PLUS = AT_FRONT + 4 * ROW
+AT_Z = AT_PLUS + 4 * ROW
 
 
 def tile_list_frame_delta_logits_kernel(
@@ -42,12 +48,19 @@ def tile_list_frame_delta_logits_kernel(
         pos1_sb = keep.tile([P, Q // LANES], U16, name="pos1_sb")
         pos2_sb = keep.tile([P, Q // LANES], U16, name="pos2_sb")
         gain_flat = keep.tile([P, P], F32, name="gain_flat")
-        lo_bf0 = keep.tile([P, 2 * K_PASS], BF16, name="lo_bf0", tag="chain", align_bytes=64)
-        gain_lo = lo_bf0[:, 0 : 2 * PACK].bitcast(F32)
+        front_bf = keep.tile([P, 2 * PACK * HALF], BF16, name="front_bf", tag="chain", align_bytes=64)
+        gain_lo = front_bf[:, PACK * HALF - PACK : PACK * HALF + PACK].bitcast(F32)
         gain_hi = keep.tile([P, PACK], F32, name="gain_hi")
-        table = [keep.tile([P, T], I32, name=f"table{a}", tag=f"table{a}", align_bytes=64) for a in range(2)]
-        table_scales = shared.tile([P, T // 4], I32, name="table_scales", offset=0, align_bytes=64)
-        lo_raw = [keep.tile([P, PACK, K_PASS], F32, name=f"lo_raw{a}", tag=f"lo_raw{a}", align_bytes=64) for a in range(2)]
+        table_scales = shared.tile([P, T // 4], I32, name="table_scales", offset=AT_SCALES, align_bytes=64)
+        table = [
+            keep.tile([P, T], I32, name="table0", align_bytes=64),
+            shared.tile([P, T], I32, name="table1", offset=AT_TABLE1, align_bytes=64),
+        ]
+        front_raw = [
+            keep.tile([P, PACK, HALF], F32, name="front_raw0"),
+            shared.tile([P, PACK, HALF], F32, name="front_raw1", offset=AT_FRONT, align_bytes=64),
+        ]
+        back_raw = [keep.tile([P, PACK, HALF], F32, name=f"back_raw{a}") for a in range(2)]
         hi_raw = [keep.tile([P, PACK, K_PASS], F32, name=f"hi_raw{a}") for a in range(2)]
         w2_codes = keep.tile([P, 2, 2 * N], U8, name="w2_codes", align_bytes=64)
         w2_planes = keep.tile([P, 2, N // 4], I32, name="w2_planes", align_bytes=64)
@@ -73,13 +86,15 @@ def tile_list_frame_delta_logits_kernel(
             )
         nc.sync.dma_start(offs_sb[:], offs)
         load_table(0)
-        load_w1(lo_raw[0][:], 0, 0, K_PASS)
+        for a in range(2):
+            load_w1(front_raw[a][:], a, 0, HALF)
         load_table(1)
-        load_w1(lo_raw[1][:], 1, 0, K_PASS)
-        load_w1(hi_raw[0][:], 0, K_PASS, H)
+        for a in range(2):
+            load_w1(back_raw[a][:], a, HALF, K_PASS)
         nc.sync.dma_start(pos1_sb[:], pos1)
         nc.sync.dma_start(pos2_sb[:], pos2)
-        load_w1(hi_raw[1][:], 1, K_PASS, H)
+        for a in range(2):
+            load_w1(hi_raw[a][:], a, K_PASS, H)
         nc.sync.dma_start(w2_codes[:].bitcast(I32), w2_words.rearrange("b p c -> p b c").bitcast(I32))
         nc.vector.memset(w2_planes[:], 0)
         for quad in range(P // QUAD):
@@ -89,73 +104,67 @@ def tile_list_frame_delta_logits_kernel(
             )
 
         nc.scalar.activation(out=zero[:], in_=one[:], func=ACT.Ln)
-        plus_rows = keep.tile([P, PACK * Q], F32, name="plus_rows")
-        minus_rows = keep.tile([P, PACK * Q], F32, name="minus_rows")
+        plus = [shared.tile([P, Q], F32, name=f"plus{t}", offset=AT_PLUS + t * ROW, align_bytes=64) for t in range(PACK)]
         hi_rows = keep.tile([P, PACK * Q], F32, name="hi_rows")
         nc.scalar.copy(
             out=hi_rows[:].rearrange("p (t q) -> p t q", t=PACK), in_=gain_hi[:].unsqueeze(2).to_broadcast([P, PACK, Q])
         )
+        upper = [hi_rows[:, t * Q : (t + 1) * Q] for t in range(PACK)]
 
-        magnitudes = [keep.tile([P, S], F32, name=f"magnitude{i}")[:] for i in range(2)]
         v_codes = [keep.tile([P, S], U32, name="v_codes0", align_bytes=64)]
         v_planes = keep.tile([P, S], U8, name="v_planes", align_bytes=64)
-        early_codes = [
-            shared.tile([P, HALF], U32, name="early_codes0", offset=T // 2, align_bytes=64),
-            keep.tile([P, HALF], U32, name="early_codes1", align_bytes=64),
-        ]
-        late_codes = [
-            keep.tile([P, HALF], U32, name="late_codes0", align_bytes=64),
-            keep.tile([P, HALF], U32, name="late_codes1", tag="lo_raw1", align_bytes=64),
-        ]
-        lo_planes = [keep.tile([P, K_PASS], U8, name=f"lo_planes{a}", align_bytes=64) for a in range(2)]
-        hi_codes = keep.tile([P, 2 * K_PASS], U32, name="hi_codes", align_bytes=64)
-        hi_planes = keep.tile([P, 2 * K_PASS], U8, name="hi_planes", align_bytes=64)
+        planes = [keep.tile([P, 2 * HALF], U8, name=f"planes{i}", align_bytes=64) for i in range(PACK)]
+        codes = []
 
-        def round_lo(dst, a, c0, c1, copy):
+        def round_lo(dst, raw, c0, c1, copy):
             copy(
                 out=dst.rearrange("p (c i j) -> p c j i", i=4, j=PACK),
-                in_=lo_raw[a][:, :, c0:c1].rearrange("p j (c i) -> p c j i", i=4),
+                in_=raw[:, :, c0:c1].rearrange("p j (c i) -> p c j i", i=4),
             )
 
-        def round_hi(dst, a, m0, m1, copy):
+        def round_hi(dst, a, t0, copy):
             copy(
-                out=dst.rearrange("p (t m j) -> p m t j", t=PACK, j=PACK)[:, m0:m1],
-                in_=hi_raw[a][:].rearrange("p j (m t) -> p m t j", t=PACK)[:, m0:m1],
+                out=dst.rearrange("p (t m j) -> p m j t", t=2, j=PACK),
+                in_=hi_raw[a][:].rearrange("p j (m t) -> p m j t", t=PACK)[:, :, :, t0 : t0 + 2],
             )
 
-        def quantize(codes, planes, src):
-            nc.vector.quantize_mx(out=codes.bitcast(FP8X4), scales=planes, in_=src)
+        def quantize(to_codes, to_planes, src):
+            nc.vector.quantize_mx(out=to_codes.bitcast(FP8X4), scales=to_planes, in_=src)
 
         def stationary(i, a):
-            if i < PACK:
-                cols = slice(i * P, (i + 1) * P)
-                codes = (early_codes, late_codes)[a][i // 2]
-                return codes[:, (i % 2) * P : (i % 2 + 1) * P], lo_planes[a][:, cols]
-            cols = slice(a * K_PASS + (i - PACK) * P, a * K_PASS + (i - PACK + 1) * P)
-            return hi_codes[:, cols], hi_planes[:, cols]
+            c0 = (i % 2) * P
+            return codes[i // 2][a][:, c0 : c0 + P], planes[i // 2][:, a * HALF + c0 : a * HALF + c0 + P]
 
         def project(i, magnitude):
             pair = i % (BANKS // 2)
             for s in range(2):
                 for a in range(2):
                     frames = slice(s * BANK, (s + 1) * BANK)
-                    codes, planes = stationary(i, a)
+                    w_codes, w_planes = stationary(i, a)
                     nc.tensor.matmul_mx(
                         out=banks[2 * pair + s][:],
-                        lhsT=codes.bitcast(FP8X4),
-                        lhsT_scale=planes,
+                        lhsT=w_codes.bitcast(FP8X4),
+                        lhsT_scale=w_planes,
                         rhs=v_codes[a][:, frames].bitcast(FP8X4),
                         rhs_scale=v_planes[4 * a :, frames],
                         start=(a == 0),
                         stop=(a == 1),
                     )
             h = ring.tile([P, S], F32, name="h")
-            for s in range(2):
-                frames = slice(s * BANK, (s + 1) * BANK)
-                nc.scalar.activation(out=magnitude[:, frames], in_=banks[2 * pair + s][:], func=ACT.Abs, bias=zero[:])
-            for s in range(2):
-                frames = slice(s * BANK, (s + 1) * BANK)
-                nc.scalar.activation(out=h[:, frames], in_=magnitude[:, frames], func=ACT.Ln, bias=one[:])
+            if i == 0:
+                steps = [(c, step) for s in range(2) for step in range(2) for c in (2 * s, 2 * s + 1)]
+                width = BANK // 2
+            else:
+                steps = [(c, step) for step in range(2) for c in range(2)]
+                width = BANK
+            for c, step in steps:
+                s, c0 = divmod(c * width, BANK)
+                part = magnitude[s][:, c0 : c0 + width]
+                if step == 0:
+                    bank = banks[2 * pair + s][:, c0 : c0 + width]
+                    nc.scalar.activation(out=part, in_=bank, func=ACT.Abs, bias=zero[:])
+                else:
+                    nc.scalar.activation(out=h[:, c * width : (c + 1) * width], in_=part, func=ACT.Ln, bias=one[:])
             return h
 
         def offsets(list_sb, j0, j1):
@@ -167,80 +176,80 @@ def tile_list_frame_delta_logits_kernel(
         gain_bank = banks[BANKS - 1]
         nc.tensor.transpose(gain_bank[:, 0:P], gain_flat[:], ident[:])
         nc.scalar.copy(out=gain_lo, in_=gain_bank[:, 0:PACK])
-        nc.scalar.copy(
-            out=plus_rows[:].rearrange("p (t q) -> p t q", q=Q), in_=gain_lo.unsqueeze(2).to_broadcast([P, PACK, Q])
-        )
-        nc.scalar.activation(
-            out=minus_rows[:].rearrange("p (t q) -> p t q", q=Q),
-            in_=gain_lo.unsqueeze(2).to_broadcast([P, PACK, Q]),
-            func=ACT.Copy,
-            scale=-1.0,
-        )
-        plus = [plus_rows[:, t * Q : (t + 1) * Q] for t in range(PACK)]
-        minus = [minus_rows[:, t * Q : (t + 1) * Q] for t in range(PACK)]
-        upper = [hi_rows[:, t * Q : (t + 1) * Q] for t in range(PACK)]
+        for t in range(PACK):
+            nc.scalar.copy(out=plus[t][:], in_=gain_lo[:, t : t + 1].to_broadcast([P, Q]))
+        gain_minus = keep.tile([P, PACK], F32, name="gain_minus")
+        nc.scalar.activation(out=gain_minus[:], in_=gain_bank[:, 0:PACK], func=ACT.Copy, scale=-1.0)
 
         nc.vector.tensor_copy(v_codes[0][:], table[0][:].bitcast(U32).indirect(offs_sb[:]))
         nc.vector.tensor_copy(v_planes[:], table_scales[:].bitcast(U8).indirect(offs_sb[:]))
-        lo_bf1 = shared.tile([P, 2 * K_PASS], BF16, name="lo_bf1", offset=0, align_bytes=64)
-        lo_bf2 = lo_raw[0][:, 0].bitcast(BF16)
-        round_lo(lo_bf0[:], 0, 0, HALF, nc.scalar.copy)
-        round_lo(lo_bf1[:], 0, HALF, K_PASS, nc.vector.tensor_copy)
-        quantize(early_codes[0][:], lo_planes[0][:, 0:HALF], lo_bf0[:])
-        quantize(early_codes[1][:], lo_planes[0][:, HALF:], lo_bf1[:])
+        for a in range(2):
+            round_lo(front_bf[:, a * PACK * HALF : (a + 1) * PACK * HALF], front_raw[a], 0, HALF, nc.scalar.copy)
+        front_codes = shared.tile([P, 2 * HALF], U32, name="front_codes", offset=AT_SCALES, align_bytes=64)
+        codes.append([front_codes[:, 0:HALF], front_codes[:, HALF:]])
+        quantize(front_codes[:], planes[0][:], front_bf[:])
+        minus_rows = shared.tile([P, PACK * Q], F32, name="minus_rows", offset=AT_FRONT, align_bytes=64)
+        nc.scalar.copy(
+            out=minus_rows[:].rearrange("p (t q) -> p t q", q=Q),
+            in_=gain_minus[:].unsqueeze(2).to_broadcast([P, PACK, Q]),
+        )
+        minus = [minus_rows[:, t * Q : (t + 1) * Q] for t in range(PACK)]
 
-        round_lo(lo_bf2, 1, HALF, K_PASS, nc.scalar.copy)
         v_codes.append(keep.tile([P, S], U32, name="v_codes1", tag="chain", align_bytes=64))
         for s in range(2):
             nc.vector.tensor_copy(
                 v_codes[1][:, s * BANK : (s + 1) * BANK],
                 table[1][:].bitcast(U32).indirect(offsets(offs_sb, s * BANK, (s + 1) * BANK)),
             )
-        hi_bf = keep.tile([P, 2 * PACK * K_PASS], BF16, name="hi_bf", tag="table1", align_bytes=64)
-        for t in range(2):
-            round_lo(hi_bf[:, t * K_PASS : (t + 1) * K_PASS], 1, t * P, (t + 1) * P, nc.vector.tensor_copy)
-        for t in range(2):
-            cols = slice(t * P, (t + 1) * P)
-            quantize(late_codes[0][:, cols], lo_planes[1][:, cols], hi_bf[:, t * K_PASS : (t + 1) * K_PASS])
-        quantize(late_codes[1][:], lo_planes[1][:, HALF:], lo_bf2)
-        round_hi(hi_bf[:, 0 : PACK * K_PASS], 0, 0, P, nc.vector.tensor_copy)
-        hi_bf1 = hi_bf[:, PACK * K_PASS :]
-        hi_bf1_f32 = hi_bf1.bitcast(F32)
+        back_bf = shared.tile([P, 2 * PACK * HALF], BF16, name="back_bf", offset=AT_TABLE1, align_bytes=64)
+        back_codes = keep.tile([P, 2 * HALF], U32, name="back_codes", align_bytes=64)
+        codes.append([back_codes[:, 0:HALF], back_codes[:, HALF:]])
+        for a in range(2):
+            round_lo(back_bf[:, a * PACK * HALF : (a + 1) * PACK * HALF], back_raw[a], 0, HALF, nc.vector.tensor_copy)
+        for a in range(2):
+            part = back_bf[:, a * PACK * HALF : (a + 1) * PACK * HALF]
+            quantize(codes[1][a], planes[1][:, a * HALF : (a + 1) * HALF], part)
 
-        spare = [keep.tile([P, Q], F32, name=f"term{i}")[:] for i in range(5)]
-        raw_flat = hi_raw[0][:].rearrange("p j c -> p (j c)")
-        terms = [
-            [raw_flat[:, 0:Q], raw_flat[:, Q : 2 * Q]],
-            [spare[0], hi_bf1_f32[:, Q:]],
-            [spare[1], spare[2]],
-            [spare[3], spare[4]],
-        ]
+        terms = [[keep.tile([P, Q], F32, name=f"term{t}_{i}")[:] for i in range(2)] for t in range(PACK)]
+        near_bf = minus_rows[:, 0 : 2 * Q].bitcast(BF16)
+        early = keep.tile([P, S + HALF], F32, name="early", align_bytes=64)
+        far_bf = early[:, HALF:].bitcast(BF16)
+        lower_magnitudes = [early[:, 0:S]] + [early[:, HALF:]] * (PACK - 1)
+        codes.append([])
+        for t in range(PACK):
+            h = project(t, [lower_magnitudes[t][:, 0:BANK], lower_magnitudes[t][:, BANK:]])
+            pick_scaled(terms[t][0], pos1_sb, plus[t], h)
+            if t in (1, 2):
+                a = t - 1
+                near_codes = shared.tile([P, HALF], U32, name=f"near_codes{a}", offset=AT_PLUS + t * ROW, align_bytes=64)
+                codes[2].append(near_codes)
+                part = near_bf[:, a * PACK * HALF : (a + 1) * PACK * HALF]
+                quantize(near_codes[:], planes[2][:, a * HALF : (a + 1) * HALF], part)
+            pick_scaled(terms[t][1], pos2_sb, minus[t], h)
+            if t < 2:
+                round_hi(near_bf[:, t * PACK * HALF : (t + 1) * PACK * HALF], t, 0, nc.vector.tensor_copy)
+        far_codes = keep.tile([P, 2 * HALF], U32, name="far_codes", align_bytes=64)
+        codes.append([far_codes[:, 0:HALF], far_codes[:, HALF:]])
+        for a in range(2):
+            round_hi(far_bf[:, a * PACK * HALF : (a + 1) * PACK * HALF], a, 2, nc.scalar.copy)
+        quantize(far_codes[:], planes[3][:], far_bf)
+        upper_magnitude = [hi_raw[a][:, 0] for a in range(2)]
 
-        h = project(0, magnitudes[0])
-        pick_scaled(terms[0][0], pos1_sb, plus[0], h)
-        pick_scaled(terms[0][1], pos2_sb, minus[0], h)
-        h = project(1, hi_bf1_f32)
-        round_hi(hi_bf1, 1, 0, P // 2, nc.scalar.copy)
-        round_hi(hi_bf1, 1, P // 2, P, nc.vector.tensor_copy)
-        pick_scaled(terms[1][0], pos1_sb, plus[1], h)
-        quantize(hi_codes[:], hi_planes[:], hi_bf[:])
-        pick_scaled(terms[1][1], pos2_sb, minus[1], h)
-        h = project(2, hi_raw[1][:, 0:2].rearrange("p j c -> p (j c)"))
-        pick_scaled(terms[2][0], pos1_sb, plus[2], h)
-        pick_scaled(terms[2][1], pos2_sb, minus[2], h)
-        h = project(3, magnitudes[1])
-        pick_scaled(terms[3][0], pos1_sb, plus[3], h)
-        pick_scaled(terms[3][1], pos2_sb, minus[3], h)
-
-        first_and_z = keep.tile([P, PACK * Q + HALF + K_PASS], F32, name="first_and_z", align_bytes=64)
-        first = first_and_z[:, 0 : PACK * Q].rearrange("p (t q) -> p t q", q=Q)
-        second = keep.tile([P, PACK, Q], F32, name="second")
+        first = keep.tile([P, PACK, Q], F32, name="first")
+        second_and_z = keep.tile([P, PACK * Q + HALF], F32, name="second_and_z", align_bytes=64)
+        second = second_and_z[:, 0 : PACK * Q].rearrange("p (t q) -> p t q", q=Q)
         z_rows = keep.tile([P, Q // P, 2, HALF], BF16, name="z_rows")
-        z_early = first_and_z[:, PACK * Q - HALF :].bitcast(BF16)
+        z_first = shared.tile([P, PACK * HALF], BF16, name="z_first", offset=AT_Z, align_bytes=64)
         z_late = keep.tile([P, PACK * HALF], BF16, name="z_late", align_bytes=64)
-        z_lo = [z_early[:, PACK * HALF :], z_late[:]]
-        z_hi = [z_early[:, 0 : PACK * HALF], z_late[:]]
+        z_lo = [z_first[:], z_late[:]]
+        z_hi = [second_and_z[:, PACK * Q - HALF :].bitcast(BF16), z_late[:]]
         z_codes = keep.tile([P, 2 * Q], U32, name="z_codes", align_bytes=64)
+
+        def z_words(half, b, q0, q1):
+            if (half, b) == (0, 1):
+                return upper_codes[:, q0:q1]
+            return z_codes[:, z_start(half, b) + q0 : z_start(half, b) + q1]
+
         z_planes = keep.tile([P, 2 * Q], U8, name="z_planes", align_bytes=64)
 
         def turn_delta(t):
@@ -255,9 +264,12 @@ def tile_list_frame_delta_logits_kernel(
                         stop=(i == 1),
                         is_transpose=True,
                     )
+
+        def round_delta(t, g0, g1):
+            bank = banks[t][:].rearrange("p (g r) -> p g r", r=P)[:, g0:g1]
             places = slice(t * P // 2, (t + 1) * P // 2)
             nc.scalar.copy(
-                out=z_rows[:, :, :, places].rearrange("p g u (m e) -> p g u m e", e=2),
+                out=z_rows[:, g0:g1, :, places].rearrange("p g u (m e) -> p g u m e", e=2),
                 in_=bank.rearrange("p g (m u e) -> p g u m e", u=2, e=2),
             )
 
@@ -291,7 +303,7 @@ def tile_list_frame_delta_logits_kernel(
                         out=bank[:, n - n0, q : q + P],
                         lhsT=w2_codes[:, b, 2 * n * P : 2 * (n + 1) * P].bitcast(FP4X4),
                         lhsT_scale=w2_planes[:, b, :].bitcast(U8)[:, n * P : (n + 1) * P],
-                        rhs=z_codes[:, cols].bitcast(FP8X4),
+                        rhs=z_words(half, b, q, q + P).bitcast(FP8X4),
                         rhs_scale=z_planes[:, cols],
                         start=(b == 0 and n == n0 and q == 0),
                         stop=(b == 1 and n == n1 - 1 and q == P),
@@ -304,26 +316,30 @@ def tile_list_frame_delta_logits_kernel(
 
         last = PACK - 1
         for t in range(last):
-            h = project(PACK + t, magnitudes[t % 2])
+            h = project(PACK + t, upper_magnitude)
             pick_scaled(first[:, t], pos1_sb, upper[t], h)
             pick_scaled(second[:, t], pos2_sb, upper[t], h)
-        turn_delta(0)
-        h = project(PACK + last, magnitudes[last % 2])
-        for t in range(1, PACK):
+        h = project(PACK + last, upper_magnitude)
+        for t in range(PACK):
             turn_delta(t)
         for half in range(2):
+            for t in range(PACK):
+                round_delta(t, 2 * half, 2 * half + 2)
             turn_back(half)
 
         pick_scaled(first[:, last], pos1_sb, upper[last], h, 0, HALF)
         pick_scaled(second[:, last], pos2_sb, upper[last], h, 0, HALF)
-        subtract(z_hi[0], 0, HALF)
-        pick_scaled(second[:, last], pos2_sb, upper[last], h, HALF, Q)
-        quantize(z_codes[:, 0:Q], z_planes[:, 0:Q], z_early)
-        for pair in range(2):
-            logit_pass(BANKS - 2 + pair, 0, 2 * pair, 2 * pair + 2, 0)
-            logit_pass(BANKS - 2 + pair, 0, 2 * pair, 2 * pair + 2, 1, copy=nc.scalar.copy)
-
         pick_scaled(first[:, last], pos1_sb, upper[last], h, HALF, Q)
+        subtract(z_hi[0], 0, HALF)
+        upper_codes = shared.tile([P, HALF], U32, name="upper_codes", offset=AT_Z, align_bytes=64)
+        for b, src in enumerate((z_lo[0], z_hi[0])):
+            cols = slice(z_start(0, b), z_start(0, b) + HALF)
+            quantize(z_words(0, b, 0, HALF), z_planes[:, cols], src)
+        pick_scaled(second[:, last], pos2_sb, upper[last], h, HALF, Q)
+        for b, copy in enumerate((None, nc.scalar.copy)):
+            for pair in range(2):
+                logit_pass(BANKS - 2 + pair, 0, 2 * pair, 2 * pair + 2, b, copy=copy)
+
         lower_cols = slice(z_start(1, 0), z_start(1, 0) + HALF)
         quantize(z_codes[:, lower_cols], z_planes[:, lower_cols], z_lo[1])
         for n in range(N // P):

@@ -25,12 +25,13 @@ BANKS = 8
 LANES = 16
 QUAD = 32
 HALF = 256
+SHARE = 64
 ROW = 4 * Q
 AT_SCALES = 0
 AT_TABLE1 = AT_SCALES + T
 AT_FRONT = AT_TABLE1 + 4 * T
 AT_PLUS = AT_FRONT + 4 * ROW
-AT_Z = AT_PLUS + 4 * ROW
+AT_Z = AT_PLUS + 5 * ROW
 
 
 def tile_list_frame_delta_logits_kernel(
@@ -84,8 +85,8 @@ def tile_list_frame_delta_logits_kernel(
             nc.gpsimd.dma_start(
                 table_scales[QUAD * quad : QUAD * quad + 8, :], tab_scales.bitcast(I32)[:, 4 * quad : 4 * quad + 4, :]
             )
-        nc.sync.dma_start(offs_sb[:], offs)
         load_table(0)
+        nc.sync.dma_start(offs_sb[:], offs)
         for a in range(2):
             load_w1(front_raw[a][:], a, 0, HALF)
         load_table(1)
@@ -104,7 +105,8 @@ def tile_list_frame_delta_logits_kernel(
             )
 
         nc.scalar.activation(out=zero[:], in_=one[:], func=ACT.Ln)
-        plus = [shared.tile([P, Q], F32, name=f"plus{t}", offset=AT_PLUS + t * ROW, align_bytes=64) for t in range(PACK)]
+        plus_at = [AT_PLUS + t * ROW + (ROW // 2 if t else 0) for t in range(PACK)]
+        plus = [shared.tile([P, Q], F32, name=f"plus{t}", offset=plus_at[t], align_bytes=64) for t in range(PACK)]
         hi_rows = keep.tile([P, PACK * Q], F32, name="hi_rows")
         nc.scalar.copy(
             out=hi_rows[:].rearrange("p (t q) -> p t q", t=PACK), in_=gain_hi[:].unsqueeze(2).to_broadcast([P, PACK, Q])
@@ -122,10 +124,10 @@ def tile_list_frame_delta_logits_kernel(
                 in_=raw[:, :, c0:c1].rearrange("p j (c i) -> p c j i", i=4),
             )
 
-        def round_hi(dst, a, t0, copy):
+        def round_hi(dst, a, t0, copy, m0=0, m1=P):
             copy(
-                out=dst.rearrange("p (t m j) -> p m j t", t=2, j=PACK),
-                in_=hi_raw[a][:].rearrange("p j (m t) -> p m j t", t=PACK)[:, :, :, t0 : t0 + 2],
+                out=dst.rearrange("p (t m j) -> p m j t", t=2, j=PACK)[:, m0:m1],
+                in_=hi_raw[a][:].rearrange("p j (m t) -> p m j t", t=PACK)[:, m0:m1, :, t0 : t0 + 2],
             )
 
         def quantize(to_codes, to_planes, src):
@@ -211,7 +213,6 @@ def tile_list_frame_delta_logits_kernel(
             quantize(codes[1][a], planes[1][:, a * HALF : (a + 1) * HALF], part)
 
         terms = [[keep.tile([P, Q], F32, name=f"term{t}_{i}")[:] for i in range(2)] for t in range(PACK)]
-        near_bf = minus_rows[:, 0 : 2 * Q].bitcast(BF16)
         early = keep.tile([P, S + HALF], F32, name="early", align_bytes=64)
         far_bf = early[:, HALF:].bitcast(BF16)
         lower_magnitudes = [early[:, 0:S]] + [early[:, HALF:]] * (PACK - 1)
@@ -219,15 +220,18 @@ def tile_list_frame_delta_logits_kernel(
         for t in range(PACK):
             h = project(t, [lower_magnitudes[t][:, 0:BANK], lower_magnitudes[t][:, BANK:]])
             pick_scaled(terms[t][0], pos1_sb, plus[t], h)
-            if t in (1, 2):
-                a = t - 1
-                near_codes = shared.tile([P, HALF], U32, name=f"near_codes{a}", offset=AT_PLUS + t * ROW, align_bytes=64)
-                codes[2].append(near_codes)
-                part = near_bf[:, a * PACK * HALF : (a + 1) * PACK * HALF]
-                quantize(near_codes[:], planes[2][:, a * HALF : (a + 1) * HALF], part)
             pick_scaled(terms[t][1], pos2_sb, minus[t], h)
-            if t < 2:
-                round_hi(near_bf[:, t * PACK * HALF : (t + 1) * PACK * HALF], t, 0, nc.vector.tensor_copy)
+            if t == 0:
+                near_bf0 = shared.tile([P, PACK * HALF], BF16, name="near_bf0", offset=plus_at[0], align_bytes=64)
+                round_hi(near_bf0[:], 0, 0, nc.vector.tensor_copy, 0, SHARE)
+            if t == 1:
+                round_hi(near_bf0[:], 0, 0, nc.scalar.copy, SHARE, P)
+                near_bf1 = shared.tile([P, PACK * HALF], BF16, name="near_bf1", offset=AT_PLUS + ROW, align_bytes=64)
+                round_hi(near_bf1[:], 1, 0, nc.vector.tensor_copy)
+                codes[2].append(shared.tile([P, HALF], U32, name="near_codes0", offset=AT_PLUS + 2 * ROW, align_bytes=64))
+                codes[2].append(keep.tile([P, HALF], U32, name="near_codes1", align_bytes=64))
+                for a, part in enumerate((near_bf0, near_bf1)):
+                    quantize(codes[2][a][:], planes[2][:, a * HALF : (a + 1) * HALF], part[:])
         far_codes = keep.tile([P, 2 * HALF], U32, name="far_codes", align_bytes=64)
         codes.append([far_codes[:, 0:HALF], far_codes[:, HALF:]])
         for a in range(2):
@@ -236,13 +240,14 @@ def tile_list_frame_delta_logits_kernel(
         upper_magnitude = [hi_raw[a][:, 0] for a in range(2)]
 
         first = keep.tile([P, PACK, Q], F32, name="first")
-        second_and_z = keep.tile([P, PACK * Q + HALF], F32, name="second_and_z", align_bytes=64)
-        second = second_and_z[:, 0 : PACK * Q].rearrange("p (t q) -> p t q", q=Q)
+        second_flat = keep.tile([P, PACK * Q], F32, name="second_flat", align_bytes=64)
+        second = second_flat[:].rearrange("p (t q) -> p t q", q=Q)
         z_rows = keep.tile([P, Q // P, 2, HALF], BF16, name="z_rows")
-        z_first = shared.tile([P, PACK * HALF], BF16, name="z_first", offset=AT_Z, align_bytes=64)
-        z_late = keep.tile([P, PACK * HALF], BF16, name="z_late", align_bytes=64)
-        z_lo = [z_first[:], z_late[:]]
-        z_hi = [second_and_z[:, PACK * Q - HALF :].bitcast(BF16), z_late[:]]
+        z_first = shared.tile([P, K_PASS], BF16, name="z_first", offset=AT_Z, align_bytes=64)
+        z_late = keep.tile([P, 2 * K_PASS], BF16, name="z_late", align_bytes=64)
+        z_lo = [z_first[:], second_flat[:, PACK * Q - HALF :].bitcast(BF16), z_late[:, 0:K_PASS], z_late[:, K_PASS:]]
+        z_upper = keep.tile([P, PACK * HALF], BF16, name="z_upper", align_bytes=64)
+        z_hi = [z_upper[:]] * 2
         z_codes = keep.tile([P, 2 * Q], U32, name="z_codes", align_bytes=64)
 
         def z_words(half, b, q0, q1):
@@ -278,10 +283,17 @@ def tile_list_frame_delta_logits_kernel(
             for g in range(2):
                 for u in range(2):
                     nc.tensor.transpose(bank[:, g, u, :], z_rows[:, 2 * half + g, u].bitcast(F32), ident[:])
-            nc.scalar.copy(
-                out=z_lo[half].bitcast(F32).rearrange("p (g q u) -> p g q u", g=2, u=2),
-                in_=bank.rearrange("p g u q -> p g q u"),
-            )
+            if half == 0:
+                for g in range(2):
+                    nc.scalar.copy(
+                        out=z_lo[g].bitcast(F32).rearrange("p (q u) -> p q u", u=2),
+                        in_=bank[:, g].rearrange("p u q -> p q u"),
+                    )
+            else:
+                nc.scalar.copy(
+                    out=z_late[:].bitcast(F32).rearrange("p (g q u) -> p g q u", g=2, u=2),
+                    in_=bank.rearrange("p g u q -> p g q u"),
+                )
 
         def subtract(dst, q0, q1):
             nc.vector.tensor_tensor(
@@ -332,16 +344,17 @@ def tile_list_frame_delta_logits_kernel(
         pick_scaled(first[:, last], pos1_sb, upper[last], h, HALF, Q)
         subtract(z_hi[0], 0, HALF)
         upper_codes = shared.tile([P, HALF], U32, name="upper_codes", offset=AT_Z, align_bytes=64)
-        for b, src in enumerate((z_lo[0], z_hi[0])):
-            cols = slice(z_start(0, b), z_start(0, b) + HALF)
-            quantize(z_words(0, b, 0, HALF), z_planes[:, cols], src)
+        for g in range(2):
+            cols = slice(z_start(0, 0) + g * P, z_start(0, 0) + (g + 1) * P)
+            quantize(z_codes[:, cols], z_planes[:, cols], z_lo[g])
+        quantize(upper_codes[:], z_planes[:, z_start(0, 1) : z_start(0, 1) + HALF], z_hi[0])
         pick_scaled(second[:, last], pos2_sb, upper[last], h, HALF, Q)
         for b, copy in enumerate((None, nc.scalar.copy)):
             for pair in range(2):
                 logit_pass(BANKS - 2 + pair, 0, 2 * pair, 2 * pair + 2, b, copy=copy)
 
         lower_cols = slice(z_start(1, 0), z_start(1, 0) + HALF)
-        quantize(z_codes[:, lower_cols], z_planes[:, lower_cols], z_lo[1])
+        quantize(z_codes[:, lower_cols], z_planes[:, lower_cols], z_late[:])
         for n in range(N // P):
             logit_pass(n, 1, n, n + 1, 0)
         for q in (0, P):

@@ -25,7 +25,6 @@ BANKS = 8
 LANES = 16
 QUAD = 32
 HALF = 256
-SHARE = 64
 ROW = 4 * Q
 AT_SCALES = 0
 AT_TABLE1 = AT_SCALES + T
@@ -85,8 +84,8 @@ def tile_list_frame_delta_logits_kernel(
             nc.gpsimd.dma_start(
                 table_scales[QUAD * quad : QUAD * quad + 8, :], tab_scales.bitcast(I32)[:, 4 * quad : 4 * quad + 4, :]
             )
-        load_table(0)
         nc.sync.dma_start(offs_sb[:], offs)
+        load_table(0)
         for a in range(2):
             load_w1(front_raw[a][:], a, 0, HALF)
         load_table(1)
@@ -124,10 +123,10 @@ def tile_list_frame_delta_logits_kernel(
                 in_=raw[:, :, c0:c1].rearrange("p j (c i) -> p c j i", i=4),
             )
 
-        def round_hi(dst, a, t0, copy, m0=0, m1=P):
+        def round_hi(dst, a, t0, copy):
             copy(
-                out=dst.rearrange("p (t m j) -> p m j t", t=2, j=PACK)[:, m0:m1],
-                in_=hi_raw[a][:].rearrange("p j (m t) -> p m j t", t=PACK)[:, m0:m1, :, t0 : t0 + 2],
+                out=dst.rearrange("p (t m j) -> p m j t", t=2, j=PACK),
+                in_=hi_raw[a][:].rearrange("p j (m t) -> p m j t", t=PACK)[:, :, :, t0 : t0 + 2],
             )
 
         def quantize(to_codes, to_planes, src):
@@ -153,20 +152,17 @@ def tile_list_frame_delta_logits_kernel(
                         stop=(a == 1),
                     )
             h = ring.tile([P, S], F32, name="h")
+            steps = [(ACT.Abs, 0, BANK), (ACT.Abs, BANK, S), (ACT.Ln, 0, BANK), (ACT.Ln, BANK, S)]
             if i == 0:
-                steps = [(c, step) for s in range(2) for step in range(2) for c in (2 * s, 2 * s + 1)]
-                width = BANK // 2
-            else:
-                steps = [(c, step) for step in range(2) for c in range(2)]
-                width = BANK
-            for c, step in steps:
-                s, c0 = divmod(c * width, BANK)
-                part = magnitude[s][:, c0 : c0 + width]
-                if step == 0:
-                    bank = banks[2 * pair + s][:, c0 : c0 + width]
-                    nc.scalar.activation(out=part, in_=bank, func=ACT.Abs, bias=zero[:])
+                steps = [(ACT.Abs, 0, HALF), (ACT.Abs, HALF, BANK), (ACT.Ln, 0, HALF), steps[1], (ACT.Ln, HALF, BANK), steps[3]]
+            for func, f0, f1 in steps:
+                s, c0 = divmod(f0, BANK)
+                part = magnitude[s][:, c0 : c0 + f1 - f0]
+                if func == ACT.Abs:
+                    bank = banks[2 * pair + s][:, c0 : c0 + f1 - f0]
+                    nc.scalar.activation(out=part, in_=bank, func=func, bias=zero[:])
                 else:
-                    nc.scalar.activation(out=h[:, c * width : (c + 1) * width], in_=part, func=ACT.Ln, bias=one[:])
+                    nc.scalar.activation(out=h[:, f0:f1], in_=part, func=func, bias=one[:])
             return h
 
         def offsets(list_sb, j0, j1):
@@ -213,31 +209,30 @@ def tile_list_frame_delta_logits_kernel(
             quantize(codes[1][a], planes[1][:, a * HALF : (a + 1) * HALF], part)
 
         terms = [[keep.tile([P, Q], F32, name=f"term{t}_{i}")[:] for i in range(2)] for t in range(PACK)]
-        early = keep.tile([P, S + HALF], F32, name="early", align_bytes=64)
-        far_bf = early[:, HALF:].bitcast(BF16)
-        lower_magnitudes = [early[:, 0:S]] + [early[:, HALF:]] * (PACK - 1)
+        early = keep.tile([P, S], F32, name="early", align_bytes=64)
+        far_bf = early[:].bitcast(BF16)
+        upper_magnitude = [hi_raw[a][:, 0] for a in range(2)]
         codes.append([])
         for t in range(PACK):
-            h = project(t, [lower_magnitudes[t][:, 0:BANK], lower_magnitudes[t][:, BANK:]])
+            if t == PACK - 1:
+                far_codes = keep.tile([P, 2 * HALF], U32, name="far_codes", align_bytes=64)
+                codes.append([far_codes[:, 0:HALF], far_codes[:, HALF:]])
+                for a in range(2):
+                    round_hi(far_bf[:, a * PACK * HALF : (a + 1) * PACK * HALF], a, 2, nc.scalar.copy)
+                quantize(far_codes[:], planes[3][:], far_bf)
+            h = project(t, upper_magnitude if t == PACK - 1 else [early[:, 0:BANK], early[:, BANK:]])
             pick_scaled(terms[t][0], pos1_sb, plus[t], h)
             pick_scaled(terms[t][1], pos2_sb, minus[t], h)
             if t == 0:
                 near_bf0 = shared.tile([P, PACK * HALF], BF16, name="near_bf0", offset=plus_at[0], align_bytes=64)
-                round_hi(near_bf0[:], 0, 0, nc.vector.tensor_copy, 0, SHARE)
+                round_hi(near_bf0[:], 0, 0, nc.vector.tensor_copy)
             if t == 1:
-                round_hi(near_bf0[:], 0, 0, nc.scalar.copy, SHARE, P)
                 near_bf1 = shared.tile([P, PACK * HALF], BF16, name="near_bf1", offset=AT_PLUS + ROW, align_bytes=64)
                 round_hi(near_bf1[:], 1, 0, nc.vector.tensor_copy)
                 codes[2].append(shared.tile([P, HALF], U32, name="near_codes0", offset=AT_PLUS + 2 * ROW, align_bytes=64))
                 codes[2].append(keep.tile([P, HALF], U32, name="near_codes1", align_bytes=64))
                 for a, part in enumerate((near_bf0, near_bf1)):
                     quantize(codes[2][a][:], planes[2][:, a * HALF : (a + 1) * HALF], part[:])
-        far_codes = keep.tile([P, 2 * HALF], U32, name="far_codes", align_bytes=64)
-        codes.append([far_codes[:, 0:HALF], far_codes[:, HALF:]])
-        for a in range(2):
-            round_hi(far_bf[:, a * PACK * HALF : (a + 1) * PACK * HALF], a, 2, nc.scalar.copy)
-        quantize(far_codes[:], planes[3][:], far_bf)
-        upper_magnitude = [hi_raw[a][:, 0] for a in range(2)]
 
         first = keep.tile([P, PACK, Q], F32, name="first")
         second_flat = keep.tile([P, PACK * Q], F32, name="second_flat", align_bytes=64)

@@ -136,21 +136,24 @@ def tile_list_frame_delta_logits_kernel(
             c0 = (i % 2) * P
             return codes[i // 2][a][:, c0 : c0 + P], planes[i // 2][:, a * HALF + c0 : a * HALF + c0 + P]
 
+        def x_pass(i, a, s):
+            frames = slice(s * BANK, (s + 1) * BANK)
+            w_codes, w_planes = stationary(i, a)
+            nc.tensor.matmul_mx(
+                out=banks[2 * (i % PACK) + s][:],
+                lhsT=w_codes.bitcast(FP8X4),
+                lhsT_scale=w_planes,
+                rhs=v_codes[a][:, frames].bitcast(FP8X4),
+                rhs_scale=v_planes[4 * a :, frames],
+                start=(a == 0),
+                stop=(a == 1),
+            )
+
         def project(i, magnitude):
-            pair = i % (BANKS // 2)
+            pair = i % PACK
             for s in range(2):
-                for a in range(2):
-                    frames = slice(s * BANK, (s + 1) * BANK)
-                    w_codes, w_planes = stationary(i, a)
-                    nc.tensor.matmul_mx(
-                        out=banks[2 * pair + s][:],
-                        lhsT=w_codes.bitcast(FP8X4),
-                        lhsT_scale=w_planes,
-                        rhs=v_codes[a][:, frames].bitcast(FP8X4),
-                        rhs_scale=v_planes[4 * a :, frames],
-                        start=(a == 0),
-                        stop=(a == 1),
-                    )
+                for a in range(1 if i < 2 else 0, 2):
+                    x_pass(i, a, s)
             h = ring.tile([P, S], F32, name="h")
             steps = [(ACT.Abs, 0, BANK), (ACT.Abs, BANK, S), (ACT.Ln, 0, BANK), (ACT.Ln, BANK, S)]
             if i == 0:
@@ -186,6 +189,9 @@ def tile_list_frame_delta_logits_kernel(
         front_codes = shared.tile([P, 2 * HALF], U32, name="front_codes", offset=AT_SCALES, align_bytes=64)
         codes.append([front_codes[:, 0:HALF], front_codes[:, HALF:]])
         quantize(front_codes[:], planes[0][:], front_bf[:])
+        for i in range(2):
+            for s in range(2):
+                x_pass(i, 0, s)
         minus_rows = shared.tile([P, PACK * Q], F32, name="minus_rows", offset=AT_FRONT, align_bytes=64)
         nc.scalar.copy(
             out=minus_rows[:].rearrange("p (t q) -> p t q", q=Q),

@@ -29,8 +29,11 @@ ROW = 4 * Q
 AT_SCALES = 0
 AT_TABLE1 = AT_SCALES + T
 AT_FRONT = AT_TABLE1 + 4 * T
-AT_PLUS = AT_FRONT + 4 * ROW
-AT_Z = AT_PLUS + 5 * ROW
+AT_STAGE = AT_TABLE1 + 2 * ROW
+AT_H = AT_FRONT + 2 * ROW
+AT_FAR = AT_STAGE - 3 * ROW // 4
+AT_RAW = AT_H + 16 * ROW
+AT_Z = AT_RAW + 8 * ROW
 
 
 def tile_list_frame_delta_logits_kernel(
@@ -39,7 +42,6 @@ def tile_list_frame_delta_logits_kernel(
     nc = tc.nc
     with ExitStack() as ctx:
         keep = ctx.enter_context(tc.tile_pool(name="keep", bufs=1))
-        ring = ctx.enter_context(tc.tile_pool(name="ring", bufs=4))
         shared = ctx.enter_context(tc.tile_pool(name="shared", bufs=1))
         psum = ctx.enter_context(tc.psum_pool(name="psum", bufs=1))
 
@@ -49,7 +51,7 @@ def tile_list_frame_delta_logits_kernel(
         pos2_sb = keep.tile([P, Q // LANES], U16, name="pos2_sb")
         gain_flat = keep.tile([P, P], F32, name="gain_flat")
         front_bf = keep.tile([P, 2 * PACK * HALF], BF16, name="front_bf", tag="chain", align_bytes=64)
-        gain_lo = front_bf[:, PACK * HALF - PACK : PACK * HALF + PACK].bitcast(F32)
+        gain_lo = keep.tile([P, PACK], F32, name="gain_lo")
         gain_hi = keep.tile([P, PACK], F32, name="gain_hi")
         table_scales = shared.tile([P, T // 4], I32, name="table_scales", offset=AT_SCALES, align_bytes=64)
         table = [
@@ -104,13 +106,6 @@ def tile_list_frame_delta_logits_kernel(
             )
 
         nc.scalar.activation(out=zero[:], in_=one[:], func=ACT.Ln)
-        plus_at = [AT_PLUS + t * ROW + (ROW // 2 if t else 0) for t in range(PACK)]
-        plus = [shared.tile([P, Q], F32, name=f"plus{t}", offset=plus_at[t], align_bytes=64) for t in range(PACK)]
-        hi_rows = keep.tile([P, PACK * Q], F32, name="hi_rows")
-        nc.scalar.copy(
-            out=hi_rows[:].rearrange("p (t q) -> p t q", t=PACK), in_=gain_hi[:].unsqueeze(2).to_broadcast([P, PACK, Q])
-        )
-        upper = [hi_rows[:, t * Q : (t + 1) * Q] for t in range(PACK)]
 
         v_codes = [keep.tile([P, S], U32, name="v_codes0", align_bytes=64)]
         v_planes = keep.tile([P, S], U8, name="v_planes", align_bytes=64)
@@ -154,7 +149,7 @@ def tile_list_frame_delta_logits_kernel(
             for s in range(2):
                 for a in range(1 if i < 2 else 0, 2):
                     x_pass(i, a, s)
-            h = ring.tile([P, S], F32, name="h")
+            h = shared.tile([P, S], F32, name=f"h{i}", offset=AT_H + 2 * ROW * i, align_bytes=64)
             steps = [(ACT.Abs, 0, BANK), (ACT.Abs, BANK, S), (ACT.Ln, 0, BANK), (ACT.Ln, BANK, S)]
             if i == 0:
                 steps = [(ACT.Abs, 0, HALF), (ACT.Abs, HALF, BANK), (ACT.Ln, 0, HALF), steps[1], (ACT.Ln, HALF, BANK), steps[3]]
@@ -174,13 +169,29 @@ def tile_list_frame_delta_logits_kernel(
         def pick_scaled(dst, pos_sb, row, h, q0=0, q1=Q):
             nc.vector.tensor_tensor(dst[:, q0:q1], h[:].indirect(offsets(pos_sb, q0, q1)), row[:, q0:q1], ALU.mult)
 
+        def pick(dst, pos_sb, h):
+            nc.vector.tensor_copy(dst, h[:].indirect(pos_sb[:]))
+
+        def pool_copy(out, in_):
+            nc.gpsimd.tensor_scalar(out, in_, 1.0, 0.0, ALU.mult, ALU.add)
+
+        def pool_round(dst, a, t0):
+            pool_copy(
+                dst.rearrange("p (t m j) -> p t m j", t=2, j=PACK),
+                hi_raw[a][:].rearrange("p j (m t) -> p t m j", t=PACK)[:, t0 : t0 + 2],
+            )
+
+        def pool_gain(dst, src, column):
+            nc.gpsimd.tensor_scalar(dst, src, column, 0.0, ALU.mult, ALU.add)
+
+        def row_at(name, offset):
+            return shared.tile([P, Q], F32, name=name, offset=offset, align_bytes=64)[:]
+
         gain_bank = banks[BANKS - 1]
         nc.tensor.transpose(gain_bank[:, 0:P], gain_flat[:], ident[:])
-        nc.scalar.copy(out=gain_lo, in_=gain_bank[:, 0:PACK])
-        for t in range(PACK):
-            nc.scalar.copy(out=plus[t][:], in_=gain_lo[:, t : t + 1].to_broadcast([P, Q]))
+        nc.scalar.copy(out=gain_lo[:], in_=gain_bank[:, 0:PACK])
         gain_minus = keep.tile([P, PACK], F32, name="gain_minus")
-        nc.scalar.activation(out=gain_minus[:], in_=gain_bank[:, 0:PACK], func=ACT.Copy, scale=-1.0)
+        nc.gpsimd.tensor_scalar(gain_minus[:], gain_lo[:], -1.0, 0.0, ALU.mult, ALU.add)
 
         nc.vector.tensor_copy(v_codes[0][:], table[0][:].bitcast(U32).indirect(offs_sb[:]))
         nc.vector.tensor_copy(v_planes[:], table_scales[:].bitcast(U8).indirect(offs_sb[:]))
@@ -192,12 +203,8 @@ def tile_list_frame_delta_logits_kernel(
         for i in range(2):
             for s in range(2):
                 x_pass(i, 0, s)
-        minus_rows = shared.tile([P, PACK * Q], F32, name="minus_rows", offset=AT_FRONT, align_bytes=64)
-        nc.scalar.copy(
-            out=minus_rows[:].rearrange("p (t q) -> p t q", q=Q),
-            in_=gain_minus[:].unsqueeze(2).to_broadcast([P, PACK, Q]),
-        )
-        minus = [minus_rows[:, t * Q : (t + 1) * Q] for t in range(PACK)]
+        last_row = row_at("last_row", AT_FRONT)
+        nc.scalar.copy(out=last_row, in_=gain_hi[:, PACK - 1 : PACK].to_broadcast([P, Q]))
 
         v_codes.append(keep.tile([P, S], U32, name="v_codes1", tag="chain", align_bytes=64))
         for s in range(2):
@@ -205,7 +212,7 @@ def tile_list_frame_delta_logits_kernel(
                 v_codes[1][:, s * BANK : (s + 1) * BANK],
                 table[1][:].bitcast(U32).indirect(offsets(offs_sb, s * BANK, (s + 1) * BANK)),
             )
-        back_bf = shared.tile([P, 2 * PACK * HALF], BF16, name="back_bf", offset=AT_TABLE1, align_bytes=64)
+        back_bf = shared.tile([P, 2 * PACK * HALF], BF16, name="back_bf", offset=AT_STAGE, align_bytes=64)
         back_codes = keep.tile([P, 2 * HALF], U32, name="back_codes", align_bytes=64)
         codes.append([back_codes[:, 0:HALF], back_codes[:, HALF:]])
         for a in range(2):
@@ -214,39 +221,48 @@ def tile_list_frame_delta_logits_kernel(
             part = back_bf[:, a * PACK * HALF : (a + 1) * PACK * HALF]
             quantize(codes[1][a], planes[1][:, a * HALF : (a + 1) * HALF], part)
 
-        terms = [[keep.tile([P, Q], F32, name=f"term{t}_{i}")[:] for i in range(2)] for t in range(PACK)]
-        early = keep.tile([P, S], F32, name="early", align_bytes=64)
-        far_bf = early[:].bitcast(BF16)
-        upper_magnitude = [hi_raw[a][:, 0] for a in range(2)]
-        codes.append([])
+        near_bf = shared.tile([P, 2 * PACK * HALF], BF16, name="near_bf", offset=AT_STAGE, align_bytes=64)
+        for a in range(2):
+            pool_round(near_bf[:, a * PACK * HALF : (a + 1) * PACK * HALF], a, 0)
+        early = keep.tile([P, BANK], F32, name="early", align_bytes=64)
+        lower_magnitude = [early[:], row_at("late", AT_FAR - ROW)]
+        upper_magnitude = [hi_raw[1][:, s] for s in range(2)]
+        raw_at = [[AT_RAW, AT_RAW + ROW], [AT_RAW + 5 * ROW // 2, AT_RAW + 4 * ROW],
+                  [AT_RAW + 5 * ROW, AT_STAGE + 5 * ROW // 4], [AT_RAW + 6 * ROW, AT_RAW + 7 * ROW]]
+        term_at = [[AT_STAGE + ROW // 4, raw_at[0][0]], [AT_FAR - ROW // 2, AT_RAW + 2 * ROW],
+                   [AT_RAW + 3 * ROW, raw_at[1][1]], raw_at[2]]
+        raws = []
         for t in range(PACK):
-            if t == PACK - 1:
-                far_codes = keep.tile([P, 2 * HALF], U32, name="far_codes", align_bytes=64)
-                codes.append([far_codes[:, 0:HALF], far_codes[:, HALF:]])
-                for a in range(2):
-                    round_hi(far_bf[:, a * PACK * HALF : (a + 1) * PACK * HALF], a, 2, nc.scalar.copy)
-                quantize(far_codes[:], planes[3][:], far_bf)
-            h = project(t, upper_magnitude if t == PACK - 1 else [early[:, 0:BANK], early[:, BANK:]])
-            pick_scaled(terms[t][0], pos1_sb, plus[t], h)
-            pick_scaled(terms[t][1], pos2_sb, minus[t], h)
-            if t == 0:
-                near_bf0 = shared.tile([P, PACK * HALF], BF16, name="near_bf0", offset=plus_at[0], align_bytes=64)
-                round_hi(near_bf0[:], 0, 0, nc.vector.tensor_copy)
-            if t == 1:
-                near_bf1 = shared.tile([P, PACK * HALF], BF16, name="near_bf1", offset=AT_PLUS + ROW, align_bytes=64)
-                round_hi(near_bf1[:], 1, 0, nc.vector.tensor_copy)
-                codes[2].append(shared.tile([P, HALF], U32, name="near_codes0", offset=AT_PLUS + 2 * ROW, align_bytes=64))
-                codes[2].append(keep.tile([P, HALF], U32, name="near_codes1", align_bytes=64))
-                for a, part in enumerate((near_bf0, near_bf1)):
-                    quantize(codes[2][a][:], planes[2][:, a * HALF : (a + 1) * HALF], part[:])
+            h = project(t, lower_magnitude)
+            raws.append([])
+            for i, pos_sb in enumerate((pos1_sb, pos2_sb)):
+                if (t, i) == (2, 1):
+                    near_codes = shared.tile([P, 2 * HALF], U32, name="near_codes", offset=AT_H + 2 * ROW, align_bytes=64)
+                    codes.append([near_codes[:, 0:HALF], near_codes[:, HALF:]])
+                    quantize(near_codes[:], planes[2][:], near_bf[:])
+                    far_bf = shared.tile([P, PACK * HALF], BF16, name="far_bf", offset=AT_FAR, align_bytes=64)
+                    pool_round(far_bf[:], 0, 2)
+                raws[t].append(row_at(f"raw{t}_{i}", raw_at[t][i]))
+                pick(raws[t][i], pos_sb, h)
+        far_parts = [far_bf[:], lower_magnitude[1].bitcast(BF16)]
+        round_hi(far_parts[1], 1, 2, nc.scalar.copy)
+        far_codes = shared.tile([P, 2 * HALF], U32, name="far_codes", offset=AT_H + 6 * ROW, align_bytes=64)
+        codes.append([far_codes[:, 0:HALF], far_codes[:, HALF:]])
+        for a in range(2):
+            quantize(codes[3][a], planes[3][:, a * HALF : (a + 1) * HALF], far_parts[a])
+        terms = []
+        for t in range(PACK):
+            terms.append([row_at(f"term{t}_{i}", term_at[t][i]) for i in range(2)])
+            for i, gains in enumerate((gain_lo, gain_minus)):
+                pool_gain(terms[t][i], raws[t][i], gains[:, t : t + 1])
 
-        first = keep.tile([P, PACK, Q], F32, name="first")
-        second_flat = keep.tile([P, PACK * Q], F32, name="second_flat", align_bytes=64)
-        second = second_flat[:].rearrange("p (t q) -> p t q", q=Q)
+        upper_flat = keep.tile([P, PACK * 2 * Q], F32, name="upper_flat", align_bytes=64)
+        upper = upper_flat[:].rearrange("p (t i q) -> p t i q", i=2, q=Q)
+        first, second = upper[:, :, 0], upper[:, :, 1]
         z_rows = keep.tile([P, Q // P, 2, HALF], BF16, name="z_rows")
         z_first = shared.tile([P, K_PASS], BF16, name="z_first", offset=AT_Z, align_bytes=64)
         z_late = keep.tile([P, 2 * K_PASS], BF16, name="z_late", align_bytes=64)
-        z_lo = [z_first[:], second_flat[:, PACK * Q - HALF :].bitcast(BF16), z_late[:, 0:K_PASS], z_late[:, K_PASS:]]
+        z_lo = [z_first[:], upper_flat[:, PACK * 2 * Q - HALF :].bitcast(BF16), z_late[:, 0:K_PASS], z_late[:, K_PASS:]]
         z_upper = keep.tile([P, PACK * HALF], BF16, name="z_upper", align_bytes=64)
         z_hi = [z_upper[:]] * 2
         z_codes = keep.tile([P, 2 * Q], U32, name="z_codes", align_bytes=64)
@@ -330,26 +346,31 @@ def tile_list_frame_delta_logits_kernel(
         last = PACK - 1
         for t in range(last):
             h = project(PACK + t, upper_magnitude)
-            pick_scaled(first[:, t], pos1_sb, upper[t], h)
-            pick_scaled(second[:, t], pos2_sb, upper[t], h)
+            pick(first[:, t], pos1_sb, h)
+            pick(second[:, t], pos2_sb, h)
+            scaled = upper_flat[:, 2 * t * Q : (2 * t + (2 if t < last - 1 else 1)) * Q]
+            pool_gain(scaled, scaled, gain_hi[:, t : t + 1])
         h = project(PACK + last, upper_magnitude)
         for t in range(PACK):
             turn_delta(t)
         for half in range(2):
             for t in range(PACK):
                 round_delta(t, 2 * half, 2 * half + 2)
+            if half == 0:
+                before = second[:, last - 1]
+                nc.scalar.activation(out=before, in_=before, func=ACT.Copy, scale=gain_hi[:, last - 1 : last])
             turn_back(half)
 
-        pick_scaled(first[:, last], pos1_sb, upper[last], h, 0, HALF)
-        pick_scaled(second[:, last], pos2_sb, upper[last], h, 0, HALF)
-        pick_scaled(first[:, last], pos1_sb, upper[last], h, HALF, Q)
+        pick_scaled(first[:, last], pos1_sb, last_row, h, 0, HALF)
+        pick_scaled(second[:, last], pos2_sb, last_row, h, 0, HALF)
+        pick_scaled(first[:, last], pos1_sb, last_row, h, HALF, Q)
         subtract(z_hi[0], 0, HALF)
         upper_codes = shared.tile([P, HALF], U32, name="upper_codes", offset=AT_Z, align_bytes=64)
         for g in range(2):
             cols = slice(z_start(0, 0) + g * P, z_start(0, 0) + (g + 1) * P)
             quantize(z_codes[:, cols], z_planes[:, cols], z_lo[g])
         quantize(upper_codes[:], z_planes[:, z_start(0, 1) : z_start(0, 1) + HALF], z_hi[0])
-        pick_scaled(second[:, last], pos2_sb, upper[last], h, HALF, Q)
+        pick_scaled(second[:, last], pos2_sb, last_row, h, HALF, Q)
         for b, copy in enumerate((None, nc.scalar.copy)):
             for pair in range(2):
                 logit_pass(BANKS - 2 + pair, 0, 2 * pair, 2 * pair + 2, b, copy=copy)

@@ -29,11 +29,10 @@ ROW = 4 * Q
 AT_SCALES = 0
 AT_TABLE1 = AT_SCALES + T
 AT_FRONT = AT_TABLE1 + 4 * T
-AT_STAGE = AT_TABLE1 + 2 * ROW
+AT_STAGE = AT_TABLE1 + ROW
 AT_H = AT_FRONT + 2 * ROW
-AT_FAR = AT_STAGE - 3 * ROW // 4
 AT_RAW = AT_H + 16 * ROW
-AT_Z = AT_RAW + 8 * ROW
+AT_Z = AT_RAW + 7 * ROW
 
 
 def tile_list_frame_delta_logits_kernel(
@@ -109,7 +108,8 @@ def tile_list_frame_delta_logits_kernel(
 
         v_codes = [keep.tile([P, S], U32, name="v_codes0", align_bytes=64)]
         v_planes = keep.tile([P, S], U8, name="v_planes", align_bytes=64)
-        planes = [keep.tile([P, 2 * HALF], U8, name=f"planes{i}", align_bytes=64) for i in range(PACK)]
+        planes = [keep.tile([P, 2 * HALF], U8, name=f"planes{i}", align_bytes=64) for i in range(2)]
+        hi_planes = keep.tile([P, 2 * K_PASS], U8, name="hi_planes", align_bytes=64)
         codes = []
 
         def round_lo(dst, raw, c0, c1, copy):
@@ -128,6 +128,9 @@ def tile_list_frame_delta_logits_kernel(
             nc.vector.quantize_mx(out=to_codes.bitcast(FP8X4), scales=to_planes, in_=src)
 
         def stationary(i, a):
+            if i >= PACK:
+                c0 = a * K_PASS + (i - PACK) * P
+                return hi_codes[:, c0 : c0 + P], hi_planes[:, c0 : c0 + P]
             c0 = (i % 2) * P
             return codes[i // 2][a][:, c0 : c0 + P], planes[i // 2][:, a * HALF + c0 : a * HALF + c0 + P]
 
@@ -175,10 +178,10 @@ def tile_list_frame_delta_logits_kernel(
         def pool_copy(out, in_):
             nc.gpsimd.tensor_scalar(out, in_, 1.0, 0.0, ALU.mult, ALU.add)
 
-        def pool_round(dst, a, t0):
+        def pool_round(dst, a, tiles):
             pool_copy(
-                dst.rearrange("p (t m j) -> p t m j", t=2, j=PACK),
-                hi_raw[a][:].rearrange("p j (m t) -> p t m j", t=PACK)[:, t0 : t0 + 2],
+                dst.rearrange("p (t m j) -> p m t j", t=tiles, j=PACK),
+                hi_raw[a][:].rearrange("p j (m t) -> p m t j", t=PACK)[:, :, 0:tiles],
             )
 
         def pool_gain(dst, src, column):
@@ -212,7 +215,9 @@ def tile_list_frame_delta_logits_kernel(
                 v_codes[1][:, s * BANK : (s + 1) * BANK],
                 table[1][:].bitcast(U32).indirect(offsets(offs_sb, s * BANK, (s + 1) * BANK)),
             )
-        back_bf = shared.tile([P, 2 * PACK * HALF], BF16, name="back_bf", offset=AT_STAGE, align_bytes=64)
+        stage = shared.tile([P, 2 * S], F32, name="stage", offset=AT_STAGE, align_bytes=64)
+        hi_bf = stage[:].bitcast(BF16)
+        back_bf = hi_bf[:, 0 : 2 * PACK * HALF]
         back_codes = keep.tile([P, 2 * HALF], U32, name="back_codes", align_bytes=64)
         codes.append([back_codes[:, 0:HALF], back_codes[:, HALF:]])
         for a in range(2):
@@ -221,35 +226,30 @@ def tile_list_frame_delta_logits_kernel(
             part = back_bf[:, a * PACK * HALF : (a + 1) * PACK * HALF]
             quantize(codes[1][a], planes[1][:, a * HALF : (a + 1) * HALF], part)
 
-        near_bf = shared.tile([P, 2 * PACK * HALF], BF16, name="near_bf", offset=AT_STAGE, align_bytes=64)
-        for a in range(2):
-            pool_round(near_bf[:, a * PACK * HALF : (a + 1) * PACK * HALF], a, 0)
+        pool_round(hi_bf[:, 0 : PACK * K_PASS], 0, PACK)
+        pool_round(hi_bf[:, PACK * K_PASS : PACK * (K_PASS + HALF)], 1, 2)
         early = keep.tile([P, BANK], F32, name="early", align_bytes=64)
-        lower_magnitude = [early[:], row_at("late", AT_FAR - ROW)]
+        lower_magnitude = [early[:], stage[:, 3 * BANK :]]
         upper_magnitude = [hi_raw[1][:, s] for s in range(2)]
-        raw_at = [[AT_RAW, AT_RAW + ROW], [AT_RAW + 5 * ROW // 2, AT_RAW + 4 * ROW],
-                  [AT_RAW + 5 * ROW, AT_STAGE + 5 * ROW // 4], [AT_RAW + 6 * ROW, AT_RAW + 7 * ROW]]
-        term_at = [[AT_STAGE + ROW // 4, raw_at[0][0]], [AT_FAR - ROW // 2, AT_RAW + 2 * ROW],
-                   [AT_RAW + 3 * ROW, raw_at[1][1]], raw_at[2]]
+        behind = [AT_STAGE - ROW + 64 + n * ROW for n in range(5)]
+        raw_at = [[AT_RAW, AT_RAW + ROW], [AT_RAW + 2 * ROW, AT_RAW + 3 * ROW], [AT_RAW + 4 * ROW, behind[4]],
+                  [AT_RAW + 5 * ROW, AT_RAW + 6 * ROW]]
+        term_at = [behind[0:2], behind[2:4], raw_at[0], raw_at[1]]
+        hi_codes = shared.tile([P, 2 * K_PASS], U32, name="hi_codes", offset=AT_H + 2 * ROW, align_bytes=64)
         raws = []
         for t in range(PACK):
-            h = project(t, lower_magnitude)
+            if t == PACK - 1:
+                round_hi(hi_bf[:, PACK * (K_PASS + HALF) :], 1, 2, nc.scalar.copy)
+                for c0, c1 in ((0, K_PASS), (K_PASS, K_PASS + HALF), (K_PASS + HALF, 2 * K_PASS)):
+                    quantize(hi_codes[:, c0:c1], hi_planes[:, c0:c1], hi_bf[:, PACK * c0 : PACK * c1])
+                raws[2].append(row_at("raw2_1", raw_at[2][1]))
+                pick(raws[2][1], pos2_sb, h)
+            h = project(t, upper_magnitude if t == PACK - 1 else lower_magnitude)
             raws.append([])
             for i, pos_sb in enumerate((pos1_sb, pos2_sb)):
-                if (t, i) == (2, 1):
-                    near_codes = shared.tile([P, 2 * HALF], U32, name="near_codes", offset=AT_H + 2 * ROW, align_bytes=64)
-                    codes.append([near_codes[:, 0:HALF], near_codes[:, HALF:]])
-                    quantize(near_codes[:], planes[2][:], near_bf[:])
-                    far_bf = shared.tile([P, PACK * HALF], BF16, name="far_bf", offset=AT_FAR, align_bytes=64)
-                    pool_round(far_bf[:], 0, 2)
-                raws[t].append(row_at(f"raw{t}_{i}", raw_at[t][i]))
-                pick(raws[t][i], pos_sb, h)
-        far_parts = [far_bf[:], lower_magnitude[1].bitcast(BF16)]
-        round_hi(far_parts[1], 1, 2, nc.scalar.copy)
-        far_codes = shared.tile([P, 2 * HALF], U32, name="far_codes", offset=AT_H + 6 * ROW, align_bytes=64)
-        codes.append([far_codes[:, 0:HALF], far_codes[:, HALF:]])
-        for a in range(2):
-            quantize(codes[3][a], planes[3][:, a * HALF : (a + 1) * HALF], far_parts[a])
+                if (t, i) != (2, 1):
+                    raws[t].append(row_at(f"raw{t}_{i}", raw_at[t][i]))
+                    pick(raws[t][i], pos_sb, h)
         terms = []
         for t in range(PACK):
             terms.append([row_at(f"term{t}_{i}", term_at[t][i]) for i in range(2)])
@@ -259,7 +259,10 @@ def tile_list_frame_delta_logits_kernel(
         upper_flat = keep.tile([P, PACK * 2 * Q], F32, name="upper_flat", align_bytes=64)
         upper = upper_flat[:].rearrange("p (t i q) -> p t i q", i=2, q=Q)
         first, second = upper[:, :, 0], upper[:, :, 1]
-        z_rows = keep.tile([P, Q // P, 2, HALF], BF16, name="z_rows")
+        z_rows = [
+            second[:, PACK - 2].bitcast(BF16).rearrange("p (g u r) -> p g u r", g=2, u=2),
+            keep.tile([P, 2, 2, HALF], BF16, name="z_rows")[:],
+        ]
         z_first = shared.tile([P, K_PASS], BF16, name="z_first", offset=AT_Z, align_bytes=64)
         z_late = keep.tile([P, 2 * K_PASS], BF16, name="z_late", align_bytes=64)
         z_lo = [z_first[:], upper_flat[:, PACK * 2 * Q - HALF :].bitcast(BF16), z_late[:, 0:K_PASS], z_late[:, K_PASS:]]
@@ -291,7 +294,7 @@ def tile_list_frame_delta_logits_kernel(
             bank = banks[t][:].rearrange("p (g r) -> p g r", r=P)[:, g0:g1]
             places = slice(t * P // 2, (t + 1) * P // 2)
             nc.scalar.copy(
-                out=z_rows[:, g0:g1, :, places].rearrange("p g u (m e) -> p g u m e", e=2),
+                out=z_rows[g0 // 2][:, :, :, places].rearrange("p g u (m e) -> p g u m e", e=2),
                 in_=bank.rearrange("p g (m u e) -> p g u m e", u=2, e=2),
             )
 
@@ -299,8 +302,9 @@ def tile_list_frame_delta_logits_kernel(
             bank = banks[PACK + half][:].rearrange("p (g u q) -> p g u q", g=2, u=2)
             for g in range(2):
                 for u in range(2):
-                    nc.tensor.transpose(bank[:, g, u, :], z_rows[:, 2 * half + g, u].bitcast(F32), ident[:])
+                    nc.tensor.transpose(bank[:, g, u, :], z_rows[half][:, g, u].bitcast(F32), ident[:])
             if half == 0:
+                nc.scalar.activation(out=second[:, last - 1], in_=unscaled, func=ACT.Copy, scale=gain_hi[:, last - 1 : last])
                 for g in range(2):
                     nc.scalar.copy(
                         out=z_lo[g].bitcast(F32).rearrange("p (q u) -> p q u", u=2),
@@ -347,7 +351,9 @@ def tile_list_frame_delta_logits_kernel(
         for t in range(last):
             h = project(PACK + t, upper_magnitude)
             pick(first[:, t], pos1_sb, h)
-            pick(second[:, t], pos2_sb, h)
+            if t == last - 1:
+                unscaled = row_at("unscaled", raw_at[2][0])
+            pick(second[:, t] if t < last - 1 else unscaled, pos2_sb, h)
             scaled = upper_flat[:, 2 * t * Q : (2 * t + (2 if t < last - 1 else 1)) * Q]
             pool_gain(scaled, scaled, gain_hi[:, t : t + 1])
         h = project(PACK + last, upper_magnitude)
@@ -356,9 +362,6 @@ def tile_list_frame_delta_logits_kernel(
         for half in range(2):
             for t in range(PACK):
                 round_delta(t, 2 * half, 2 * half + 2)
-            if half == 0:
-                before = second[:, last - 1]
-                nc.scalar.activation(out=before, in_=before, func=ACT.Copy, scale=gain_hi[:, last - 1 : last])
             turn_back(half)
 
         pick_scaled(first[:, last], pos1_sb, last_row, h, 0, HALF)

@@ -32,7 +32,6 @@ AT_FRONT = AT_TABLE1 + 4 * T
 AT_STAGE = AT_TABLE1 + ROW
 AT_H = AT_FRONT + 2 * ROW
 AT_RAW = AT_H + 16 * ROW
-AT_Z = AT_RAW + 7 * ROW
 
 
 def tile_list_frame_delta_logits_kernel(
@@ -256,24 +255,17 @@ def tile_list_frame_delta_logits_kernel(
             for i, gains in enumerate((gain_lo, gain_minus)):
                 pool_gain(terms[t][i], raws[t][i], gains[:, t : t + 1])
 
-        upper_flat = keep.tile([P, PACK * 2 * Q], F32, name="upper_flat", align_bytes=64)
-        upper = upper_flat[:].rearrange("p (t i q) -> p t i q", i=2, q=Q)
+        upper_flat = keep.tile([P, PACK * 2 * Q + Q], F32, name="upper_flat", align_bytes=64)
+        upper = upper_flat[:, 0 : PACK * 2 * Q].rearrange("p (t i q) -> p t i q", i=2, q=Q)
         first, second = upper[:, :, 0], upper[:, :, 1]
         z_rows = [
             second[:, PACK - 2].bitcast(BF16).rearrange("p (g u r) -> p g u r", g=2, u=2),
             keep.tile([P, 2, 2, HALF], BF16, name="z_rows")[:],
         ]
-        z_first = shared.tile([P, K_PASS], BF16, name="z_first", offset=AT_Z, align_bytes=64)
-        z_late = keep.tile([P, 2 * K_PASS], BF16, name="z_late", align_bytes=64)
-        z_lo = [z_first[:], upper_flat[:, PACK * 2 * Q - HALF :].bitcast(BF16), z_late[:, 0:K_PASS], z_late[:, K_PASS:]]
-        z_upper = keep.tile([P, PACK * HALF], BF16, name="z_upper", align_bytes=64)
-        z_hi = [z_upper[:]] * 2
+        z_late = keep.tile([P, PACK * HALF], BF16, name="z_late", align_bytes=64)
+        z_lo = [upper_flat[:, PACK * 2 * Q - HALF : PACK * 2 * Q + HALF].bitcast(BF16), z_late[:]]
+        z_hi = [upper_flat[:, PACK * 2 * Q :].bitcast(BF16)] * 2
         z_codes = keep.tile([P, 2 * Q], U32, name="z_codes", align_bytes=64)
-
-        def z_words(half, b, q0, q1):
-            if (half, b) == (0, 1):
-                return upper_codes[:, q0:q1]
-            return z_codes[:, z_start(half, b) + q0 : z_start(half, b) + q1]
 
         z_planes = keep.tile([P, 2 * Q], U8, name="z_planes", align_bytes=64)
 
@@ -299,22 +291,16 @@ def tile_list_frame_delta_logits_kernel(
             )
 
         def turn_back(half):
-            bank = banks[PACK + half][:].rearrange("p (g u q) -> p g u q", g=2, u=2)
+            bank = banks[PACK + 1 - half][:].rearrange("p (g u q) -> p g u q", g=2, u=2)
             for g in range(2):
                 for u in range(2):
                     nc.tensor.transpose(bank[:, g, u, :], z_rows[half][:, g, u].bitcast(F32), ident[:])
             if half == 0:
                 nc.scalar.activation(out=second[:, last - 1], in_=unscaled, func=ACT.Copy, scale=gain_hi[:, last - 1 : last])
-                for g in range(2):
-                    nc.scalar.copy(
-                        out=z_lo[g].bitcast(F32).rearrange("p (q u) -> p q u", u=2),
-                        in_=bank[:, g].rearrange("p u q -> p q u"),
-                    )
-            else:
-                nc.scalar.copy(
-                    out=z_late[:].bitcast(F32).rearrange("p (g q u) -> p g q u", g=2, u=2),
-                    in_=bank.rearrange("p g u q -> p g q u"),
-                )
+            nc.scalar.copy(
+                out=z_lo[half].bitcast(F32).rearrange("p (g q u) -> p g q u", g=2, u=2),
+                in_=bank.rearrange("p g u q -> p g q u"),
+            )
 
         def subtract(dst, q0, q1):
             nc.vector.tensor_tensor(
@@ -327,25 +313,26 @@ def tile_list_frame_delta_logits_kernel(
         def z_start(half, b):
             return half * Q + (1 - b) * HALF
 
-        def logit_pass(bank_no, half, n0, n1, b, groups=(0, P), copy=None):
-            bank = banks[bank_no][:, 0 : (n1 - n0) * HALF].rearrange("p (n q) -> p n q", q=HALF)
-            for n in range(n0, n1):
-                for q in groups:
-                    cols = slice(z_start(half, b) + q, z_start(half, b) + q + P)
-                    nc.tensor.matmul_mx(
-                        out=bank[:, n - n0, q : q + P],
-                        lhsT=w2_codes[:, b, 2 * n * P : 2 * (n + 1) * P].bitcast(FP4X4),
-                        lhsT_scale=w2_planes[:, b, :].bitcast(U8)[:, n * P : (n + 1) * P],
-                        rhs=z_words(half, b, q, q + P).bitcast(FP8X4),
-                        rhs_scale=z_planes[:, cols],
-                        start=(b == 0 and n == n0 and q == 0),
-                        stop=(b == 1 and n == n1 - 1 and q == P),
-                    )
+        def quantize_z(half, b, src, q0=0, q1=HALF):
+            cols = slice(z_start(half, b) + q0, z_start(half, b) + q1)
+            quantize(z_codes[:, cols], z_planes[:, cols], src[:, PACK * q0 : PACK * q1])
+
+        def logit_pass(half, n, b, q0=0, q1=HALF, copy=None):
+            bank = banks[(BANKS - 1 - n) if half == 0 else n][:, 0:HALF]
+            cols = slice(z_start(half, b) + q0, z_start(half, b) + q1)
+            nc.tensor.matmul_mx(
+                out=bank[:, q0:q1],
+                lhsT=w2_codes[:, b, 2 * n * P : 2 * (n + 1) * P].bitcast(FP4X4),
+                lhsT_scale=w2_planes[:, b, :].bitcast(U8)[:, n * P : (n + 1) * P],
+                rhs=z_codes[:, cols].bitcast(FP8X4),
+                rhs_scale=z_planes[:, cols],
+                start=(b == 0),
+                stop=(b == 1 and q1 == HALF),
+            )
             if copy is not None:
-                staged = keep.tile([P, n1 - n0, HALF], F32, name=f"staged{bank_no}")
+                staged = keep.tile([P, HALF], F32, name=f"staged{half}_{n}")
                 copy(out=staged[:], in_=bank)
-                rows = out[n0 * P : n1 * P, half * HALF : (half + 1) * HALF]
-                nc.sync.dma_start(rows.rearrange("(n p) q -> p n q", p=P), staged[:])
+                nc.sync.dma_start(out[n * P : (n + 1) * P, half * HALF : (half + 1) * HALF], staged[:])
 
         last = PACK - 1
         for t in range(last):
@@ -367,27 +354,22 @@ def tile_list_frame_delta_logits_kernel(
         pick_scaled(first[:, last], pos1_sb, last_row, h, 0, HALF)
         pick_scaled(second[:, last], pos2_sb, last_row, h, 0, HALF)
         pick_scaled(first[:, last], pos1_sb, last_row, h, HALF, Q)
+        quantize_z(0, 0, z_lo[0])
         subtract(z_hi[0], 0, HALF)
-        upper_codes = shared.tile([P, HALF], U32, name="upper_codes", offset=AT_Z, align_bytes=64)
-        for g in range(2):
-            cols = slice(z_start(0, 0) + g * P, z_start(0, 0) + (g + 1) * P)
-            quantize(z_codes[:, cols], z_planes[:, cols], z_lo[g])
-        quantize(upper_codes[:], z_planes[:, z_start(0, 1) : z_start(0, 1) + HALF], z_hi[0])
         pick_scaled(second[:, last], pos2_sb, last_row, h, HALF, Q)
+        quantize_z(0, 1, z_hi[0])
         for b, copy in enumerate((None, nc.scalar.copy)):
-            for pair in range(2):
-                logit_pass(BANKS - 2 + pair, 0, 2 * pair, 2 * pair + 2, b, copy=copy)
+            for n in range(N // P):
+                logit_pass(0, n, b, copy=copy)
 
-        lower_cols = slice(z_start(1, 0), z_start(1, 0) + HALF)
-        quantize(z_codes[:, lower_cols], z_planes[:, lower_cols], z_late[:])
+        quantize_z(1, 0, z_lo[1])
         for n in range(N // P):
-            logit_pass(n, 1, n, n + 1, 0)
+            logit_pass(1, n, 0)
         for q in (0, P):
             subtract(z_hi[1][:, PACK * q : PACK * (q + P)], HALF + q, HALF + q + P)
         for q in (0, P):
-            cols = slice(z_start(1, 1) + q, z_start(1, 1) + q + P)
-            quantize(z_codes[:, cols], z_planes[:, cols], z_hi[1][:, PACK * q : PACK * (q + P)])
+            quantize_z(1, 1, z_hi[1], q, q + P)
         for n in range(N // P):
-            logit_pass(n, 1, n, n + 1, 1, groups=(0,))
+            logit_pass(1, n, 1, 0, P)
         for n in range(N // P):
-            logit_pass(n, 1, n, n + 1, 1, groups=(P,), copy=nc.vector.tensor_copy if n % 2 else nc.scalar.copy)
+            logit_pass(1, n, 1, P, HALF, copy=nc.vector.tensor_copy if n % 2 else nc.scalar.copy)

@@ -31,7 +31,10 @@ AT_TABLE1 = AT_SCALES + T
 AT_FRONT = AT_TABLE1 + 4 * T
 AT_STAGE = AT_TABLE1 + ROW
 AT_H = AT_FRONT + 2 * ROW
-AT_RAW = AT_H + 16 * ROW
+AT_EARLY = AT_H + 16 * ROW
+AT_LATE = AT_EARLY + ROW
+AT_FAR = AT_LATE + 2 * ROW
+AT_RAW = AT_FAR + 2 * ROW
 
 
 def tile_list_frame_delta_logits_kernel(
@@ -128,8 +131,8 @@ def tile_list_frame_delta_logits_kernel(
 
         def stationary(i, a):
             if i >= PACK:
-                c0 = a * K_PASS + (i - PACK) * P
-                return hi_codes[:, c0 : c0 + P], hi_planes[:, c0 : c0 + P]
+                c0 = (i - PACK) * P
+                return hi_codes[a][:, c0 : c0 + P], hi_planes[:, a * K_PASS + c0 : a * K_PASS + c0 + P]
             c0 = (i % 2) * P
             return codes[i // 2][a][:, c0 : c0 + P], planes[i // 2][:, a * HALF + c0 : a * HALF + c0 + P]
 
@@ -214,9 +217,8 @@ def tile_list_frame_delta_logits_kernel(
                 v_codes[1][:, s * BANK : (s + 1) * BANK],
                 table[1][:].bitcast(U32).indirect(offsets(offs_sb, s * BANK, (s + 1) * BANK)),
             )
-        stage = shared.tile([P, 2 * S], F32, name="stage", offset=AT_STAGE, align_bytes=64)
-        hi_bf = stage[:].bitcast(BF16)
-        back_bf = hi_bf[:, 0 : 2 * PACK * HALF]
+        stage = shared.tile([P, S], F32, name="stage", offset=AT_STAGE, align_bytes=64)
+        back_bf = stage[:].bitcast(BF16)
         back_codes = keep.tile([P, 2 * HALF], U32, name="back_codes", align_bytes=64)
         codes.append([back_codes[:, 0:HALF], back_codes[:, HALF:]])
         for a in range(2):
@@ -225,46 +227,54 @@ def tile_list_frame_delta_logits_kernel(
             part = back_bf[:, a * PACK * HALF : (a + 1) * PACK * HALF]
             quantize(codes[1][a], planes[1][:, a * HALF : (a + 1) * HALF], part)
 
-        pool_round(hi_bf[:, 0 : PACK * K_PASS], 0, PACK)
-        pool_round(hi_bf[:, PACK * K_PASS : PACK * (K_PASS + HALF)], 1, 2)
-        early = keep.tile([P, BANK], F32, name="early", align_bytes=64)
-        lower_magnitude = [early[:], stage[:, 3 * BANK :]]
+        pool_round(back_bf, 0, PACK)
+        far = row_at("far", AT_FAR)
+        far_bf = far.bitcast(BF16)
+        magnitudes = [[far, row_at("early", AT_EARLY)]] * 2 + [[far, row_at("late", AT_LATE)]]
         upper_magnitude = [hi_raw[1][:, s] for s in range(2)]
-        behind = [AT_STAGE - ROW + 64 + n * ROW for n in range(5)]
-        raw_at = [[AT_RAW, AT_RAW + ROW], [AT_RAW + 2 * ROW, AT_RAW + 3 * ROW], [AT_RAW + 4 * ROW, behind[4]],
+        raw_at = [[AT_RAW, AT_RAW + 3 * ROW // 2], [AT_RAW + 3 * ROW, None], [AT_RAW + 4 * ROW, AT_FAR + ROW // 2],
                   [AT_RAW + 5 * ROW, AT_RAW + 6 * ROW]]
-        term_at = [behind[0:2], behind[2:4], raw_at[0], raw_at[1]]
-        hi_codes = shared.tile([P, 2 * K_PASS], U32, name="hi_codes", offset=AT_H + 2 * ROW, align_bytes=64)
-        raws = []
+        term_at = [[AT_FAR - ROW // 2, raw_at[0][0]], [AT_RAW + ROW, AT_RAW + 2 * ROW], [raw_at[1][0], raw_at[2][0]],
+                   [AT_RAW + 7 * ROW, AT_RAW + 8 * ROW]]
+        hi_codes = []
+        raws = [[None, None] for t in range(PACK)]
+
+        def gather_lower(t, i, h):
+            raws[t][i] = stage[:, BANK:] if (t, i) == (1, 1) else row_at(f"raw{t}_{i}", raw_at[t][i])
+            pick(raws[t][i], (pos1_sb, pos2_sb)[i], h)
+
         for t in range(PACK):
             if t == PACK - 1:
-                round_hi(hi_bf[:, PACK * (K_PASS + HALF) :], 1, 2, nc.scalar.copy)
-                for c0, c1 in ((0, K_PASS), (K_PASS, K_PASS + HALF), (K_PASS + HALF, 2 * K_PASS)):
-                    quantize(hi_codes[:, c0:c1], hi_planes[:, c0:c1], hi_bf[:, PACK * c0 : PACK * c1])
-                raws[2].append(row_at("raw2_1", raw_at[2][1]))
-                pick(raws[2][1], pos2_sb, h)
-            h = project(t, upper_magnitude if t == PACK - 1 else lower_magnitude)
-            raws.append([])
-            for i, pos_sb in enumerate((pos1_sb, pos2_sb)):
-                if (t, i) != (2, 1):
-                    raws[t].append(row_at(f"raw{t}_{i}", raw_at[t][i]))
-                    pick(raws[t][i], pos_sb, h)
+                magnitudes.append([row_at(f"last{s}", AT_H + s * ROW) for s in range(2)])
+            h = project(t, magnitudes[t])
+            gather_lower(t, 0, h)
+            if t == 1:
+                hi_codes.append(shared.tile([P, K_PASS], U32, name="hi_codes0", offset=AT_EARLY, align_bytes=64))
+                quantize(hi_codes[0][:], hi_planes[:, 0:K_PASS], back_bf)
+                pool_round(back_bf[:, 0 : PACK * HALF], 1, 2)
+            if t == 2:
+                round_hi(far_bf, 1, 2, nc.scalar.copy)
+                hi_codes.append(shared.tile([P, K_PASS], U32, name="hi_codes1", offset=AT_LATE, align_bytes=64))
+                for c0, src in ((0, back_bf[:, 0 : PACK * HALF]), (HALF, far_bf)):
+                    quantize(hi_codes[1][:, c0 : c0 + HALF], hi_planes[:, K_PASS + c0 : K_PASS + c0 + HALF], src)
+            gather_lower(t, 1, h)
         terms = []
         for t in range(PACK):
             terms.append([row_at(f"term{t}_{i}", term_at[t][i]) for i in range(2)])
             for i, gains in enumerate((gain_lo, gain_minus)):
                 pool_gain(terms[t][i], raws[t][i], gains[:, t : t + 1])
 
-        upper_flat = keep.tile([P, PACK * 2 * Q + Q], F32, name="upper_flat", align_bytes=64)
-        upper = upper_flat[:, 0 : PACK * 2 * Q].rearrange("p (t i q) -> p t i q", i=2, q=Q)
+        upper_flat = keep.tile([P, PACK * 2 * Q], F32, name="upper_flat", align_bytes=64)
+        upper = upper_flat[:].rearrange("p (t i q) -> p t i q", i=2, q=Q)
         first, second = upper[:, :, 0], upper[:, :, 1]
         z_rows = [
             second[:, PACK - 2].bitcast(BF16).rearrange("p (g u r) -> p g u r", g=2, u=2),
             keep.tile([P, 2, 2, HALF], BF16, name="z_rows")[:],
         ]
+        z_early = [upper[:, PACK - 1, i, HALF:].bitcast(BF16) for i in range(2)]
         z_late = keep.tile([P, PACK * HALF], BF16, name="z_late", align_bytes=64)
-        z_lo = [upper_flat[:, PACK * 2 * Q - HALF : PACK * 2 * Q + HALF].bitcast(BF16), z_late[:]]
-        z_hi = [upper_flat[:, PACK * 2 * Q :].bitcast(BF16)] * 2
+        z_upper = keep.tile([P, PACK * HALF], BF16, name="z_upper", align_bytes=64)
+        z_hi = [z_upper[:]] * 2
         z_codes = keep.tile([P, 2 * Q], U32, name="z_codes", align_bytes=64)
 
         z_planes = keep.tile([P, 2 * Q], U8, name="z_planes", align_bytes=64)
@@ -290,17 +300,27 @@ def tile_list_frame_delta_logits_kernel(
                 in_=bank.rearrange("p g (m u e) -> p g u m e", u=2, e=2),
             )
 
+        def scale_unscaled(q0, q1):
+            gains = gain_hi[:, last - 1 : last]
+            nc.scalar.activation(out=second[:, last - 1, q0:q1], in_=unscaled[:, q0:q1], func=ACT.Copy, scale=gains)
+
         def turn_back(half):
             bank = banks[PACK + 1 - half][:].rearrange("p (g u q) -> p g u q", g=2, u=2)
             for g in range(2):
                 for u in range(2):
                     nc.tensor.transpose(bank[:, g, u, :], z_rows[half][:, g, u].bitcast(F32), ident[:])
             if half == 0:
-                nc.scalar.activation(out=second[:, last - 1], in_=unscaled, func=ACT.Copy, scale=gain_hi[:, last - 1 : last])
-            nc.scalar.copy(
-                out=z_lo[half].bitcast(F32).rearrange("p (g q u) -> p g q u", g=2, u=2),
-                in_=bank.rearrange("p g u q -> p g q u"),
-            )
+                scale_unscaled(0, HALF)
+                for g in range(2):
+                    nc.scalar.copy(
+                        out=z_early[g].bitcast(F32).rearrange("p (q u) -> p q u", u=2),
+                        in_=bank[:, g].rearrange("p u q -> p q u"),
+                    )
+            else:
+                nc.scalar.copy(
+                    out=z_late[:].bitcast(F32).rearrange("p (g q u) -> p g q u", g=2, u=2),
+                    in_=bank.rearrange("p g u q -> p g q u"),
+                )
 
         def subtract(dst, q0, q1):
             nc.vector.tensor_tensor(
@@ -315,7 +335,7 @@ def tile_list_frame_delta_logits_kernel(
 
         def quantize_z(half, b, src, q0=0, q1=HALF):
             cols = slice(z_start(half, b) + q0, z_start(half, b) + q1)
-            quantize(z_codes[:, cols], z_planes[:, cols], src[:, PACK * q0 : PACK * q1])
+            quantize(z_codes[:, cols], z_planes[:, cols], src)
 
         def logit_pass(half, n, b, q0=0, q1=HALF, copy=None):
             bank = banks[(BANKS - 1 - n) if half == 0 else n][:, 0:HALF]
@@ -326,7 +346,7 @@ def tile_list_frame_delta_logits_kernel(
                 lhsT_scale=w2_planes[:, b, :].bitcast(U8)[:, n * P : (n + 1) * P],
                 rhs=z_codes[:, cols].bitcast(FP8X4),
                 rhs_scale=z_planes[:, cols],
-                start=(b == 0),
+                start=(b == 0 and q0 == 0),
                 stop=(b == 1 and q1 == HALF),
             )
             if copy is not None:
@@ -339,7 +359,7 @@ def tile_list_frame_delta_logits_kernel(
             h = project(PACK + t, upper_magnitude)
             pick(first[:, t], pos1_sb, h)
             if t == last - 1:
-                unscaled = row_at("unscaled", raw_at[2][0])
+                unscaled = row_at("unscaled", raw_at[3][0])
             pick(second[:, t] if t < last - 1 else unscaled, pos2_sb, h)
             scaled = upper_flat[:, 2 * t * Q : (2 * t + (2 if t < last - 1 else 1)) * Q]
             pool_gain(scaled, scaled, gain_hi[:, t : t + 1])
@@ -353,22 +373,26 @@ def tile_list_frame_delta_logits_kernel(
 
         pick_scaled(first[:, last], pos1_sb, last_row, h, 0, HALF)
         pick_scaled(second[:, last], pos2_sb, last_row, h, 0, HALF)
-        pick_scaled(first[:, last], pos1_sb, last_row, h, HALF, Q)
-        quantize_z(0, 0, z_lo[0])
         subtract(z_hi[0], 0, HALF)
-        pick_scaled(second[:, last], pos2_sb, last_row, h, HALF, Q)
+        scale_unscaled(HALF, Q)
+        for g in range(2):
+            quantize_z(0, 0, z_early[g], g * P, (g + 1) * P)
         quantize_z(0, 1, z_hi[0])
-        for b, copy in enumerate((None, nc.scalar.copy)):
+        pick_scaled(first[:, last], pos1_sb, last_row, h, HALF, Q)
+        pick_scaled(second[:, last], pos2_sb, last_row, h, HALF, Q)
+        for g in range(2):
             for n in range(N // P):
-                logit_pass(0, n, b, copy=copy)
+                logit_pass(0, n, 0, g * P, (g + 1) * P)
+        for n in range(N // P):
+            logit_pass(0, n, 1, copy=nc.scalar.copy)
 
-        quantize_z(1, 0, z_lo[1])
+        quantize_z(1, 0, z_late[:])
         for n in range(N // P):
             logit_pass(1, n, 0)
         for q in (0, P):
             subtract(z_hi[1][:, PACK * q : PACK * (q + P)], HALF + q, HALF + q + P)
         for q in (0, P):
-            quantize_z(1, 1, z_hi[1], q, q + P)
+            quantize_z(1, 1, z_hi[1][:, PACK * q : PACK * (q + P)], q, q + P)
         for n in range(N // P):
             logit_pass(1, n, 1, 0, P)
         for n in range(N // P):

@@ -35,6 +35,8 @@ AT_EARLY = AT_H + 16 * ROW
 AT_LATE = AT_EARLY + ROW
 AT_FAR = AT_LATE + 2 * ROW
 AT_RAW = AT_FAR + 2 * ROW
+AT_ROWS = AT_RAW + 9 * ROW
+AT_Z = AT_ROWS + 2 * ROW
 
 
 def tile_list_frame_delta_logits_kernel(
@@ -172,10 +174,10 @@ def tile_list_frame_delta_logits_kernel(
             return list_sb[:, j0 // LANES : j1 // LANES]
 
         def pick_scaled(dst, pos_sb, row, h, q0=0, q1=Q):
-            nc.vector.tensor_tensor(dst[:, q0:q1], h[:].indirect(offsets(pos_sb, q0, q1)), row[:, q0:q1], ALU.mult)
+            nc.vector.tensor_tensor(dst[:, q0:q1], h[:].indirect(offsets(pos_sb, q0, q1)), row, ALU.mult)
 
-        def pick(dst, pos_sb, h):
-            nc.vector.tensor_copy(dst, h[:].indirect(pos_sb[:]))
+        def pick(dst, pos_sb, h, q0=0, q1=Q):
+            nc.vector.tensor_copy(dst[:, q0:q1], h[:].indirect(offsets(pos_sb, q0, q1)))
 
         def pool_copy(out, in_):
             nc.gpsimd.tensor_scalar(out, in_, 1.0, 0.0, ALU.mult, ALU.add)
@@ -208,8 +210,8 @@ def tile_list_frame_delta_logits_kernel(
         for i in range(2):
             for s in range(2):
                 x_pass(i, 0, s)
-        last_row = row_at("last_row", AT_FRONT)
-        nc.scalar.copy(out=last_row, in_=gain_hi[:, PACK - 1 : PACK].to_broadcast([P, Q]))
+        first_rows = shared.tile([P, 2, HALF], F32, name="first_rows", offset=AT_FRONT, align_bytes=64)
+        nc.scalar.copy(out=first_rows[:], in_=gain_hi[:, PACK - 2 :].unsqueeze(2).to_broadcast([P, 2, HALF]))
 
         v_codes.append(keep.tile([P, S], U32, name="v_codes1", tag="chain", align_bytes=64))
         for s in range(2):
@@ -264,15 +266,17 @@ def tile_list_frame_delta_logits_kernel(
             for i, gains in enumerate((gain_lo, gain_minus)):
                 pool_gain(terms[t][i], raws[t][i], gains[:, t : t + 1])
 
-        upper_flat = keep.tile([P, PACK * 2 * Q], F32, name="upper_flat", align_bytes=64)
-        upper = upper_flat[:].rearrange("p (t i q) -> p t i q", i=2, q=Q)
-        first, second = upper[:, :, 0], upper[:, :, 1]
-        z_rows = [
-            second[:, PACK - 2].bitcast(BF16).rearrange("p (g u r) -> p g u r", g=2, u=2),
-            keep.tile([P, 2, 2, HALF], BF16, name="z_rows")[:],
+        first, second = [
+            keep.tile([P, PACK * Q], F32, name=name, align_bytes=64)[:].rearrange("p (t q) -> p t q", q=Q)
+            for name in ("first", "second")
         ]
-        z_early = [upper[:, PACK - 1, i, HALF:].bitcast(BF16) for i in range(2)]
+        z_rows = [
+            shared.tile([P, 2, 2, HALF], BF16, name=f"z_rows{half}", offset=AT_ROWS + half * ROW, align_bytes=64)
+            for half in range(2)
+        ]
+        z_first = shared.tile([P, PACK * HALF], BF16, name="z_first", offset=AT_Z, align_bytes=64)
         z_late = keep.tile([P, PACK * HALF], BF16, name="z_late", align_bytes=64)
+        z_lo = [z_first, z_late]
         z_upper = keep.tile([P, PACK * HALF], BF16, name="z_upper", align_bytes=64)
         z_hi = [z_upper[:]] * 2
         z_codes = keep.tile([P, 2 * Q], U32, name="z_codes", align_bytes=64)
@@ -300,27 +304,15 @@ def tile_list_frame_delta_logits_kernel(
                 in_=bank.rearrange("p g (m u e) -> p g u m e", u=2, e=2),
             )
 
-        def scale_unscaled(q0, q1):
-            gains = gain_hi[:, last - 1 : last]
-            nc.scalar.activation(out=second[:, last - 1, q0:q1], in_=unscaled[:, q0:q1], func=ACT.Copy, scale=gains)
-
         def turn_back(half):
             bank = banks[PACK + 1 - half][:].rearrange("p (g u q) -> p g u q", g=2, u=2)
             for g in range(2):
                 for u in range(2):
                     nc.tensor.transpose(bank[:, g, u, :], z_rows[half][:, g, u].bitcast(F32), ident[:])
-            if half == 0:
-                scale_unscaled(0, HALF)
-                for g in range(2):
-                    nc.scalar.copy(
-                        out=z_early[g].bitcast(F32).rearrange("p (q u) -> p q u", u=2),
-                        in_=bank[:, g].rearrange("p u q -> p q u"),
-                    )
-            else:
-                nc.scalar.copy(
-                    out=z_late[:].bitcast(F32).rearrange("p (g q u) -> p g q u", g=2, u=2),
-                    in_=bank.rearrange("p g u q -> p g q u"),
-                )
+            nc.scalar.copy(
+                out=z_lo[half][:].bitcast(F32).rearrange("p (g q u) -> p g q u", g=2, u=2),
+                in_=bank.rearrange("p g u q -> p g q u"),
+            )
 
         def subtract(dst, q0, q1):
             nc.vector.tensor_tensor(
@@ -333,9 +325,14 @@ def tile_list_frame_delta_logits_kernel(
         def z_start(half, b):
             return half * Q + (1 - b) * HALF
 
+        def z_words(half, b, q0, q1):
+            if (half, b) == (0, 1):
+                return upper_codes[:, q0:q1]
+            return z_codes[:, z_start(half, b) + q0 : z_start(half, b) + q1]
+
         def quantize_z(half, b, src, q0=0, q1=HALF):
             cols = slice(z_start(half, b) + q0, z_start(half, b) + q1)
-            quantize(z_codes[:, cols], z_planes[:, cols], src)
+            quantize(z_words(half, b, q0, q1), z_planes[:, cols], src)
 
         def logit_pass(half, n, b, q0=0, q1=HALF, copy=None):
             bank = banks[(BANKS - 1 - n) if half == 0 else n][:, 0:HALF]
@@ -344,7 +341,7 @@ def tile_list_frame_delta_logits_kernel(
                 out=bank[:, q0:q1],
                 lhsT=w2_codes[:, b, 2 * n * P : 2 * (n + 1) * P].bitcast(FP4X4),
                 lhsT_scale=w2_planes[:, b, :].bitcast(U8)[:, n * P : (n + 1) * P],
-                rhs=z_codes[:, cols].bitcast(FP8X4),
+                rhs=z_words(half, b, q0, q1).bitcast(FP8X4),
                 rhs_scale=z_planes[:, cols],
                 start=(b == 0 and q0 == 0),
                 stop=(b == 1 and q1 == HALF),
@@ -358,11 +355,14 @@ def tile_list_frame_delta_logits_kernel(
         for t in range(last):
             h = project(PACK + t, upper_magnitude)
             pick(first[:, t], pos1_sb, h)
-            if t == last - 1:
-                unscaled = row_at("unscaled", raw_at[3][0])
-            pick(second[:, t] if t < last - 1 else unscaled, pos2_sb, h)
-            scaled = upper_flat[:, 2 * t * Q : (2 * t + (2 if t < last - 1 else 1)) * Q]
-            pool_gain(scaled, scaled, gain_hi[:, t : t + 1])
+            if t < last - 1:
+                pick(second[:, t], pos2_sb, h)
+                for part in (first, second):
+                    pool_gain(part[:, t], part[:, t], gain_hi[:, t : t + 1])
+            else:
+                pool_gain(first[:, t, 0:HALF], first[:, t, 0:HALF], gain_hi[:, t : t + 1])
+                pick(second[:, t], pos2_sb, h, HALF, Q)
+                pick_scaled(second[:, t], pos2_sb, first_rows[:, 0], h, 0, HALF)
         h = project(PACK + last, upper_magnitude)
         for t in range(PACK):
             turn_delta(t)
@@ -370,19 +370,25 @@ def tile_list_frame_delta_logits_kernel(
             for t in range(PACK):
                 round_delta(t, 2 * half, 2 * half + 2)
             turn_back(half)
+            if half == 0:
+                late_row = shared.tile([P, HALF], F32, name="late_row", offset=AT_ROWS, align_bytes=64)
+                nc.scalar.copy(out=late_row[:], in_=gain_hi[:, last:].to_broadcast([P, HALF]))
+        late_gain = shared.tile([P, 1], F32, name="late_gain", offset=AT_ROWS + ROW, align_bytes=64)
+        nc.scalar.copy(out=late_gain[:], in_=gain_hi[:, last - 1 : last])
 
-        pick_scaled(first[:, last], pos1_sb, last_row, h, 0, HALF)
-        pick_scaled(second[:, last], pos2_sb, last_row, h, 0, HALF)
+        pick_scaled(first[:, last], pos1_sb, first_rows[:, 1], h, 0, HALF)
+        pick_scaled(second[:, last], pos2_sb, first_rows[:, 1], h, 0, HALF)
         subtract(z_hi[0], 0, HALF)
-        scale_unscaled(HALF, Q)
-        for g in range(2):
-            quantize_z(0, 0, z_early[g], g * P, (g + 1) * P)
+        for part in (first, second):
+            rest = part[:, last - 1, HALF:]
+            nc.scalar.activation(out=rest, in_=rest, func=ACT.Copy, scale=late_gain[:])
+        quantize_z(0, 0, z_first[:])
+        upper_codes = shared.tile([P, HALF], U32, name="upper_codes", offset=AT_Z, align_bytes=64)
         quantize_z(0, 1, z_hi[0])
-        pick_scaled(first[:, last], pos1_sb, last_row, h, HALF, Q)
-        pick_scaled(second[:, last], pos2_sb, last_row, h, HALF, Q)
-        for g in range(2):
-            for n in range(N // P):
-                logit_pass(0, n, 0, g * P, (g + 1) * P)
+        pick_scaled(first[:, last], pos1_sb, late_row[:], h, HALF, Q)
+        pick_scaled(second[:, last], pos2_sb, late_row[:], h, HALF, Q)
+        for n in range(N // P):
+            logit_pass(0, n, 0)
         for n in range(N // P):
             logit_pass(0, n, 1, copy=nc.scalar.copy)
 

@@ -29,8 +29,9 @@ ROW = 4 * Q
 AT_SCALES = 0
 AT_TABLE1 = AT_SCALES + T
 AT_FRONT = AT_TABLE1 + 4 * T
-AT_STAGE = AT_TABLE1 + ROW
-AT_H = AT_FRONT + 2 * ROW
+AT_CODES1 = AT_FRONT + 2 * ROW
+AT_STAGE = AT_CODES1 + 2 * ROW
+AT_H = AT_STAGE + 2 * ROW
 AT_EARLY = AT_H + 16 * ROW
 AT_LATE = AT_EARLY + ROW
 AT_FAR = AT_LATE + 2 * ROW
@@ -53,7 +54,7 @@ def tile_list_frame_delta_logits_kernel(
         pos1_sb = keep.tile([P, Q // LANES], U16, name="pos1_sb")
         pos2_sb = keep.tile([P, Q // LANES], U16, name="pos2_sb")
         gain_flat = keep.tile([P, P], F32, name="gain_flat")
-        front_bf = keep.tile([P, 2 * PACK * HALF], BF16, name="front_bf", tag="chain", align_bytes=64)
+        front_bf = shared.tile([P, 2 * PACK * HALF], BF16, name="front_bf", offset=AT_CODES1 + ROW, align_bytes=64)
         gain_lo = keep.tile([P, PACK], F32, name="gain_lo")
         gain_hi = keep.tile([P, PACK], F32, name="gain_hi")
         table_scales = shared.tile([P, T // 4], I32, name="table_scales", offset=AT_SCALES, align_bytes=64)
@@ -213,7 +214,7 @@ def tile_list_frame_delta_logits_kernel(
         first_rows = shared.tile([P, 2, HALF], F32, name="first_rows", offset=AT_FRONT, align_bytes=64)
         nc.scalar.copy(out=first_rows[:], in_=gain_hi[:, PACK - 2 :].unsqueeze(2).to_broadcast([P, 2, HALF]))
 
-        v_codes.append(keep.tile([P, S], U32, name="v_codes1", tag="chain", align_bytes=64))
+        v_codes.append(shared.tile([P, S], U32, name="v_codes1", offset=AT_CODES1, align_bytes=64))
         for s in range(2):
             nc.vector.tensor_copy(
                 v_codes[1][:, s * BANK : (s + 1) * BANK],
@@ -234,7 +235,7 @@ def tile_list_frame_delta_logits_kernel(
         far_bf = far.bitcast(BF16)
         magnitudes = [[far, row_at("early", AT_EARLY)]] * 2 + [[far, row_at("late", AT_LATE)]]
         upper_magnitude = [hi_raw[1][:, s] for s in range(2)]
-        raw_at = [[AT_RAW, AT_RAW + 3 * ROW // 2], [AT_RAW + 3 * ROW, None], [AT_RAW + 4 * ROW, AT_FAR + ROW // 2],
+        raw_at = [[AT_RAW, AT_RAW + 3 * ROW // 2], [AT_RAW + 3 * ROW, None], [AT_RAW + 4 * ROW, None],
                   [AT_RAW + 5 * ROW, AT_RAW + 6 * ROW]]
         term_at = [[AT_FAR - ROW // 2, raw_at[0][0]], [AT_RAW + ROW, AT_RAW + 2 * ROW], [raw_at[1][0], raw_at[2][0]],
                    [AT_RAW + 7 * ROW, AT_RAW + 8 * ROW]]
@@ -242,7 +243,7 @@ def tile_list_frame_delta_logits_kernel(
         raws = [[None, None] for t in range(PACK)]
 
         def gather_lower(t, i, h):
-            raws[t][i] = stage[:, BANK:] if (t, i) == (1, 1) else row_at(f"raw{t}_{i}", raw_at[t][i])
+            raws[t][i] = hi_raw[t - 1][:, 2] if raw_at[t][i] is None else row_at(f"raw{t}_{i}", raw_at[t][i])
             pick(raws[t][i], (pos1_sb, pos2_sb)[i], h)
 
         for t in range(PACK):
@@ -266,10 +267,8 @@ def tile_list_frame_delta_logits_kernel(
             for i, gains in enumerate((gain_lo, gain_minus)):
                 pool_gain(terms[t][i], raws[t][i], gains[:, t : t + 1])
 
-        first, second = [
-            keep.tile([P, PACK * Q], F32, name=name, align_bytes=64)[:].rearrange("p (t q) -> p t q", q=Q)
-            for name in ("first", "second")
-        ]
+        both = keep.tile([P, 2, PACK, Q], F32, name="both", align_bytes=64)
+        second, first = both[:, 0], both[:, 1]
         z_rows = [
             shared.tile([P, 2, 2, HALF], BF16, name=f"z_rows{half}", offset=AT_ROWS + half * ROW, align_bytes=64)
             for half in range(2)
@@ -363,6 +362,8 @@ def tile_list_frame_delta_logits_kernel(
                 pool_gain(first[:, t, 0:HALF], first[:, t, 0:HALF], gain_hi[:, t : t + 1])
                 pick(second[:, t], pos2_sb, h, HALF, Q)
                 pick_scaled(second[:, t], pos2_sb, first_rows[:, 0], h, 0, HALF)
+                rest = both[:, :, t, HALF:]
+                nc.vector.tensor_scalar(rest, rest, gain_hi[:, t : t + 1], None, ALU.mult)
         h = project(PACK + last, upper_magnitude)
         for t in range(PACK):
             turn_delta(t)
@@ -372,20 +373,15 @@ def tile_list_frame_delta_logits_kernel(
             turn_back(half)
             if half == 0:
                 late_row = shared.tile([P, HALF], F32, name="late_row", offset=AT_ROWS, align_bytes=64)
-                nc.scalar.copy(out=late_row[:], in_=gain_hi[:, last:].to_broadcast([P, HALF]))
-        late_gain = shared.tile([P, 1], F32, name="late_gain", offset=AT_ROWS + ROW, align_bytes=64)
-        nc.scalar.copy(out=late_gain[:], in_=gain_hi[:, last - 1 : last])
+                nc.scalar.copy(out=late_row[:], in_=first_rows[:, 1])
 
         pick_scaled(first[:, last], pos1_sb, first_rows[:, 1], h, 0, HALF)
         pick_scaled(second[:, last], pos2_sb, first_rows[:, 1], h, 0, HALF)
+        pick_scaled(first[:, last], pos1_sb, first_rows[:, 1], h, HALF, Q)
         subtract(z_hi[0], 0, HALF)
-        for part in (first, second):
-            rest = part[:, last - 1, HALF:]
-            nc.scalar.activation(out=rest, in_=rest, func=ACT.Copy, scale=late_gain[:])
         quantize_z(0, 0, z_first[:])
-        upper_codes = shared.tile([P, HALF], U32, name="upper_codes", offset=AT_Z, align_bytes=64)
+        upper_codes = shared.tile([P, HALF], U32, name="upper_codes", offset=AT_FRONT, align_bytes=64)
         quantize_z(0, 1, z_hi[0])
-        pick_scaled(first[:, last], pos1_sb, late_row[:], h, HALF, Q)
         pick_scaled(second[:, last], pos2_sb, late_row[:], h, HALF, Q)
         for n in range(N // P):
             logit_pass(0, n, 0)

@@ -25,13 +25,15 @@ BANKS = 8
 LANES = 16
 QUAD = 32
 HALF = 256
+POOL_SHARE = 88
+LAP = 128
 ROW = 4 * Q
 AT_SCALES = 0
 AT_TABLE1 = AT_SCALES + T
 AT_FRONT = AT_TABLE1 + 4 * T
 AT_CODES1 = AT_FRONT + 2 * ROW
 AT_STAGE = AT_CODES1 + 2 * ROW
-AT_H = AT_STAGE + 2 * ROW
+AT_H = AT_STAGE + 4 * ROW
 AT_EARLY = AT_H + 16 * ROW
 AT_LATE = AT_EARLY + ROW
 AT_FAR = AT_LATE + 2 * ROW
@@ -97,10 +99,10 @@ def tile_list_frame_delta_logits_kernel(
         load_table(1)
         for a in range(2):
             load_w1(back_raw[a][:], a, HALF, K_PASS)
+        load_w1(hi_raw[0][:], 0, K_PASS, H)
         nc.sync.dma_start(pos1_sb[:], pos1)
         nc.sync.dma_start(pos2_sb[:], pos2)
-        for a in range(2):
-            load_w1(hi_raw[a][:], a, K_PASS, H)
+        load_w1(hi_raw[1][:], 1, K_PASS, H)
         nc.sync.dma_start(w2_codes[:].bitcast(I32), w2_words.rearrange("b p c -> p b c").bitcast(I32))
         nc.vector.memset(w2_planes[:], 0)
         for quad in range(P // QUAD):
@@ -220,17 +222,23 @@ def tile_list_frame_delta_logits_kernel(
                 v_codes[1][:, s * BANK : (s + 1) * BANK],
                 table[1][:].bitcast(U32).indirect(offsets(offs_sb, s * BANK, (s + 1) * BANK)),
             )
-        stage = shared.tile([P, S], F32, name="stage", offset=AT_STAGE, align_bytes=64)
-        back_bf = stage[:].bitcast(BF16)
+        piece = PACK * HALF
+        stage = shared.tile([P, 4 * piece - 2 * LAP], BF16, name="stage", offset=AT_STAGE, align_bytes=64)
+        hi_bf = stage[:, piece - LAP : 3 * piece - LAP]
+        back_bf = [stage[:, 3 * piece - 2 * LAP :], stage[:, 0:piece]]
         back_codes = keep.tile([P, 2 * HALF], U32, name="back_codes", align_bytes=64)
         codes.append([back_codes[:, 0:HALF], back_codes[:, HALF:]])
         for a in range(2):
-            round_lo(back_bf[:, a * PACK * HALF : (a + 1) * PACK * HALF], back_raw[a], 0, HALF, nc.vector.tensor_copy)
+            round_lo(back_bf[a], back_raw[a], 0, HALF, nc.vector.tensor_copy)
         for a in range(2):
-            part = back_bf[:, a * PACK * HALF : (a + 1) * PACK * HALF]
-            quantize(codes[1][a], planes[1][:, a * HALF : (a + 1) * HALF], part)
+            quantize(codes[1][a], planes[1][:, a * HALF : (a + 1) * HALF], back_bf[a])
 
-        pool_round(back_bf, 0, PACK)
+        rounded = hi_bf.rearrange("p (t m j) -> p m t j", t=PACK, j=PACK)
+        source = hi_raw[0][:].rearrange("p j (m t) -> p m t j", t=PACK)
+        nc.vector.tensor_copy(
+            rounded[:, POOL_SHARE:].rearrange("p m t j -> p m j t"), source[:, POOL_SHARE:].rearrange("p m t j -> p m j t")
+        )
+        pool_copy(rounded[:, 0:POOL_SHARE], source[:, 0:POOL_SHARE])
         far = row_at("far", AT_FAR)
         far_bf = far.bitcast(BF16)
         magnitudes = [[far, row_at("early", AT_EARLY)]] * 2 + [[far, row_at("late", AT_LATE)]]
@@ -253,12 +261,12 @@ def tile_list_frame_delta_logits_kernel(
             gather_lower(t, 0, h)
             if t == 1:
                 hi_codes.append(shared.tile([P, K_PASS], U32, name="hi_codes0", offset=AT_EARLY, align_bytes=64))
-                quantize(hi_codes[0][:], hi_planes[:, 0:K_PASS], back_bf)
-                pool_round(back_bf[:, 0 : PACK * HALF], 1, 2)
+                quantize(hi_codes[0][:], hi_planes[:, 0:K_PASS], hi_bf)
+                pool_round(hi_bf[:, 0:piece], 1, 2)
             if t == 2:
                 round_hi(far_bf, 1, 2, nc.scalar.copy)
                 hi_codes.append(shared.tile([P, K_PASS], U32, name="hi_codes1", offset=AT_LATE, align_bytes=64))
-                for c0, src in ((0, back_bf[:, 0 : PACK * HALF]), (HALF, far_bf)):
+                for c0, src in ((0, hi_bf[:, 0:piece]), (HALF, far_bf)):
                     quantize(hi_codes[1][:, c0 : c0 + HALF], hi_planes[:, K_PASS + c0 : K_PASS + c0 + HALF], src)
             gather_lower(t, 1, h)
         terms = []
@@ -362,8 +370,6 @@ def tile_list_frame_delta_logits_kernel(
                 pool_gain(first[:, t, 0:HALF], first[:, t, 0:HALF], gain_hi[:, t : t + 1])
                 pick(second[:, t], pos2_sb, h, HALF, Q)
                 pick_scaled(second[:, t], pos2_sb, first_rows[:, 0], h, 0, HALF)
-                rest = both[:, :, t, HALF:]
-                nc.vector.tensor_scalar(rest, rest, gain_hi[:, t : t + 1], None, ALU.mult)
         h = project(PACK + last, upper_magnitude)
         for t in range(PACK):
             turn_delta(t)
@@ -374,11 +380,15 @@ def tile_list_frame_delta_logits_kernel(
             if half == 0:
                 late_row = shared.tile([P, HALF], F32, name="late_row", offset=AT_ROWS, align_bytes=64)
                 nc.scalar.copy(out=late_row[:], in_=first_rows[:, 1])
+        late_gain = shared.tile([P, 1], F32, name="late_gain", offset=AT_ROWS + ROW, align_bytes=64)
+        nc.scalar.copy(out=late_gain[:], in_=gain_hi[:, last - 1 : last])
 
         pick_scaled(first[:, last], pos1_sb, first_rows[:, 1], h, 0, HALF)
         pick_scaled(second[:, last], pos2_sb, first_rows[:, 1], h, 0, HALF)
         pick_scaled(first[:, last], pos1_sb, first_rows[:, 1], h, HALF, Q)
         subtract(z_hi[0], 0, HALF)
+        rest = both[:, :, last - 1, HALF:]
+        nc.scalar.activation(out=rest, in_=rest, func=ACT.Copy, scale=late_gain[:])
         quantize_z(0, 0, z_first[:])
         upper_codes = shared.tile([P, HALF], U32, name="upper_codes", offset=AT_FRONT, align_bytes=64)
         quantize_z(0, 1, z_hi[0])

@@ -25,8 +25,9 @@ BANKS = 8
 LANES = 16
 QUAD = 32
 HALF = 256
-POOL_SHARE = 88
+POOL_SHARE = 64
 LAP = 128
+POOL_EARLY = 32
 ROW = 4 * Q
 AT_SCALES = 0
 AT_TABLE1 = AT_SCALES + T
@@ -185,10 +186,10 @@ def tile_list_frame_delta_logits_kernel(
         def pool_copy(out, in_):
             nc.gpsimd.tensor_scalar(out, in_, 1.0, 0.0, ALU.mult, ALU.add)
 
-        def pool_round(dst, a, tiles):
+        def pool_round(dst, a, tiles, m0, m1):
             pool_copy(
-                dst.rearrange("p (t m j) -> p m t j", t=tiles, j=PACK),
-                hi_raw[a][:].rearrange("p j (m t) -> p m t j", t=PACK)[:, :, 0:tiles],
+                dst.rearrange("p (t m j) -> p m t j", t=tiles, j=PACK)[:, m0:m1],
+                hi_raw[a][:].rearrange("p j (m t) -> p m t j", t=PACK)[:, m0:m1, 0:tiles],
             )
 
         def pool_gain(dst, src, column):
@@ -238,7 +239,9 @@ def tile_list_frame_delta_logits_kernel(
         nc.vector.tensor_copy(
             rounded[:, POOL_SHARE:].rearrange("p m t j -> p m j t"), source[:, POOL_SHARE:].rearrange("p m t j -> p m j t")
         )
-        pool_copy(rounded[:, 0:POOL_SHARE], source[:, 0:POOL_SHARE])
+        pool_round(hi_bf, 0, PACK, 0, POOL_SHARE)
+        near_bf = back_bf[1]
+        pool_round(near_bf, 1, 2, 0, POOL_EARLY)
         far = row_at("far", AT_FAR)
         far_bf = far.bitcast(BF16)
         magnitudes = [[far, row_at("early", AT_EARLY)]] * 2 + [[far, row_at("late", AT_LATE)]]
@@ -262,11 +265,11 @@ def tile_list_frame_delta_logits_kernel(
             if t == 1:
                 hi_codes.append(shared.tile([P, K_PASS], U32, name="hi_codes0", offset=AT_EARLY, align_bytes=64))
                 quantize(hi_codes[0][:], hi_planes[:, 0:K_PASS], hi_bf)
-                pool_round(hi_bf[:, 0:piece], 1, 2)
+                pool_round(near_bf, 1, 2, POOL_EARLY, P)
             if t == 2:
                 round_hi(far_bf, 1, 2, nc.scalar.copy)
                 hi_codes.append(shared.tile([P, K_PASS], U32, name="hi_codes1", offset=AT_LATE, align_bytes=64))
-                for c0, src in ((0, hi_bf[:, 0:piece]), (HALF, far_bf)):
+                for c0, src in ((0, near_bf), (HALF, far_bf)):
                     quantize(hi_codes[1][:, c0 : c0 + HALF], hi_planes[:, K_PASS + c0 : K_PASS + c0 + HALF], src)
             gather_lower(t, 1, h)
         terms = []

from contextlib import ExitStack

import concourse.mybir as mybir
from concourse.masks import make_identity

K, T, S, Q, H, N = 1024, 4096, 1024, 512, 1024, 512
FLOPS = 2 * K * H * S + 2 * H * N * Q

F32 = mybir.dt.float32
BF16 = mybir.dt.bfloat16
I32 = mybir.dt.int32
U32 = mybir.dt.uint32
U16 = mybir.dt.uint16
U8 = mybir.dt.uint8
FP8X4 = mybir.dt.float8_e4m3fn_x4
FP4X4 = mybir.dt.float4_e2m1fn_x4
ACT = mybir.ActivationFunctionType
ALU = mybir.AluOpType

P = 128
PACK = 4
K_PASS = P * PACK
BANK = 512
BANKS = 8
LANES = 16
QUAD = 32
HALF = 256
POOL_SHARE = 64
LAP = 128
POOL_EARLY = 32
ROW = 4 * Q
AT_SCALES = 0
AT_TABLE1 = AT_SCALES + T
AT_FRONT = AT_TABLE1 + 4 * T
AT_CODES1 = AT_FRONT + 2 * ROW
AT_STAGE = AT_CODES1 + 2 * ROW
AT_H = AT_STAGE + 4 * ROW
AT_EARLY = AT_H + 16 * ROW
AT_LATE = AT_EARLY + ROW
AT_FAR = AT_LATE + 2 * ROW
AT_RAW = AT_FAR + 2 * ROW
AT_ROWS = AT_RAW + 9 * ROW
AT_Z = AT_ROWS + 2 * ROW


def tile_list_frame_delta_logits_kernel(
    tc, tab_words, tab_scales, offs, pos1, pos2, w1, gain, w2_words, w2_scales, out
):
    nc = tc.nc
    with ExitStack() as ctx:
        keep = ctx.enter_context(tc.tile_pool(name="keep", bufs=1))
        shared = ctx.enter_context(tc.tile_pool(name="shared", bufs=1))
        psum = ctx.enter_context(tc.psum_pool(name="psum", bufs=1))

        banks = [psum.tile([P, BANK], F32, name=f"bank{i}") for i in range(BANKS)]
        offs_sb = keep.tile([P, S // LANES], U16, name="offs_sb")
        pos1_sb = keep.tile([P, Q // LANES], U16, name="pos1_sb")
        pos2_sb = keep.tile([P, Q // LANES], U16, name="pos2_sb")
        gain_flat = keep.tile([P, P], F32, name="gain_flat")
        front_bf = shared.tile([P, 2 * PACK * HALF], BF16, name="front_bf", offset=AT_CODES1 + ROW, align_bytes=64)
        gain_lo = keep.tile([P, PACK], F32, name="gain_lo")
        gain_hi = keep.tile([P, PACK], F32, name="gain_hi")
        table_scales = shared.tile([P, T // 4], I32, name="table_scales", offset=AT_SCALES, align_bytes=64)
        table = [
            keep.tile([P, T], I32, name="table0", align_bytes=64),
            shared.tile([P, T], I32, name="table1", offset=AT_TABLE1, align_bytes=64),
        ]
        front_raw = [
            keep.tile([P, PACK, HALF], F32, name="front_raw0"),
            shared.tile([P, PACK, HALF], F32, name="front_raw1", offset=AT_FRONT, align_bytes=64),
        ]
        back_raw = [keep.tile([P, PACK, HALF], F32, name=f"back_raw{a}") for a in range(2)]
        hi_raw = [keep.tile([P, PACK, K_PASS], F32, name=f"hi_raw{a}") for a in range(2)]
        w2_codes = keep.tile([P, 2, 2 * N], U8, name="w2_codes", align_bytes=64)
        w2_planes = keep.tile([P, 2, N // 4], I32, name="w2_planes", align_bytes=64)
        one = keep.tile([P, 1], F32, name="one")
        zero = keep.tile([P, 1], F32, name="zero")
        ident = keep.tile([P, P], F32, name="ident")

        def load_table(a):
            nc.sync.dma_start(table[a][:], tab_words[a].rearrange("p t i -> p (t i)").bitcast(I32))

        def load_w1(dst, a, c0, c1):
            nc.sync.dma_start(dst, w1[a * K_PASS : (a + 1) * K_PASS, c0:c1].rearrange("(p j) c -> p j c", j=PACK))

        nc.vector.memset(gain_flat[:], 0.0)
        nc.vector.memset(table_scales[:], 0)
        nc.vector.memset(one[:], 1.0)
        make_identity(nc, ident[:])
        nc.scalar.dma_start(gain_hi[:], gain[K_PASS:H].rearrange("(p t) -> p t", t=PACK))
        nc.scalar.dma_start(gain_flat[0:PACK, :], gain[0:K_PASS].rearrange("(t p) -> t p", p=P))
        for quad in range(P // QUAD):
            nc.gpsimd.dma_start(
                table_scales[QUAD * quad : QUAD * quad + 8, :], tab_scales.bitcast(I32)[:, 4 * quad : 4 * quad + 4, :]
            )
        nc.sync.dma_start(offs_sb[:], offs)
        load_table(0)
        for a in range(2):
            load_w1(front_raw[a][:], a, 0, HALF)
        load_table(1)
        for a in range(2):
            load_w1(back_raw[a][:], a, HALF, K_PASS)
        load_w1(hi_raw[0][:], 0, K_PASS, H)
        nc.sync.dma_start(pos1_sb[:], pos1)
        nc.sync.dma_start(pos2_sb[:], pos2)
        load_w1(hi_raw[1][:], 1, K_PASS, H)
        nc.sync.dma_start(w2_codes[:].bitcast(I32), w2_words.rearrange("b p c -> p b c").bitcast(I32))
        nc.vector.memset(w2_planes[:], 0)
        for quad in range(P // QUAD):
            nc.sync.dma_start(
                w2_planes[QUAD * quad : QUAD * quad + 4, :, :],
                w2_scales.bitcast(I32)[:, 4 * quad : 4 * quad + 4, :].rearrange("b r c -> r b c"),
            )

        nc.scalar.activation(out=zero[:], in_=one[:], func=ACT.Ln)

        v_codes = [keep.tile([P, S], U32, name="v_codes0", align_bytes=64)]
        v_planes = keep.tile([P, S], U8, name="v_planes", align_bytes=64)
        planes = [keep.tile([P, 2 * HALF], U8, name=f"planes{i}", align_bytes=64) for i in range(2)]
        hi_planes = keep.tile([P, 2 * K_PASS], U8, name="hi_planes", align_bytes=64)
        codes = []

        def round_lo(dst, raw, c0, c1, copy):
            copy(
                out=dst.rearrange("p (c i j) -> p c j i", i=4, j=PACK),
                in_=raw[:, :, c0:c1].rearrange("p j (c i) -> p c j i", i=4),
            )

        def round_hi(dst, a, t0, copy):
            copy(
                out=dst.rearrange("p (t m j) -> p m j t", t=2, j=PACK),
                in_=hi_raw[a][:].rearrange("p j (m t) -> p m j t", t=PACK)[:, :, :, t0 : t0 + 2],
            )

        def quantize(to_codes, to_planes, src):
            nc.vector.quantize_mx(out=to_codes.bitcast(FP8X4), scales=to_planes, in_=src)

        def stationary(i, a):
            if i >= PACK:
                c0 = (i - PACK) * P
                return hi_codes[a][:, c0 : c0 + P], hi_planes[:, a * K_PASS + c0 : a * K_PASS + c0 + P]
            c0 = (i % 2) * P
            return codes[i // 2][a][:, c0 : c0 + P], planes[i // 2][:, a * HALF + c0 : a * HALF + c0 + P]

        def x_pass(i, a, s):
            frames = slice(s * BANK, (s + 1) * BANK)
            w_codes, w_planes = stationary(i, a)
            nc.tensor.matmul_mx(
                out=banks[2 * (i % PACK) + s][:],
                lhsT=w_codes.bitcast(FP8X4),
                lhsT_scale=w_planes,
                rhs=v_codes[a][:, frames].bitcast(FP8X4),
                rhs_scale=v_planes[4 * a :, frames],
                start=(a == 0),
                stop=(a == 1),
            )

        def project(i, magnitude):
            pair = i % PACK
            for s in range(2):
                for a in range(1 if i < 2 else 0, 2):
                    x_pass(i, a, s)
            h = shared.tile([P, S], F32, name=f"h{i}", offset=AT_H + 2 * ROW * i, align_bytes=64)
            steps = [(ACT.Abs, 0, BANK), (ACT.Abs, BANK, S), (ACT.Ln, 0, BANK), (ACT.Ln, BANK, S)]
            if i == 0:
                steps = [(ACT.Abs, 0, HALF), (ACT.Abs, HALF, BANK), (ACT.Ln, 0, HALF), steps[1], (ACT.Ln, HALF, BANK), steps[3]]
            for func, f0, f1 in steps:
                s, c0 = divmod(f0, BANK)
                part = magnitude[s][:, c0 : c0 + f1 - f0]
                if func == ACT.Abs:
                    bank = banks[2 * pair + s][:, c0 : c0 + f1 - f0]
                    nc.scalar.activation(out=part, in_=bank, func=func, bias=zero[:])
                else:
                    nc.scalar.activation(out=h[:, f0:f1], in_=part, func=func, bias=one[:])
            return h

        def offsets(list_sb, j0, j1):
            return list_sb[:, j0 // LANES : j1 // LANES]

        def pick_scaled(dst, pos_sb, row, h, q0=0, q1=Q):
            nc.vector.tensor_tensor(dst[:, q0:q1], h[:].indirect(offsets(pos_sb, q0, q1)), row, ALU.mult)

        def pick(dst, pos_sb, h, q0=0, q1=Q):
            nc.vector.tensor_copy(dst[:, q0:q1], h[:].indirect(offsets(pos_sb, q0, q1)))

        def pool_copy(out, in_):
            nc.gpsimd.tensor_scalar(out, in_, 1.0, 0.0, ALU.mult, ALU.add)

        def pool_round(dst, a, tiles, m0, m1):
            pool_copy(
                dst.rearrange("p (t m j) -> p m t j", t=tiles, j=PACK)[:, m0:m1],
                hi_raw[a][:].rearrange("p j (m t) -> p m t j", t=PACK)[:, m0:m1, 0:tiles],
            )

        def pool_gain(dst, src, column):
            nc.gpsimd.tensor_scalar(dst, src, column, 0.0, ALU.mult, ALU.add)

        def row_at(name, offset):
            return shared.tile([P, Q], F32, name=name, offset=offset, align_bytes=64)[:]

        gain_bank = banks[BANKS - 1]
        nc.tensor.transpose(gain_bank[:, 0:P], gain_flat[:], ident[:])
        nc.scalar.copy(out=gain_lo[:], in_=gain_bank[:, 0:PACK])
        gain_minus = keep.tile([P, PACK], F32, name="gain_minus")
        nc.gpsimd.tensor_scalar(gain_minus[:], gain_lo[:], -1.0, 0.0, ALU.mult, ALU.add)

        nc.vector.tensor_copy(v_codes[0][:], table[0][:].bitcast(U32).indirect(offs_sb[:]))
        nc.vector.tensor_copy(v_planes[:], table_scales[:].bitcast(U8).indirect(offs_sb[:]))
        for a in range(2):
            round_lo(front_bf[:, a * PACK * HALF : (a + 1) * PACK * HALF], front_raw[a], 0, HALF, nc.scalar.copy)
        front_codes = shared.tile([P, 2 * HALF], U32, name="front_codes", offset=AT_SCALES, align_bytes=64)
        codes.append([front_codes[:, 0:HALF], front_codes[:, HALF:]])
        quantize(front_codes[:], planes[0][:], front_bf[:])
        for i in range(2):
            for s in range(2):
                x_pass(i, 0, s)
        first_rows = shared.tile([P, 2, HALF], F32, name="first_rows", offset=AT_FRONT, align_bytes=64)
        nc.scalar.copy(out=first_rows[:], in_=gain_hi[:, PACK - 2 :].unsqueeze(2).to_broadcast([P, 2, HALF]))

        v_codes.append(shared.tile([P, S], U32, name="v_codes1", offset=AT_CODES1, align_bytes=64))
        for s in range(2):
            nc.vector.tensor_copy(
                v_codes[1][:, s * BANK : (s + 1) * BANK],
                table[1][:].bitcast(U32).indirect(offsets(offs_sb, s * BANK, (s + 1) * BANK)),
            )
        piece = PACK * HALF
        stage = shared.tile([P, 4 * piece - 2 * LAP], BF16, name="stage", offset=AT_STAGE, align_bytes=64)
        hi_bf = stage[:, piece - LAP : 3 * piece - LAP]
        back_bf = [stage[:, 3 * piece - 2 * LAP :], stage[:, 0:piece]]
        back_codes = keep.tile([P, 2 * HALF], U32, name="back_codes", align_bytes=64)
        codes.append([back_codes[:, 0:HALF], back_codes[:, HALF:]])
        for a in range(2):
            round_lo(back_bf[a], back_raw[a], 0, HALF, nc.vector.tensor_copy)
        for a in range(2):
            quantize(codes[1][a], planes[1][:, a * HALF : (a + 1) * HALF], back_bf[a])

        rounded = hi_bf.rearrange("p (t m j) -> p m t j", t=PACK, j=PACK)
        source = hi_raw[0][:].rearrange("p j (m t) -> p m t j", t=PACK)
        nc.vector.tensor_copy(
            rounded[:, POOL_SHARE:].rearrange("p m t j -> p m j t"), source[:, POOL_SHARE:].rearrange("p m t j -> p m j t")
        )
        pool_round(hi_bf, 0, PACK, 0, POOL_SHARE)
        near_bf = back_bf[1]
        pool_round(near_bf, 1, 2, 0, POOL_EARLY)
        far = row_at("far", AT_FAR)
        far_bf = far.bitcast(BF16)
        magnitudes = [[far, row_at("early", AT_EARLY)]] * 2 + [[far, row_at("late", AT_LATE)]]
        upper_magnitude = [hi_raw[1][:, s] for s in range(2)]
        raw_at = [[AT_RAW, AT_RAW + 3 * ROW // 2], [AT_RAW + 3 * ROW, None], [AT_RAW + 4 * ROW, None],
                  [AT_RAW + 5 * ROW, AT_RAW + 6 * ROW]]
        term_at = [[AT_FAR - ROW // 2, raw_at[0][0]], [AT_RAW + ROW, AT_RAW + 2 * ROW], [raw_at[1][0], raw_at[2][0]],
                   [AT_RAW + 7 * ROW, AT_RAW + 8 * ROW]]
        hi_codes = []
        raws = [[None, None] for t in range(PACK)]

        def gather_lower(t, i, h):
            raws[t][i] = hi_raw[t - 1][:, 2] if raw_at[t][i] is None else row_at(f"raw{t}_{i}", raw_at[t][i])
            pick(raws[t][i], (pos1_sb, pos2_sb)[i], h)

        for t in range(PACK):
            if t == PACK - 1:
                magnitudes.append([row_at(f"last{s}", AT_H + s * ROW) for s in range(2)])
            h = project(t, magnitudes[t])
            gather_lower(t, 0, h)
            if t == 1:
                hi_codes.append(shared.tile([P, K_PASS], U32, name="hi_codes0", offset=AT_EARLY, align_bytes=64))
                quantize(hi_codes[0][:], hi_planes[:, 0:K_PASS], hi_bf)
                pool_round(near_bf, 1, 2, POOL_EARLY, P)
            if t == 2:
                round_hi(far_bf, 1, 2, nc.scalar.copy)
                hi_codes.append(shared.tile([P, K_PASS], U32, name="hi_codes1", offset=AT_LATE, align_bytes=64))
                for c0, src in ((0, near_bf), (HALF, far_bf)):
                    quantize(hi_codes[1][:, c0 : c0 + HALF], hi_planes[:, K_PASS + c0 : K_PASS + c0 + HALF], src)
            gather_lower(t, 1, h)
        terms = []
        for t in range(PACK):
            terms.append([row_at(f"term{t}_{i}", term_at[t][i]) for i in range(2)])
            for i, gains in enumerate((gain_lo, gain_minus)):
                pool_gain(terms[t][i], raws[t][i], gains[:, t : t + 1])

        both = keep.tile([P, 2, PACK, Q], F32, name="both", align_bytes=64)
        second, first = both[:, 0], both[:, 1]
        z_rows = [
            shared.tile([P, 2, 2, HALF], BF16, name=f"z_rows{half}", offset=AT_ROWS + half * ROW, align_bytes=64)
            for half in range(2)
        ]
        z_first = shared.tile([P, PACK * HALF], BF16, name="z_first", offset=AT_Z, align_bytes=64)
        z_late = keep.tile([P, PACK * HALF], BF16, name="z_late", align_bytes=64)
        z_lo = [z_first, z_late]
        z_upper = keep.tile([P, PACK * HALF], BF16, name="z_upper", align_bytes=64)
        z_hi = [z_upper[:]] * 2
        z_codes = keep.tile([P, 2 * Q], U32, name="z_codes", align_bytes=64)

        z_planes = keep.tile([P, 2 * Q], U8, name="z_planes", align_bytes=64)

        def turn_delta(t):
            bank = banks[t][:].rearrange("p (g r) -> p g r", r=P)
            for g in range(Q // P):
                for i in range(2):
                    nc.tensor.matmul(
                        bank[:, g, :],
                        terms[t][i][:, g * P : (g + 1) * P],
                        ident[:],
                        start=(i == 0),
                        stop=(i == 1),
                        is_transpose=True,
                    )

        def round_delta(t, g0, g1):
            bank = banks[t][:].rearrange("p (g r) -> p g r", r=P)[:, g0:g1]
            places = slice(t * P // 2, (t + 1) * P // 2)
            nc.scalar.copy(
                out=z_rows[g0 // 2][:, :, :, places].rearrange("p g u (m e) -> p g u m e", e=2),
                in_=bank.rearrange("p g (m u e) -> p g u m e", u=2, e=2),
            )

        def turn_back(half):
            bank = banks[PACK + 1 - half][:].rearrange("p (g u q) -> p g u q", g=2, u=2)
            for g in range(2):
                for u in range(2):
                    nc.tensor.transpose(bank[:, g, u, :], z_rows[half][:, g, u].bitcast(F32), ident[:])
            nc.scalar.copy(
                out=z_lo[half][:].bitcast(F32).rearrange("p (g q u) -> p g q u", g=2, u=2),
                in_=bank.rearrange("p g u q -> p g q u"),
            )

        def subtract(dst, q0, q1):
            nc.vector.tensor_tensor(
                dst.rearrange("p (c i t) -> p c t i", i=2, t=PACK),
                first[:, :, q0:q1].rearrange("p t (c i) -> p c t i", i=2),
                second[:, :, q0:q1].rearrange("p t (c i) -> p c t i", i=2),
                ALU.subtract,
            )

        def z_start(half, b):
            return half * Q + (1 - b) * HALF

        def z_words(half, b, q0, q1):
            if (half, b) == (0, 1):
                return upper_codes[:, q0:q1]
            return z_codes[:, z_start(half, b) + q0 : z_start(half, b) + q1]

        def quantize_z(half, b, src, q0=0, q1=HALF):
            cols = slice(z_start(half, b) + q0, z_start(half, b) + q1)
            quantize(z_words(half, b, q0, q1), z_planes[:, cols], src)

        def logit_pass(half, n, b, q0=0, q1=HALF, copy=None):
            bank = banks[(BANKS - 1 - n) if half == 0 else n][:, 0:HALF]
            cols = slice(z_start(half, b) + q0, z_start(half, b) + q1)
            nc.tensor.matmul_mx(
                out=bank[:, q0:q1],
                lhsT=w2_codes[:, b, 2 * n * P : 2 * (n + 1) * P].bitcast(FP4X4),
                lhsT_scale=w2_planes[:, b, :].bitcast(U8)[:, n * P : (n + 1) * P],
                rhs=z_words(half, b, q0, q1).bitcast(FP8X4),
                rhs_scale=z_planes[:, cols],
                start=(b == 0 and q0 == 0),
                stop=(b == 1 and q1 == HALF),
            )
            if copy is not None:
                staged = keep.tile([P, HALF], F32, name=f"staged{half}_{n}")
                copy(out=staged[:], in_=bank)
                nc.sync.dma_start(out[n * P : (n + 1) * P, half * HALF : (half + 1) * HALF], staged[:])

        last = PACK - 1
        for t in range(last):
            h = project(PACK + t, upper_magnitude)
            pick(first[:, t], pos1_sb, h)
            if t < last - 1:
                pick(second[:, t], pos2_sb, h)
                for part in (first, second):
                    pool_gain(part[:, t], part[:, t], gain_hi[:, t : t + 1])
            else:
                pool_gain(first[:, t, 0:HALF], first[:, t, 0:HALF], gain_hi[:, t : t + 1])
                pick(second[:, t], pos2_sb, h, HALF, Q)
                pick_scaled(second[:, t], pos2_sb, first_rows[:, 0], h, 0, HALF)
        h = project(PACK + last, upper_magnitude)
        for t in range(PACK):
            turn_delta(t)
        for half in range(2):
            for t in range(PACK):
                round_delta(t, 2 * half, 2 * half + 2)
            turn_back(half)
            if half == 0:
                late_row = shared.tile([P, HALF], F32, name="late_row", offset=AT_ROWS, align_bytes=64)
                nc.scalar.copy(out=late_row[:], in_=first_rows[:, 1])
        late_gain = shared.tile([P, 1], F32, name="late_gain", offset=AT_ROWS + ROW, align_bytes=64)
        nc.scalar.copy(out=late_gain[:], in_=gain_hi[:, last - 1 : last])

        pick_scaled(first[:, last], pos1_sb, first_rows[:, 1], h, 0, HALF)
        pick_scaled(second[:, last], pos2_sb, first_rows[:, 1], h, 0, HALF)
        pick_scaled(first[:, last], pos1_sb, first_rows[:, 1], h, HALF, Q)
        subtract(z_hi[0], 0, HALF)
        rest = both[:, :, last - 1, HALF:]
        nc.scalar.activation(out=rest, in_=rest, func=ACT.Copy, scale=late_gain[:])
        quantize_z(0, 0, z_first[:])
        upper_codes = shared.tile([P, HALF], U32, name="upper_codes", offset=AT_FRONT, align_bytes=64)
        quantize_z(0, 1, z_hi[0])
        pick_scaled(second[:, last], pos2_sb, late_row[:], h, HALF, Q)
        for n in range(N // P):
            logit_pass(0, n, 0)
        for n in range(N // P):
            logit_pass(0, n, 1, copy=nc.scalar.copy)

        quantize_z(1, 0, z_late[:])
        for n in range(N // P):
            logit_pass(1, n, 0)
        for q in (0, P):
            subtract(z_hi[1][:, PACK * q : PACK * (q + P)], HALF + q, HALF + q + P)
        for q in (0, P):
            quantize_z(1, 1, z_hi[1][:, PACK * q : PACK * (q + P)], q, q + P)
        for n in range(N // P):
            logit_pass(1, n, 1, 0, P)
        for n in range(N // P):
            logit_pass(1, n, 1, P, HALF, copy=nc.vector.tensor_copy if n % 2 else nc.scalar.copy)
